import numpy as np
import ml_dtypes


def mxq(x, axis, fmt="e4m3"):
    dtype, down = {"e4m3": (ml_dtypes.float8_e4m3fn, 7), "e5m2": (ml_dtypes.float8_e5m2, 14)}[fmt]
    v = np.moveaxis(np.asarray(x, np.float32).astype(ml_dtypes.bfloat16).astype(np.float64), axis, -1)
    blocks = v.reshape(v.shape[:-1] + (-1, 32))
    amax = np.abs(blocks).max(-1, keepdims=True)
    byte = np.maximum(np.where(amax > 0, np.frexp(amax)[1] - 1 + 127, 0) - down, 1)
    scale = np.exp2(byte - 127.0)
    codes = (blocks / scale).astype(np.float32).astype(dtype).astype(np.float64)
    return np.moveaxis((codes * scale).reshape(v.shape), -1, axis)


WIDE = False


def mx_kscale(k):
    if not WIDE:
        return np.ones(k)
    levels = np.array([10, -10, 5, -5, 0])
    if k % 512:
        return np.exp2(np.random.permutation(np.resize(levels, k // 32))).repeat(32)
    a = np.empty((k // 512, 16))
    for p in range(k // 512):
        a[p, :8] = np.random.permutation(np.resize(levels, 8))
        for g in range(8):
            far = levels[np.abs(levels - a[p, g]) >= 10]
            a[p, g + 8] = far[np.random.randint(len(far))]
    return np.exp2(a.ravel()).repeat(32)


def f64(x):
    return np.asarray(x).astype(np.float64)


def striped(idx):
    return np.tile(idx.reshape(-1, 16).T, (8, 1)).astype(np.uint16)


def unstriped(offs):
    return offs[:16].T.reshape(-1).astype(np.int64)


E2M1 = np.array([0.0, 0.5, 1.0, 1.5, 2.0, 3.0, 4.0, 6.0, -0.0, -0.5, -1.0, -1.5, -2.0, -3.0, -4.0, -6.0])


def pack_weight(w, fmt):
    k, n = w.shape
    w = f64(np.asarray(w, np.float32).astype(ml_dtypes.bfloat16)).reshape(k // 32, 32, n)
    amax = np.abs(w).max(1)
    if fmt == "e4m3":
        byte = np.frexp(amax)[1] - 1 + 127 - 7
    else:
        mant, ex = np.frexp(amax / 6.0)
        byte = np.where(mant > 0.5, ex, ex - 1) + 127
    byte = np.clip(np.where(amax > 0, byte, 1), 1, 254)
    scaled = (w * np.exp2(127.0 - byte)[:, None, :]).reshape(k, n).astype(np.float32)
    by_word = np.ascontiguousarray(scaled.reshape(k // 512, 128, 4, n).transpose(0, 1, 3, 2))
    if fmt == "e4m3":
        words = by_word.astype(ml_dtypes.float8_e4m3fn).view(np.uint8)
    else:
        c = by_word.astype(ml_dtypes.float4_e2m1fn).view(np.uint8) & 0xF
        words = (c[..., 0::2] | (c[..., 1::2] << 4)).reshape(k // 512, 128, 2 * n)
    return np.ascontiguousarray(words), np.ascontiguousarray(byte.astype(np.uint8).reshape(k // 512, 16, n))


def unpack_weight(words, scales, fmt):
    g, _, n = scales.shape
    words = np.ascontiguousarray(words).reshape(g, 128, n, -1)
    if fmt == "e4m3":
        vals = words.view(ml_dtypes.float8_e4m3fn).astype(np.float64)
    else:
        nib = np.empty((g, 128, n, 4), np.uint8)
        nib[..., 0::2] = words & 0xF
        nib[..., 1::2] = words >> 4
        vals = E2M1[nib]
    vals = vals * np.repeat(np.exp2(scales.astype(np.float64) - 127.0), 8, axis=1)[..., None]
    return vals.transpose(0, 1, 3, 2).reshape(g * 512, n)


def gelu(v):
    return 0.5 * v * (1.0 + np.tanh(np.sqrt(2.0 / np.pi) * (v + 0.044715 * v**3)))


K, H, N, T, S, P = 1536, 1024, 512, 2048, 1024, 512

def setup_inputs():
    n = np.random.standard_normal
    s = mx_kscale(K)[:, None]
    u = mx_kscale(H)[:, None]
    tab_words, tab_scales = pack_weight(n((K, T)) * s, "e4m3")
    w1 = (n((K, H)) / np.sqrt(K) / s).astype(np.float32)
    w2_words, w2_scales = pack_weight((0.1 + n((H, N))) / np.sqrt(H) / u, "e2m1")
    gain = (np.exp(0.3 * n(H)) * u[:, 0]).astype(np.float32)
    return {
        "tab_words": tab_words, "tab_scales": tab_scales,
        "offs": striped(np.random.permutation(T)[:S]),
        "pos1": striped(np.random.permutation(S)[:P]),
        "pos2": striped(np.random.permutation(S)[:P]),
        "w1": w1, "gain": gain,
        "w2_words": w2_words, "w2_scales": w2_scales,
    }

def reference(tab_words, tab_scales, offs, pos1, pos2, w1, gain, w2_words, w2_scales):
    v = unpack_weight(tab_words, tab_scales, "e4m3")[:, unstriped(offs)]
    x = mxq(f64(w1), 0, "e4m3").T @ v
    h = np.exp(-np.square(x))
    a = h[:, unstriped(pos1)]
    b = h[:, unstriped(pos2)]
    z = f64(gain)[:, None] * a * b
    y = unpack_weight(w2_words, w2_scales, "e2m1").T @ mxq(z, 0, "e4m3")
    return np.sqrt(np.abs(y))

@@ -1,0 +1,250 @@
+from contextlib import ExitStack
+
+import concourse.mybir as mybir
+
+K, H, N, T, S, P = 1536, 1024, 512, 2048, 1024, 512
+FLOPS = 2 * K * H * S + 2 * H * N * P
+
+F32 = mybir.dt.float32
+BF16 = mybir.dt.bfloat16
+I32 = mybir.dt.int32
+U32 = mybir.dt.uint32
+U16 = mybir.dt.uint16
+U8 = mybir.dt.uint8
+FP8X4 = mybir.dt.float8_e4m3fn_x4
+FP4X4 = mybir.dt.float4_e2m1fn_x4
+ACT = mybir.ActivationFunctionType
+MULT = mybir.AluOpType.mult
+
+PART = 128
+PACK = 4
+PASS = PART * PACK
+K_PASSES = K // PASS
+R_PASSES = H // PASS
+BANK = 512
+STRIPE = 16
+GAIN_W = 256
+QUARTER = 128
+
+
+def tile_list_stereo_disparity_cost_kernel(tc, tab_words, tab_scales, offs, pos1, pos2, w1, gain, w2_words, w2_scales, out):
+    nc = tc.nc
+    with ExitStack() as ctx:
+        keep = ctx.enter_context(tc.tile_pool(name="keep", bufs=1))
+        ring = ctx.enter_context(tc.tile_pool(name="ring", bufs=3))
+        resp = ctx.enter_context(tc.tile_pool(name="resp", bufs=8))
+        psum_a = ctx.enter_context(tc.psum_pool(name="psum_a", bufs=1))
+        psum_b = ctx.enter_context(tc.psum_pool(name="psum_b", bufs=4))
+
+        offs_sb = keep.tile([PART, S // STRIPE], U16, name="offs_sb")
+        pos1_sb = keep.tile([PART, P // STRIPE], U16, name="pos1_sb")
+        pos2_sb = keep.tile([PART, P // STRIPE], U16, name="pos2_sb")
+        gain_sb = keep.tile([PART, R_PASSES * PACK], F32, name="gain_sb")
+        gain_wide = keep.tile([PART, R_PASSES * PACK, GAIN_W], F32, name="gain_wide")
+        table = [keep.tile([PART, T], I32, name="table%d" % a, align_bytes=64) for a in range(K_PASSES)]
+        table_sc = keep.tile([PART, T // 4], I32, name="table_sc", align_bytes=64)
+        v_words = [keep.tile([PART, S], U32, name="v_words%d" % a, align_bytes=64) for a in range(K_PASSES)]
+        v_sc = keep.tile([PART, S], U8, name="v_sc", align_bytes=64)
+        w1_raw = {}
+        w1_bf = {}
+        w1_words = {}
+        w1_sc = {}
+        for b in range(R_PASSES):
+            for a in range(K_PASSES):
+                w1_raw[b, a] = keep.tile([PART, PACK, PASS], F32, name="w1_raw%d%d" % (b, a))
+                w1_words[b, a] = keep.tile([PART, PASS], U32, name="w1_words%d%d" % (b, a), align_bytes=64)
+                w1_sc[b, a] = keep.tile([PART, PASS], U8, name="w1_sc%d%d" % (b, a), align_bytes=64)
+        w2_sb = keep.tile([PART, R_PASSES, N // 2], I32, name="w2_sb", align_bytes=64)
+        w2_sc = keep.tile([PART, R_PASSES, N // 4], I32, name="w2_sc", align_bytes=64)
+        z_f32 = [keep.tile([PART, PACK, P], F32, name="z_f32%d" % b) for b in range(R_PASSES)]
+        z_bf = [keep.tile([PART, P * PACK], BF16, name="z_bf%d" % b, align_bytes=64) for b in range(R_PASSES)]
+        z_words = [keep.tile([PART, P], U32, name="z_words%d" % b, align_bytes=64) for b in range(R_PASSES)]
+        z_sc = [keep.tile([PART, P], U8, name="z_sc%d" % b, align_bytes=64) for b in range(R_PASSES)]
+        warm = keep.tile([PART, 1], F32, name="warm")
+
+        def load_w1(b, a):
+            rows = w1[a * PASS : (a + 1) * PASS, b * PASS : (b + 1) * PASS]
+            nc.sync.dma_start(out=w1_raw[b, a][:], in_=rows.rearrange("(p j) c -> p j c", j=PACK))
+
+        def load_table(a):
+            nc.sync.dma_start(out=table[a][:], in_=tab_words[a].rearrange("p t i -> p (t i)").bitcast(I32))
+
+        nc.vector.memset(table_sc[:], 0)
+        nc.vector.memset(w2_sc[:], 0)
+        nc.sync.dma_start(offs_sb[:], offs)
+        load_table(0)
+        for a in range(K_PASSES):
+            for q in range(4):
+                queue = nc.gpsimd if (a == 2 and q > 0) else nc.scalar
+                queue.dma_start(out=table_sc[32 * q + 4 * a : 32 * q + 4 * a + 4, :], in_=tab_scales[a, 4 * q : 4 * q + 4, :].bitcast(I32))
+        nc.gpsimd.dma_start(out=gain_sb[:].rearrange("p (b t) -> p b t", t=PACK), in_=gain.rearrange("(b p t) -> p b t", b=R_PASSES, t=PACK))
+        load_table(1)
+        for a in range(K_PASSES):
+            load_w1(0, a)
+        load_table(2)
+        nc.sync.dma_start(pos1_sb[:], pos1)
+        nc.sync.dma_start(pos2_sb[:], pos2)
+        for a in range(K_PASSES):
+            load_w1(1, a)
+        nc.sync.dma_start(out=w2_sb[:], in_=w2_words.rearrange("b p c -> p b c").bitcast(I32))
+        for q in range(4):
+            nc.sync.dma_start(out=w2_sc[32 * q : 32 * q + 4, :, :], in_=w2_scales[:, 4 * q : 4 * q + 4, :].rearrange("b r n -> r b n").bitcast(I32))
+
+        def copy_on(engine, dst, src):
+            if engine == "scalar":
+                nc.scalar.copy(out=dst, in_=src)
+            else:
+                nc.vector.tensor_copy(out=dst, in_=src)
+
+        def cast_w1(b, a, engine, m0=0, m1=PART):
+            if (b, a) not in w1_bf:
+                w1_bf[b, a] = ring.tile([PART, PASS * PACK], BF16, name="w1_bf", align_bytes=64)
+            dst = w1_bf[b, a][:].rearrange("p (t m j) -> p m j t", t=PACK, j=PACK)[:, m0:m1]
+            src = w1_raw[b, a][:].rearrange("p j (m t) -> p m j t", t=PACK)[:, m0:m1]
+            copy_on(engine, dst, src)
+
+        def quant_w1(b, a, c0=0, c1=PASS):
+            nc.vector.quantize_mx(
+                out=w1_words[b, a][:, c0:c1].bitcast(FP8X4), scales=w1_sc[b, a][:, c0:c1], in_=w1_bf[b, a][:, PACK * c0 : PACK * c1]
+            )
+
+        def gather_words(a, j0, j1):
+            nc.vector.tensor_copy(v_words[a][:, j0:j1], table[a][:].bitcast(U32).indirect(offs_sb[:, j0 // STRIPE : j1 // STRIPE]))
+
+        def x_pass(acc, b, t, a, j0, j1):
+            cols = slice(t * PART, (t + 1) * PART)
+            nc.tensor.matmul_mx(
+                out=acc,
+                lhsT=w1_words[b, a][:, cols].bitcast(FP8X4),
+                lhsT_scale=w1_sc[b, a][:, cols],
+                rhs=v_words[a][:, j0:j1].bitcast(FP8X4),
+                rhs_scale=v_sc[4 * a : PART, j0:j1],
+                start=(a == 0),
+                stop=(a == K_PASSES - 1),
+            )
+
+        h = {}
+
+        def respond(b, t):
+            h[b, t] = resp.tile([PART, S], F32, name="h")
+            squares = []
+            for j0 in range(0, S, BANK):
+                acc = psum_b.tile([PART, BANK], F32, name="x_acc")
+                for a in range(K_PASSES):
+                    x_pass(acc[:], b, t, a, j0, j0 + BANK)
+                sq = ring.tile([PART, BANK], F32, name="sq", bufs=4)
+                nc.scalar.activation(out=sq[:], in_=acc[:], func=ACT.Square)
+                squares.append(sq)
+            for j0, sq in zip(range(0, S, BANK), squares):
+                nc.scalar.activation(out=h[b, t][:, j0 : j0 + BANK], in_=sq[:], func=ACT.Exp, scale=-1.0)
+
+        left = {}
+
+        def gather_left(b, t, i0, i1, place=None):
+            if place is None:
+                place = ring.tile([PART, GAIN_W], F32, name="left", bufs=4)
+            left[b, t, i0] = place
+            nc.vector.tensor_tensor(
+                left[b, t, i0][:, : i1 - i0],
+                h[b, t][:].indirect(pos1_sb[:, i0 // STRIPE : i1 // STRIPE]),
+                gain_wide[:, PACK * b + t, : i1 - i0],
+                MULT,
+            )
+
+        def gather_right(b, t, i0, i1):
+            nc.vector.tensor_tensor(
+                z_f32[b][:, t, i0:i1],
+                h[b, t][:].indirect(pos2_sb[:, i0 // STRIPE : i1 // STRIPE]),
+                left[b, t, i0][:, : i1 - i0],
+                MULT,
+            )
+
+        def match(b, t, between=None, place=None):
+            for i0 in range(0, P, GAIN_W):
+                gather_left(b, t, i0, i0 + GAIN_W, None if place is None else place[:, i0 : i0 + GAIN_W])
+            if between is not None:
+                between()
+            for i0 in range(0, P, GAIN_W):
+                gather_right(b, t, i0, i0 + GAIN_W)
+
+        def cast_z(b, i0, i1, engine):
+            dst = z_bf[b][:, PACK * i0 : PACK * i1].rearrange("p (c i t) -> p c t i", i=4, t=PACK)
+            src = z_f32[b][:, :, i0:i1].rearrange("p t (c i) -> p c t i", i=4)
+            copy_on(engine, dst, src)
+
+        def quant_z(b, i0, i1):
+            nc.vector.quantize_mx(out=z_words[b][:, i0:i1].bitcast(FP8X4), scales=z_sc[b][:, i0:i1], in_=z_bf[b][:, PACK * i0 : PACK * i1])
+
+        def pool_costs(q):
+            cols = slice(q * QUARTER, (q + 1) * QUARTER)
+            acc = psum_a.tile([PART, N // PART, QUARTER], F32, name="bank%d" % q)
+            for nt in range(N // PART):
+                for b in range(R_PASSES):
+                    nc.tensor.matmul_mx(
+                        out=acc[:, nt, :],
+                        lhsT=w2_sb[:, b, :].bitcast(U8)[:, 2 * PART * nt : 2 * PART * (nt + 1)].bitcast(FP4X4),
+                        lhsT_scale=w2_sc[:, b, :].bitcast(U8)[:, PART * nt : PART * (nt + 1)],
+                        rhs=z_words[b][:, cols].bitcast(FP8X4),
+                        rhs_scale=z_sc[b][:, cols],
+                        start=(b == 0),
+                        stop=(b == R_PASSES - 1),
+                    )
+            mag = ring.tile([PART, N // PART, QUARTER], F32, name="mag")
+            nc.scalar.activation(out=mag[:], in_=acc[:], func=ACT.Abs)
+            cost = ring.tile([PART, N // PART, QUARTER], F32, name="cost", bufs=4)
+            nc.scalar.activation(out=cost[:], in_=mag[:], func=ACT.Sqrt)
+            nc.sync.dma_start(out=out.rearrange("(nt p) i -> p nt i", p=PART)[:, :, cols], in_=cost[:])
+
+        nc.scalar.copy(out=gain_wide[:], in_=gain_sb[:].unsqueeze(2).to_broadcast([PART, R_PASSES * PACK, GAIN_W]))
+        gather_words(0, 0, S)
+        gather_words(1, 0, S)
+        nc.vector.tensor_copy(v_sc[:], table_sc[:].bitcast(U8).indirect(offs_sb[:]))
+        cast_w1(0, 0, "scalar")
+        cast_w1(0, 1, "vector")
+        quant_w1(0, 0)
+        quant_w1(0, 1)
+        cast_w1(0, 2, "vector", 0, 80)
+        cast_w1(0, 2, "scalar", 80, PART)
+        quant_w1(0, 2)
+        first_w = 256
+        first = [psum_a.tile([PART, BANK], F32, name="bank%d" % s) for s in range(S // first_w)]
+        for s in range(S // first_w):
+            x_pass(first[s][:, :first_w], 0, 0, 0, s * first_w, (s + 1) * first_w)
+        for s in range(S // first_w):
+            x_pass(first[s][:, :first_w], 0, 0, 1, s * first_w, (s + 1) * first_w)
+        h[0, 0] = resp.tile([PART, S], F32, name="h")
+        for s in range(S // first_w):
+            gather_words(2, s * first_w, (s + 1) * first_w)
+            x_pass(first[s][:, :first_w], 0, 0, 2, s * first_w, (s + 1) * first_w)
+            sq = ring.tile([PART, BANK], F32, name="sq", bufs=4)
+            nc.scalar.activation(out=sq[:, :first_w], in_=first[s][:, :first_w], func=ACT.Square)
+            nc.scalar.activation(out=h[0, 0][:, s * first_w : (s + 1) * first_w], in_=sq[:, :first_w], func=ACT.Exp, scale=-1.0)
+
+        for t in range(1, PACK):
+            respond(0, t)
+        cast_w1(1, 0, "vector")
+        match(0, 0, lambda: quant_w1(1, 0), w1_raw[1, 0][:, 0, :])
+        cast_w1(1, 1, "vector")
+        cast_w1(1, 2, "vector")
+        quant_w1(1, 1)
+        quant_w1(1, 2, 0, 128)
+        quant_w1(1, 2, 128, 256)
+        quant_w1(1, 2, 256, 512)
+        for t in range(PACK - 1):
+            respond(1, t)
+        match(0, 1, None, w1_raw[1, 2][:, 0, :])
+        match(0, 2, None, w1_raw[1, 2][:, 1, :])
+        match(0, 3, None, w1_raw[1, 2][:, 2, :])
+        cast_z(0, 0, P, "scalar")
+        respond(1, PACK - 1)
+        nc.scalar.activation(out=warm[:], in_=h[1, PACK - 1][:, S - 1 : S], func=ACT.Sqrt)
+        match(1, 0)
+        match(1, 1)
+        match(1, 2, lambda: quant_z(0, 0, P))
+        for q in range(P // QUARTER):
+            i0, i1 = q * QUARTER, (q + 1) * QUARTER
+            gather_left(1, 3, i0, i1)
+            gather_right(1, 3, i0, i1)
+            cast_z(1, i0, i1, "vector")
+            quant_z(1, i0, i1)
+            pool_costs(q)

@@ -72,12 +72,12 @@ def tile_list_stereo_disparity_cost_kernel(tc, tab_words, tab_scales, offs, pos1
         nc.vector.memset(table_sc[:], 0)
         nc.vector.memset(w2_sc[:], 0)
         nc.sync.dma_start(offs_sb[:], offs)
+        nc.scalar.dma_start(out=gain_sb[:].rearrange("p (b t) -> p b t", t=PACK), in_=gain.rearrange("(b p t) -> p b t", b=R_PASSES, t=PACK))
         load_table(0)
         for a in range(K_PASSES):
-            for q in range(4):
-                queue = nc.gpsimd if (a == 2 and q > 0) else nc.scalar
-                queue.dma_start(out=table_sc[32 * q + 4 * a : 32 * q + 4 * a + 4, :], in_=tab_scales[a, 4 * q : 4 * q + 4, :].bitcast(I32))
-        nc.gpsimd.dma_start(out=gain_sb[:].rearrange("p (b t) -> p b t", t=PACK), in_=gain.rearrange("(b p t) -> p b t", b=R_PASSES, t=PACK))
+            for r in range(4):
+                queue = nc.gpsimd if (a == 2 and r > 0) else nc.scalar
+                queue.dma_start(out=table_sc[4 * a + r : PART : 32, :], in_=tab_scales[a, r:16:4, :].bitcast(I32))
         load_table(1)
         for a in range(K_PASSES):
             load_w1(0, a)
@@ -87,8 +87,8 @@ def tile_list_stereo_disparity_cost_kernel(tc, tab_words, tab_scales, offs, pos1
         for a in range(K_PASSES):
             load_w1(1, a)
         nc.sync.dma_start(out=w2_sb[:], in_=w2_words.rearrange("b p c -> p b c").bitcast(I32))
-        for q in range(4):
-            nc.sync.dma_start(out=w2_sc[32 * q : 32 * q + 4, :, :], in_=w2_scales[:, 4 * q : 4 * q + 4, :].rearrange("b r n -> r b n").bitcast(I32))
+        for r in range(4):
+            nc.sync.dma_start(out=w2_sc[r:PART:32, :, :], in_=w2_scales[:, r:16:4, :].rearrange("b q n -> q b n").bitcast(I32))
 
         def copy_on(engine, dst, src):
             if engine == "scalar":
@@ -125,14 +125,17 @@ def tile_list_stereo_disparity_cost_kernel(tc, tab_words, tab_scales, offs, pos1
 
         h = {}
 
-        def respond(b, t):
+        def respond(b, t, place=None):
             h[b, t] = resp.tile([PART, S], F32, name="h")
             squares = []
             for j0 in range(0, S, BANK):
                 acc = psum_b.tile([PART, BANK], F32, name="x_acc")
                 for a in range(K_PASSES):
                     x_pass(acc[:], b, t, a, j0, j0 + BANK)
-                sq = ring.tile([PART, BANK], F32, name="sq", bufs=4)
+                if place is None:
+                    sq = ring.tile([PART, BANK], F32, name="sq", bufs=4)
+                else:
+                    sq = place[:, j0 // BANK, :]
                 nc.scalar.activation(out=sq[:], in_=acc[:], func=ACT.Square)
                 squares.append(sq)
             for j0, sq in zip(range(0, S, BANK), squares):
@@ -175,27 +178,58 @@ def tile_list_stereo_disparity_cost_kernel(tc, tab_words, tab_scales, offs, pos1
         def quant_z(b, i0, i1):
             nc.vector.quantize_mx(out=z_words[b][:, i0:i1].bitcast(FP8X4), scales=z_sc[b][:, i0:i1], in_=z_bf[b][:, PACK * i0 : PACK * i1])
 
-        def pool_costs(q):
+        def y_pass(acc, nt, b, q):
             cols = slice(q * QUARTER, (q + 1) * QUARTER)
+            nc.tensor.matmul_mx(
+                out=acc,
+                lhsT=w2_sb[:, b, :].bitcast(U8)[:, 2 * PART * nt : 2 * PART * (nt + 1)].bitcast(FP4X4),
+                lhsT_scale=w2_sc[:, b, :].bitcast(U8)[:, PART * nt : PART * (nt + 1)],
+                rhs=z_words[b][:, cols].bitcast(FP8X4),
+                rhs_scale=z_sc[b][:, cols],
+                start=(b == 0),
+                stop=(b == R_PASSES - 1),
+            )
+
+        out_rows = out.rearrange("(nt p) i -> p nt i", p=PART)
+
+        def pool_costs(q):
             acc = psum_a.tile([PART, N // PART, QUARTER], F32, name="bank%d" % q)
             for nt in range(N // PART):
                 for b in range(R_PASSES):
-                    nc.tensor.matmul_mx(
-                        out=acc[:, nt, :],
-                        lhsT=w2_sb[:, b, :].bitcast(U8)[:, 2 * PART * nt : 2 * PART * (nt + 1)].bitcast(FP4X4),
-                        lhsT_scale=w2_sc[:, b, :].bitcast(U8)[:, PART * nt : PART * (nt + 1)],
-                        rhs=z_words[b][:, cols].bitcast(FP8X4),
-                        rhs_scale=z_sc[b][:, cols],
-                        start=(b == 0),
-                        stop=(b == R_PASSES - 1),
-                    )
+                    y_pass(acc[:, nt, :], nt, b, q)
             mag = ring.tile([PART, N // PART, QUARTER], F32, name="mag")
             nc.scalar.activation(out=mag[:], in_=acc[:], func=ACT.Abs)
             cost = ring.tile([PART, N // PART, QUARTER], F32, name="cost", bufs=4)
             nc.scalar.activation(out=cost[:], in_=mag[:], func=ACT.Sqrt)
-            nc.sync.dma_start(out=out.rearrange("(nt p) i -> p nt i", p=PART)[:, :, cols], in_=cost[:])
+            nc.sync.dma_start(out=out_rows[:, :, q * QUARTER : (q + 1) * QUARTER], in_=cost[:])
 
-        nc.scalar.copy(out=gain_wide[:], in_=gain_sb[:].unsqueeze(2).to_broadcast([PART, R_PASSES * PACK, GAIN_W]))
+        def open_quarter(q, pool, name):
+            accs = []
+            for nt in range(N // PART):
+                acc = pool.tile([PART, BANK], F32, name=name.replace("%d", str(nt)))
+                y_pass(acc[:, :QUARTER], nt, 0, q)
+                accs.append(acc)
+            return accs
+
+        def close_quarter(q, accs, engine, step):
+            mag = ring.tile([PART, N // PART, QUARTER], F32, name="mag")
+            cost = ring.tile([PART, N // PART, QUARTER], F32, name="cost", bufs=4)
+            for nt in range(N // PART):
+                y_pass(accs[nt][:, :QUARTER], nt, 1, q)
+            if engine == "scalar":
+                for nt in range(N // PART):
+                    nc.scalar.activation(out=mag[:, nt, :], in_=accs[nt][:, :QUARTER], func=ACT.Abs)
+            else:
+                neg = ring.tile([PART, N // PART, QUARTER], F32, name="neg", bufs=1)
+                for nt in range(N // PART):
+                    nc.vector.tensor_scalar(out=neg[:, nt, :], in0=accs[nt][:, :QUARTER], scalar1=-1.0, scalar2=None, op0=MULT)
+                for nt in range(N // PART):
+                    nc.vector.tensor_tensor(mag[:, nt, :], accs[nt][:, :QUARTER], neg[:, nt, :], mybir.AluOpType.max)
+            for n0 in range(0, N // PART, step):
+                nc.scalar.activation(out=cost[:, n0 : n0 + step, :], in_=mag[:, n0 : n0 + step, :], func=ACT.Sqrt)
+                nc.sync.dma_start(out=out_rows[:, n0 : n0 + step, q * QUARTER : (q + 1) * QUARTER], in_=cost[:, n0 : n0 + step, :])
+
+        nc.vector.tensor_copy(out=gain_wide[:], in_=gain_sb[:].unsqueeze(2).to_broadcast([PART, R_PASSES * PACK, GAIN_W]))
         gather_words(0, 0, S)
         gather_words(1, 0, S)
         nc.vector.tensor_copy(v_sc[:], table_sc[:].bitcast(U8).indirect(offs_sb[:]))
@@ -203,11 +237,11 @@ def tile_list_stereo_disparity_cost_kernel(tc, tab_words, tab_scales, offs, pos1
         cast_w1(0, 1, "vector")
         quant_w1(0, 0)
         quant_w1(0, 1)
-        cast_w1(0, 2, "vector", 0, 80)
-        cast_w1(0, 2, "scalar", 80, PART)
+        cast_w1(0, 2, "vector", 0, 72)
+        cast_w1(0, 2, "scalar", 72, PART)
         quant_w1(0, 2)
         first_w = 256
-        first = [psum_a.tile([PART, BANK], F32, name="bank%d" % s) for s in range(S // first_w)]
+        first = [psum_b.tile([PART, BANK], F32, name="x_acc") for s in range(S // first_w)]
         for s in range(S // first_w):
             x_pass(first[s][:, :first_w], 0, 0, 0, s * first_w, (s + 1) * first_w)
         for s in range(S // first_w):
@@ -220,31 +254,52 @@ def tile_list_stereo_disparity_cost_kernel(tc, tab_words, tab_scales, offs, pos1
             nc.scalar.activation(out=sq[:, :first_w], in_=first[s][:, :first_w], func=ACT.Square)
             nc.scalar.activation(out=h[0, 0][:, s * first_w : (s + 1) * first_w], in_=sq[:, :first_w], func=ACT.Exp, scale=-1.0)
 
-        for t in range(1, PACK):
-            respond(0, t)
+        respond(0, 1)
+        respond(0, 2)
         cast_w1(1, 0, "vector")
         match(0, 0, lambda: quant_w1(1, 0), w1_raw[1, 0][:, 0, :])
-        cast_w1(1, 1, "vector")
-        cast_w1(1, 2, "vector")
-        quant_w1(1, 1)
+        cast_w1(1, 1, "vector", 0, 128)
+        match(0, 1, lambda: quant_w1(1, 1), w1_raw[1, 1][:, 0, :])
+        cast_w1(1, 2, "scalar", 0, PART)
         quant_w1(1, 2, 0, 128)
         quant_w1(1, 2, 128, 256)
         quant_w1(1, 2, 256, 512)
-        for t in range(PACK - 1):
-            respond(1, t)
-        match(0, 1, None, w1_raw[1, 2][:, 0, :])
-        match(0, 2, None, w1_raw[1, 2][:, 1, :])
-        match(0, 3, None, w1_raw[1, 2][:, 2, :])
+        respond(0, 3, w1_raw[1, 2])
+        respond(1, 0)
+        respond(1, 1)
+        respond(1, 2)
+        match(0, 2, None, w1_raw[1, 2][:, 2, :])
+        match(0, 3, None, w1_raw[1, 2][:, 3, :])
         cast_z(0, 0, P, "scalar")
-        respond(1, PACK - 1)
+        respond(1, 3)
         nc.scalar.activation(out=warm[:], in_=h[1, PACK - 1][:, S - 1 : S], func=ACT.Sqrt)
         match(1, 0)
         match(1, 1)
-        match(1, 2, lambda: quant_z(0, 0, P))
-        for q in range(P // QUARTER):
-            i0, i1 = q * QUARTER, (q + 1) * QUARTER
-            gather_left(1, 3, i0, i1)
-            gather_right(1, 3, i0, i1)
-            cast_z(1, i0, i1, "vector")
-            quant_z(1, i0, i1)
-            pool_costs(q)
+        match(1, 2)
+        quant_z(0, 0, P)
+        first_accs = open_quarter(0, psum_a, "bank%d")
+        last_accs = open_quarter(3, psum_b, "x_acc")
+        gather_left(1, 3, 0, 128, None)
+        gather_right(1, 3, 0, 128)
+        cast_z(1, 0, 128, "vector")
+        quant_z(1, 0, 128)
+        close_quarter(0, first_accs, "scalar", 4)
+        gather_left(1, 3, 128, 256, None)
+        gather_right(1, 3, 128, 256)
+        cast_z(1, 128, 256, "vector")
+        quant_z(1, 128, 256)
+        pool_costs(1)
+        gather_left(1, 3, 256, 384, z_f32[1][:, 0, 0:128])
+        gather_right(1, 3, 256, 384)
+        cast_z(1, 256, 384, "vector")
+        quant_z(1, 256, 384)
+        pool_costs(2)
+        gather_left(1, 3, 384, 512, z_f32[1][:, 0, 128:256])
+        left[1, 3, 448] = left[1, 3, 384][:, 64:]
+        gather_right(1, 3, 384, 448)
+        gather_right(1, 3, 448, 512)
+        cast_z(1, 384, 448, "vector")
+        cast_z(1, 448, 512, "vector")
+        quant_z(1, 384, 448)
+        quant_z(1, 448, 512)
+        close_quarter(3, last_accs, "vector", 2)

@@ -23,8 +23,9 @@ K_PASSES = K // PASS
 R_PASSES = H // PASS
 BANK = 512
 STRIPE = 16
-GAIN_W = 256
 QUARTER = 128
+CHUNKS = P // QUARTER
+SPANS = [(0, 256), (256, 384), (384, 512)]
 
 
 def tile_list_stereo_disparity_cost_kernel(tc, tab_words, tab_scales, offs, pos1, pos2, w1, gain, w2_words, w2_scales, out):
@@ -33,14 +34,14 @@ def tile_list_stereo_disparity_cost_kernel(tc, tab_words, tab_scales, offs, pos1
         keep = ctx.enter_context(tc.tile_pool(name="keep", bufs=1))
         ring = ctx.enter_context(tc.tile_pool(name="ring", bufs=3))
         resp = ctx.enter_context(tc.tile_pool(name="resp", bufs=8))
-        psum_a = ctx.enter_context(tc.psum_pool(name="psum_a", bufs=1))
-        psum_b = ctx.enter_context(tc.psum_pool(name="psum_b", bufs=4))
+        psum = ctx.enter_context(tc.psum_pool(name="psum", bufs=8))
 
         offs_sb = keep.tile([PART, S // STRIPE], U16, name="offs_sb")
         pos1_sb = keep.tile([PART, P // STRIPE], U16, name="pos1_sb")
         pos2_sb = keep.tile([PART, P // STRIPE], U16, name="pos2_sb")
         gain_sb = keep.tile([PART, R_PASSES * PACK], F32, name="gain_sb")
-        gain_wide = keep.tile([PART, R_PASSES * PACK, GAIN_W], F32, name="gain_wide")
+        lane0 = keep.tile([PART, PACK + 1, P], F32, name="lane0")
+        lane1 = [keep.tile([PART, PACK + 1, i1 - i0], F32, name="lane1_%d" % i0) for i0, i1 in SPANS]
         table = [keep.tile([PART, T], I32, name="table%d" % a, align_bytes=64) for a in range(K_PASSES)]
         table_sc = keep.tile([PART, T // 4], I32, name="table_sc", align_bytes=64)
         v_words = [keep.tile([PART, S], U32, name="v_words%d" % a, align_bytes=64) for a in range(K_PASSES)]
@@ -56,8 +57,6 @@ def tile_list_stereo_disparity_cost_kernel(tc, tab_words, tab_scales, offs, pos1
                 w1_sc[b, a] = keep.tile([PART, PASS], U8, name="w1_sc%d%d" % (b, a), align_bytes=64)
         w2_sb = keep.tile([PART, R_PASSES, N // 2], I32, name="w2_sb", align_bytes=64)
         w2_sc = keep.tile([PART, R_PASSES, N // 4], I32, name="w2_sc", align_bytes=64)
-        z_f32 = [keep.tile([PART, PACK, P], F32, name="z_f32%d" % b) for b in range(R_PASSES)]
-        z_bf = [keep.tile([PART, P * PACK], BF16, name="z_bf%d" % b, align_bytes=64) for b in range(R_PASSES)]
         z_words = [keep.tile([PART, P], U32, name="z_words%d" % b, align_bytes=64) for b in range(R_PASSES)]
         z_sc = [keep.tile([PART, P], U8, name="z_sc%d" % b, align_bytes=64) for b in range(R_PASSES)]
         warm = keep.tile([PART, 1], F32, name="warm")
@@ -69,18 +68,23 @@ def tile_list_stereo_disparity_cost_kernel(tc, tab_words, tab_scales, offs, pos1
         def load_table(a):
             nc.sync.dma_start(out=table[a][:], in_=tab_words[a].rearrange("p t i -> p (t i)").bitcast(I32))
 
+        def load_scales(queue, rows):
+            for a, r in rows:
+                queue.dma_start(out=table_sc[4 * a + r : PART : 32, :], in_=tab_scales[a, r:16:4, :].bitcast(I32))
+
+        scale_rows = [(a, r) for a in range(K_PASSES) for r in range(4)]
         nc.vector.memset(table_sc[:], 0)
         nc.vector.memset(w2_sc[:], 0)
         nc.sync.dma_start(offs_sb[:], offs)
-        nc.scalar.dma_start(out=gain_sb[:].rearrange("p (b t) -> p b t", t=PACK), in_=gain.rearrange("(b p t) -> p b t", b=R_PASSES, t=PACK))
         load_table(0)
-        for a in range(K_PASSES):
-            for r in range(4):
-                queue = nc.gpsimd if (a == 2 and r > 0) else nc.scalar
-                queue.dma_start(out=table_sc[4 * a + r : PART : 32, :], in_=tab_scales[a, r:16:4, :].bitcast(I32))
+        nc.sync.dma_start(out=gain_sb[:].rearrange("p (b t) -> p b t", t=PACK), in_=gain.rearrange("(b p t) -> p b t", b=R_PASSES, t=PACK))
+        load_scales(nc.gpsimd, scale_rows[10:])
+        load_scales(nc.sync, scale_rows[:4])
         load_table(1)
-        for a in range(K_PASSES):
-            load_w1(0, a)
+        load_scales(nc.sync, scale_rows[4:10])
+        load_w1(0, 0)
+        load_w1(0, 1)
+        load_w1(0, 2)
         load_table(2)
         nc.sync.dma_start(pos1_sb[:], pos1)
         nc.sync.dma_start(pos2_sb[:], pos2)
@@ -125,60 +129,32 @@ def tile_list_stereo_disparity_cost_kernel(tc, tab_words, tab_scales, offs, pos1
 
         h = {}
 
-        def respond(b, t, place=None):
+        def respond(b, t, sq):
             h[b, t] = resp.tile([PART, S], F32, name="h")
-            squares = []
             for j0 in range(0, S, BANK):
-                acc = psum_b.tile([PART, BANK], F32, name="x_acc")
+                acc = psum.tile([PART, BANK], F32, name="bank")
                 for a in range(K_PASSES):
                     x_pass(acc[:], b, t, a, j0, j0 + BANK)
-                if place is None:
-                    sq = ring.tile([PART, BANK], F32, name="sq", bufs=4)
-                else:
-                    sq = place[:, j0 // BANK, :]
-                nc.scalar.activation(out=sq[:], in_=acc[:], func=ACT.Square)
-                squares.append(sq)
-            for j0, sq in zip(range(0, S, BANK), squares):
-                nc.scalar.activation(out=h[b, t][:, j0 : j0 + BANK], in_=sq[:], func=ACT.Exp, scale=-1.0)
+                nc.scalar.activation(out=sq[:, j0 : j0 + BANK], in_=acc[:], func=ACT.Square)
+            for j0 in range(0, S, BANK):
+                nc.scalar.activation(out=h[b, t][:, j0 : j0 + BANK], in_=sq[:, j0 : j0 + BANK], func=ACT.Exp, scale=-1.0)
 
-        left = {}
+        def new_sq():
+            return ring.tile([PART, S], F32, name="sq", bufs=2)
 
-        def gather_left(b, t, i0, i1, place=None):
-            if place is None:
-                place = ring.tile([PART, GAIN_W], F32, name="left", bufs=4)
-            left[b, t, i0] = place
-            nc.vector.tensor_tensor(
-                left[b, t, i0][:, : i1 - i0],
-                h[b, t][:].indirect(pos1_sb[:, i0 // STRIPE : i1 // STRIPE]),
-                gain_wide[:, PACK * b + t, : i1 - i0],
-                MULT,
-            )
+        def gather_left(b, t, i0, i1, left, gains):
+            nc.vector.tensor_tensor(left, h[b, t][:].indirect(pos1_sb[:, i0 // STRIPE : i1 // STRIPE]), gains, MULT)
 
-        def gather_right(b, t, i0, i1):
-            nc.vector.tensor_tensor(
-                z_f32[b][:, t, i0:i1],
-                h[b, t][:].indirect(pos2_sb[:, i0 // STRIPE : i1 // STRIPE]),
-                left[b, t, i0][:, : i1 - i0],
-                MULT,
-            )
+        def gather_right(b, t, i0, i1, left, z):
+            nc.vector.tensor_tensor(z, h[b, t][:].indirect(pos2_sb[:, i0 // STRIPE : i1 // STRIPE]), left, MULT)
 
-        def match(b, t, between=None, place=None):
-            for i0 in range(0, P, GAIN_W):
-                gather_left(b, t, i0, i0 + GAIN_W, None if place is None else place[:, i0 : i0 + GAIN_W])
-            if between is not None:
-                between()
-            for i0 in range(0, P, GAIN_W):
-                gather_right(b, t, i0, i0 + GAIN_W)
+        def cast_z(dst, src, engine):
+            copy_on(engine, dst.rearrange("p (c i t) -> p c t i", i=4, t=PACK), src.rearrange("p t (c i) -> p c t i", i=4))
 
-        def cast_z(b, i0, i1, engine):
-            dst = z_bf[b][:, PACK * i0 : PACK * i1].rearrange("p (c i t) -> p c t i", i=4, t=PACK)
-            src = z_f32[b][:, :, i0:i1].rearrange("p t (c i) -> p c t i", i=4)
-            copy_on(engine, dst, src)
+        def quant_z(b, i0, i1, src):
+            nc.vector.quantize_mx(out=z_words[b][:, i0:i1].bitcast(FP8X4), scales=z_sc[b][:, i0:i1], in_=src)
 
-        def quant_z(b, i0, i1):
-            nc.vector.quantize_mx(out=z_words[b][:, i0:i1].bitcast(FP8X4), scales=z_sc[b][:, i0:i1], in_=z_bf[b][:, PACK * i0 : PACK * i1])
-
-        def y_pass(acc, nt, b, q):
+        def y_pass(acc, nt, b, q, start, stop):
             cols = slice(q * QUARTER, (q + 1) * QUARTER)
             nc.tensor.matmul_mx(
                 out=acc,
@@ -186,50 +162,33 @@ def tile_list_stereo_disparity_cost_kernel(tc, tab_words, tab_scales, offs, pos1
                 lhsT_scale=w2_sc[:, b, :].bitcast(U8)[:, PART * nt : PART * (nt + 1)],
                 rhs=z_words[b][:, cols].bitcast(FP8X4),
                 rhs_scale=z_sc[b][:, cols],
-                start=(b == 0),
-                stop=(b == R_PASSES - 1),
+                start=start,
+                stop=stop,
             )
 
         out_rows = out.rearrange("(nt p) i -> p nt i", p=PART)
+        y_acc = {}
 
-        def pool_costs(q):
-            acc = psum_a.tile([PART, N // PART, QUARTER], F32, name="bank%d" % q)
-            for nt in range(N // PART):
-                for b in range(R_PASSES):
-                    y_pass(acc[:, nt, :], nt, b, q)
-            mag = ring.tile([PART, N // PART, QUARTER], F32, name="mag")
-            nc.scalar.activation(out=mag[:], in_=acc[:], func=ACT.Abs)
-            cost = ring.tile([PART, N // PART, QUARTER], F32, name="cost", bufs=4)
-            nc.scalar.activation(out=cost[:], in_=mag[:], func=ACT.Sqrt)
-            nc.sync.dma_start(out=out_rows[:, :, q * QUARTER : (q + 1) * QUARTER], in_=cost[:])
+        def open_y(q, n0, n1):
+            y_acc[q, n0] = psum.tile([PART, N // PART, QUARTER], F32, name="bank")
+            for nt in range(n0, n1):
+                y_pass(y_acc[q, n0][:, nt - n0, :], nt, 0, q, nt == n0, False)
 
-        def open_quarter(q, pool, name):
-            accs = []
-            for nt in range(N // PART):
-                acc = pool.tile([PART, BANK], F32, name=name.replace("%d", str(nt)))
-                y_pass(acc[:, :QUARTER], nt, 0, q)
-                accs.append(acc)
-            return accs
+        def close_y(q, n0, n1):
+            for nt in range(n0, n1):
+                y_pass(y_acc[q, n0][:, nt - n0, :], nt, 1, q, False, nt == n1 - 1)
 
-        def close_quarter(q, accs, engine, step):
-            mag = ring.tile([PART, N // PART, QUARTER], F32, name="mag")
-            cost = ring.tile([PART, N // PART, QUARTER], F32, name="cost", bufs=4)
-            for nt in range(N // PART):
-                y_pass(accs[nt][:, :QUARTER], nt, 1, q)
-            if engine == "scalar":
-                for nt in range(N // PART):
-                    nc.scalar.activation(out=mag[:, nt, :], in_=accs[nt][:, :QUARTER], func=ACT.Abs)
-            else:
-                neg = ring.tile([PART, N // PART, QUARTER], F32, name="neg", bufs=1)
-                for nt in range(N // PART):
-                    nc.vector.tensor_scalar(out=neg[:, nt, :], in0=accs[nt][:, :QUARTER], scalar1=-1.0, scalar2=None, op0=MULT)
-                for nt in range(N // PART):
-                    nc.vector.tensor_tensor(mag[:, nt, :], accs[nt][:, :QUARTER], neg[:, nt, :], mybir.AluOpType.max)
-            for n0 in range(0, N // PART, step):
-                nc.scalar.activation(out=cost[:, n0 : n0 + step, :], in_=mag[:, n0 : n0 + step, :], func=ACT.Sqrt)
-                nc.sync.dma_start(out=out_rows[:, n0 : n0 + step, q * QUARTER : (q + 1) * QUARTER], in_=cost[:, n0 : n0 + step, :])
+        def magnitude(q, n0, n1, mag):
+            nc.scalar.activation(out=mag[:, n0:n1, :], in_=y_acc[q, n0][:, : n1 - n0, :], func=ACT.Abs)
 
-        nc.vector.tensor_copy(out=gain_wide[:], in_=gain_sb[:].unsqueeze(2).to_broadcast([PART, R_PASSES * PACK, GAIN_W]))
+        def root_and_store(q, n0, n1, mag):
+            cost = ring.tile([PART, N // PART, QUARTER], F32, name="cost", bufs=5)
+            nc.scalar.activation(out=cost[:, n0:n1, :], in_=mag[:, n0:n1, :], func=ACT.Sqrt)
+            nc.sync.dma_start(out=out_rows[:, n0:n1, q * QUARTER : (q + 1) * QUARTER], in_=cost[:, n0:n1, :])
+
+        nc.scalar.copy(out=lane0[:, :PACK, :], in_=gain_sb[:, :PACK].unsqueeze(2).to_broadcast([PART, PACK, P]))
+        for lane, (i0, i1) in zip(lane1, SPANS):
+            nc.scalar.copy(out=lane[:, :PACK, :], in_=gain_sb[:, PACK:].unsqueeze(2).to_broadcast([PART, PACK, i1 - i0]))
         gather_words(0, 0, S)
         gather_words(1, 0, S)
         nc.vector.tensor_copy(v_sc[:], table_sc[:].bitcast(U8).indirect(offs_sb[:]))
@@ -241,65 +200,126 @@ def tile_list_stereo_disparity_cost_kernel(tc, tab_words, tab_scales, offs, pos1
         cast_w1(0, 2, "scalar", 72, PART)
         quant_w1(0, 2)
         first_w = 256
-        first = [psum_b.tile([PART, BANK], F32, name="x_acc") for s in range(S // first_w)]
+        first = [psum.tile([PART, BANK], F32, name="bank") for s in range(S // first_w)]
         for s in range(S // first_w):
             x_pass(first[s][:, :first_w], 0, 0, 0, s * first_w, (s + 1) * first_w)
         for s in range(S // first_w):
             x_pass(first[s][:, :first_w], 0, 0, 1, s * first_w, (s + 1) * first_w)
         h[0, 0] = resp.tile([PART, S], F32, name="h")
+        sq = new_sq()
         for s in range(S // first_w):
+            cols = slice(s * first_w, (s + 1) * first_w)
             gather_words(2, s * first_w, (s + 1) * first_w)
             x_pass(first[s][:, :first_w], 0, 0, 2, s * first_w, (s + 1) * first_w)
-            sq = ring.tile([PART, BANK], F32, name="sq", bufs=4)
-            nc.scalar.activation(out=sq[:, :first_w], in_=first[s][:, :first_w], func=ACT.Square)
-            nc.scalar.activation(out=h[0, 0][:, s * first_w : (s + 1) * first_w], in_=sq[:, :first_w], func=ACT.Exp, scale=-1.0)
+            nc.scalar.activation(out=sq[:, cols], in_=first[s][:, :first_w], func=ACT.Square)
+            nc.scalar.activation(out=h[0, 0][:, cols], in_=sq[:, cols], func=ACT.Exp, scale=-1.0)
 
-        respond(0, 1)
-        respond(0, 2)
+        for t in range(1, PACK):
+            respond(0, t, new_sq())
+        lefts = [w1_raw[1, 1][:, 0, :]] + [w1_raw[1, 2][:, j, :] for j in range(PACK - 1)]
         cast_w1(1, 0, "vector")
-        match(0, 0, lambda: quant_w1(1, 0), w1_raw[1, 0][:, 0, :])
-        cast_w1(1, 1, "vector", 0, 128)
-        match(0, 1, lambda: quant_w1(1, 1), w1_raw[1, 1][:, 0, :])
-        cast_w1(1, 2, "scalar", 0, PART)
+        quant_w1(1, 0)
+        cast_w1(1, 1, "vector")
+        gather_left(0, 0, 0, P, lefts[0], lane0[:, 0, :])
+        quant_w1(1, 1)
+        cast_w1(1, 2, "vector")
         quant_w1(1, 2, 0, 128)
+        gather_left(0, 1, 0, P, lefts[1], lane0[:, 1, :])
         quant_w1(1, 2, 128, 256)
         quant_w1(1, 2, 256, 512)
-        respond(0, 3, w1_raw[1, 2])
-        respond(1, 0)
-        respond(1, 1)
-        respond(1, 2)
-        match(0, 2, None, w1_raw[1, 2][:, 2, :])
-        match(0, 3, None, w1_raw[1, 2][:, 3, :])
-        cast_z(0, 0, P, "scalar")
-        respond(1, 3)
+        for t in range(PACK - 1):
+            respond(1, t, new_sq())
+        respond(1, PACK - 1, ring.tile([PART, S], F32, name="sq_last", tag="z0", bufs=1, align_bytes=64))
+        for t in range(PACK):
+            if t + 2 < PACK:
+                gather_left(0, t + 2, 0, P, lefts[t + 2], lane0[:, t + 2, :])
+            gather_right(0, t, 0, P, lefts[t], lane0[:, t + 1, :])
         nc.scalar.activation(out=warm[:], in_=h[1, PACK - 1][:, S - 1 : S], func=ACT.Sqrt)
-        match(1, 0)
-        match(1, 1)
-        match(1, 2)
-        quant_z(0, 0, P)
-        first_accs = open_quarter(0, psum_a, "bank%d")
-        last_accs = open_quarter(3, psum_b, "x_acc")
-        gather_left(1, 3, 0, 128, None)
-        gather_right(1, 3, 0, 128)
-        cast_z(1, 0, 128, "vector")
-        quant_z(1, 0, 128)
-        close_quarter(0, first_accs, "scalar", 4)
-        gather_left(1, 3, 128, 256, None)
-        gather_right(1, 3, 128, 256)
-        cast_z(1, 128, 256, "vector")
-        quant_z(1, 128, 256)
-        pool_costs(1)
-        gather_left(1, 3, 256, 384, z_f32[1][:, 0, 0:128])
-        gather_right(1, 3, 256, 384)
-        cast_z(1, 256, 384, "vector")
-        quant_z(1, 256, 384)
-        pool_costs(2)
-        gather_left(1, 3, 384, 512, z_f32[1][:, 0, 128:256])
-        left[1, 3, 448] = left[1, 3, 384][:, 64:]
-        gather_right(1, 3, 384, 448)
-        gather_right(1, 3, 448, 512)
-        cast_z(1, 384, 448, "vector")
-        cast_z(1, 448, 512, "vector")
-        quant_z(1, 384, 448)
-        quant_z(1, 448, 512)
-        close_quarter(3, last_accs, "vector", 2)
+        z0_bf = ring.tile([PART, P * PACK], BF16, name="z0_bf", tag="z0", bufs=1, align_bytes=64)
+        cast_z(z0_bf[:], lane0[:, 1:, :], "scalar")
+
+        steps = len(SPANS) * PACK
+        used = {}
+        z1_bf = {}
+
+        def left_step(k):
+            c, t = divmod(k, PACK)
+            i0, i1 = SPANS[c]
+            used[k] = lefts[t][:, : i1 - i0]
+            gather_left(1, t, i0, i1, used[k], lane1[c][:, t, :])
+
+        def right_step(k, c0=0, c1=None):
+            c, t = divmod(k, PACK)
+            i0, i1 = SPANS[c]
+            if c1 is None:
+                c1 = i1 - i0
+            gather_right(1, t, i0 + c0, i0 + c1, used[k][:, c0:c1], lane1[c][:, t + 1, c0:c1])
+
+        def advance(k0, k1):
+            for k in range(k0, k1):
+                if k < steps:
+                    left_step(k)
+                right_step(k - 2)
+
+        def cast_chunk(c):
+            i0, i1 = SPANS[c]
+            z1_bf[c] = ring.tile([PART, (i1 - i0) * PACK], BF16, name="z1_bf", tag="c%d" % c, bufs=1, align_bytes=64)
+            cast_z(z1_bf[c][:], lane1[c][:, 1:, :], "scalar")
+
+        def quant_chunk(c):
+            quant_z(1, SPANS[c][0], SPANS[c][1], z1_bf[c][:])
+
+        def move_lefts(tag):
+            place = ring.tile([PART, 2, QUARTER], F32, name="left", tag=tag, bufs=1, align_bytes=64)
+            lefts[0] = place[:, 0, :]
+            lefts[1] = place[:, 1, :]
+
+        def finish(q):
+            mag = ring.tile([PART, N // PART, QUARTER], F32, name="mag", bufs=2)
+            magnitude(q, 0, 4, mag)
+            return mag
+
+        left_step(0)
+        left_step(1)
+        advance(2, 4)
+        right_step(2)
+        right_step(3)
+        quant_z(0, 0, P, z0_bf[:])
+        cast_chunk(0)
+        move_lefts("z0")
+        left_step(4)
+        left_step(5)
+        advance(6, 8)
+        quant_chunk(0)
+        for q in (0, 1):
+            open_y(q, 0, 4)
+            close_y(q, 0, 4)
+        open_y(2, 0, 4)
+        open_y(3, 0, 2)
+        open_y(3, 2, 4)
+        move_lefts("c0")
+        advance(8, 10)
+        cast_chunk(1)
+        mags = [finish(0), finish(1)]
+        root_and_store(0, 0, 4, mags[0])
+        root_and_store(1, 0, 4, mags[1])
+        advance(10, 13)
+        quant_chunk(1)
+        close_y(2, 0, 4)
+        root_and_store(2, 0, 4, finish(2))
+        last = CHUNKS - 1
+        half = QUARTER // 2
+        z_last = ring.tile([PART, QUARTER * PACK], BF16, name="z1_last", bufs=1, align_bytes=64)
+        for c0 in (0, half):
+            right_step(steps - 1, c0, c0 + half)
+        for c0 in (0, half):
+            cast_z(z_last[:, PACK * c0 : PACK * (c0 + half)], lane1[-1][:, 1:, c0 : c0 + half], "vector")
+        for c0 in (0, half):
+            quant_z(1, last * QUARTER + c0, last * QUARTER + c0 + half, z_last[:, PACK * c0 : PACK * (c0 + half)])
+        close_y(last, 0, 2)
+        close_y(last, 2, 4)
+        mag_last = ring.tile([PART, N // PART, QUARTER], F32, name="mag_last", bufs=1)
+        magnitude(last, 0, 2, mag_last)
+        magnitude(last, 2, 4, mag_last)
+        root_and_store(last, 0, 2, mag_last)
+        root_and_store(last, 2, 4, mag_last)

@@ -24,6 +24,9 @@ R_PASSES = H // PASS
 BANK = 512
 STRIPE = 16
 QUARTER = 128
+GAIN_W = 256
+HALF = 64
+GROUPS = [(0, 256), (256, 512), (512, 1024)]
 CHUNKS = P // QUARTER
 SPANS = [(0, 256), (256, 384), (384, 512)]
 
@@ -39,22 +42,25 @@ def tile_list_stereo_disparity_cost_kernel(tc, tab_words, tab_scales, offs, pos1
         offs_sb = keep.tile([PART, S // STRIPE], U16, name="offs_sb")
         pos1_sb = keep.tile([PART, P // STRIPE], U16, name="pos1_sb")
         pos2_sb = keep.tile([PART, P // STRIPE], U16, name="pos2_sb")
+        gain_raw = keep.tile([PART, PACK, PACK], F32, name="gain_raw")
         gain_sb = keep.tile([PART, R_PASSES * PACK], F32, name="gain_sb")
-        lane0 = keep.tile([PART, PACK + 1, P], F32, name="lane0")
-        lane1 = [keep.tile([PART, PACK + 1, i1 - i0], F32, name="lane1_%d" % i0) for i0, i1 in SPANS]
-        table = [keep.tile([PART, T], I32, name="table%d" % a, align_bytes=64) for a in range(K_PASSES)]
+        gain_wide = keep.tile([PART, R_PASSES * PACK - 1, GAIN_W], F32, name="gain_wide")
+        z0_late = keep.tile([PART, 2, P], F32, name="z0_late")
+        rows = keep.tile([PART, PACK, S], F32, name="rows", align_bytes=64)
+        z_last = keep.tile([PART, PACK, QUARTER], F32, name="z_last")
+        table = [keep.tile([PART, T], I32, name="table", tag="table%d" % a, align_bytes=64) for a in range(K_PASSES)]
         table_sc = keep.tile([PART, T // 4], I32, name="table_sc", align_bytes=64)
         v_words = [keep.tile([PART, S], U32, name="v_words%d" % a, align_bytes=64) for a in range(K_PASSES)]
         v_sc = keep.tile([PART, S], U8, name="v_sc", align_bytes=64)
         w1_raw = {}
         w1_bf = {}
+        w1_stage = {}
         w1_words = {}
         w1_sc = {}
-        for b in range(R_PASSES):
+        for b, (r0, r1) in enumerate(GROUPS):
             for a in range(K_PASSES):
-                w1_raw[b, a] = keep.tile([PART, PACK, PASS], F32, name="w1_raw%d%d" % (b, a))
-                w1_words[b, a] = keep.tile([PART, PASS], U32, name="w1_words%d%d" % (b, a), align_bytes=64)
-                w1_sc[b, a] = keep.tile([PART, PASS], U8, name="w1_sc%d%d" % (b, a), align_bytes=64)
+                w1_raw[b, a] = keep.tile([PART, PACK, r1 - r0], F32, name="w1_raw", tag="raw%d%d" % (b, a), align_bytes=64)
+                w1_sc[b, a] = keep.tile([PART, r1 - r0], U8, name="w1_sc%d%d" % (b, a), align_bytes=64)
         w2_sb = keep.tile([PART, R_PASSES, N // 2], I32, name="w2_sb", align_bytes=64)
         w2_sc = keep.tile([PART, R_PASSES, N // 4], I32, name="w2_sc", align_bytes=64)
         z_words = [keep.tile([PART, P], U32, name="z_words%d" % b, align_bytes=64) for b in range(R_PASSES)]
@@ -62,34 +68,35 @@ def tile_list_stereo_disparity_cost_kernel(tc, tab_words, tab_scales, offs, pos1
         warm = keep.tile([PART, 1], F32, name="warm")
 
         def load_w1(b, a):
-            rows = w1[a * PASS : (a + 1) * PASS, b * PASS : (b + 1) * PASS]
+            rows = w1[a * PASS : (a + 1) * PASS, GROUPS[b][0] : GROUPS[b][1]]
             nc.sync.dma_start(out=w1_raw[b, a][:], in_=rows.rearrange("(p j) c -> p j c", j=PACK))
 
         def load_table(a):
             nc.sync.dma_start(out=table[a][:], in_=tab_words[a].rearrange("p t i -> p (t i)").bitcast(I32))
 
-        def load_scales(queue, rows):
-            for a, r in rows:
-                queue.dma_start(out=table_sc[4 * a + r : PART : 32, :], in_=tab_scales[a, r:16:4, :].bitcast(I32))
+        def load_scales(queue, q):
+            queue.dma_start(out=table_sc[32 * q : 32 * q + 12, :], in_=tab_scales[:, 4 * q : 4 * q + 4, :].bitcast(I32))
 
-        scale_rows = [(a, r) for a in range(K_PASSES) for r in range(4)]
-        nc.vector.memset(table_sc[:], 0)
+        nc.gpsimd.memset(table_sc[:], 0)
         nc.vector.memset(w2_sc[:], 0)
         nc.sync.dma_start(offs_sb[:], offs)
+        for e in range(2):
+            nc.scalar.dma_start(out=gain_raw[HALF * e : HALF * (e + 1)], in_=gain.rearrange("(k m t) -> m k t", k=PACK, t=PACK))
         load_table(0)
-        nc.sync.dma_start(out=gain_sb[:].rearrange("p (b t) -> p b t", t=PACK), in_=gain.rearrange("(b p t) -> p b t", b=R_PASSES, t=PACK))
-        load_scales(nc.gpsimd, scale_rows[10:])
-        load_scales(nc.sync, scale_rows[:4])
-        load_table(1)
-        load_scales(nc.sync, scale_rows[4:10])
+        for q in range(4):
+            load_scales(nc.sync if q < 2 else nc.scalar, q)
         load_w1(0, 0)
+        load_table(1)
         load_w1(0, 1)
-        load_w1(0, 2)
         load_table(2)
-        nc.sync.dma_start(pos1_sb[:], pos1)
-        nc.sync.dma_start(pos2_sb[:], pos2)
+        load_w1(0, 2)
         for a in range(K_PASSES):
             load_w1(1, a)
+        load_w1(2, 0)
+        nc.sync.dma_start(pos1_sb[:], pos1)
+        load_w1(2, 1)
+        nc.sync.dma_start(pos2_sb[:], pos2)
+        load_w1(2, 2)
         nc.sync.dma_start(out=w2_sb[:], in_=w2_words.rearrange("b p c -> p b c").bitcast(I32))
         for r in range(4):
             nc.sync.dma_start(out=w2_sc[r:PART:32, :, :], in_=w2_scales[:, r:16:4, :].rearrange("b q n -> q b n").bitcast(I32))
@@ -100,14 +107,21 @@ def tile_list_stereo_disparity_cost_kernel(tc, tab_words, tab_scales, offs, pos1
             else:
                 nc.vector.tensor_copy(out=dst, in_=src)
 
-        def cast_w1(b, a, engine, m0=0, m1=PART):
+        def cast_w1(b, a, engine, place=None, t0=0, t1=PACK):
+            width = GROUPS[b][1] - GROUPS[b][0]
             if (b, a) not in w1_bf:
-                w1_bf[b, a] = ring.tile([PART, PASS * PACK], BF16, name="w1_bf", align_bytes=64)
-            dst = w1_bf[b, a][:].rearrange("p (t m j) -> p m j t", t=PACK, j=PACK)[:, m0:m1]
-            src = w1_raw[b, a][:].rearrange("p j (m t) -> p m j t", t=PACK)[:, m0:m1]
+                w1_stage[b, a] = keep.tile([PART, width * PACK // 2], F32, name="w1_bf", tag=place or "bf%d%d" % (b, a), align_bytes=64)
+                w1_bf[b, a] = w1_stage[b, a][:].bitcast(BF16)
+            dst = w1_bf[b, a].rearrange("p (t m j) -> p m j t", t=PACK, j=PACK)[:, :, :, t0:t1]
+            src = w1_raw[b, a][:].rearrange("p j (m t) -> p m j t", t=PACK)[:, :, :, t0:t1]
             copy_on(engine, dst, src)
 
-        def quant_w1(b, a, c0=0, c1=PASS):
+        def quant_w1(b, a, c0=0, c1=None, place=None):
+            width = GROUPS[b][1] - GROUPS[b][0]
+            if c1 is None:
+                c1 = width
+            if (b, a) not in w1_words:
+                w1_words[b, a] = keep.tile([PART, width], U32, name="w1_words", tag=place or "words%d%d" % (b, a), align_bytes=64)
             nc.vector.quantize_mx(
                 out=w1_words[b, a][:, c0:c1].bitcast(FP8X4), scales=w1_sc[b, a][:, c0:c1], in_=w1_bf[b, a][:, PACK * c0 : PACK * c1]
             )
@@ -129,11 +143,11 @@ def tile_list_stereo_disparity_cost_kernel(tc, tab_words, tab_scales, offs, pos1
 
         h = {}
 
-        def respond(b, t, sq):
+        def respond(b, t, sq, opened=None):
             h[b, t] = resp.tile([PART, S], F32, name="h")
             for j0 in range(0, S, BANK):
-                acc = psum.tile([PART, BANK], F32, name="bank")
-                for a in range(K_PASSES):
+                acc = psum.tile([PART, BANK], F32, name="bank") if opened is None else opened[j0 // BANK]
+                for a in range(0 if opened is None else K_PASSES - 1, K_PASSES):
                     x_pass(acc[:], b, t, a, j0, j0 + BANK)
                 nc.scalar.activation(out=sq[:, j0 : j0 + BANK], in_=acc[:], func=ACT.Square)
             for j0 in range(0, S, BANK):
@@ -186,140 +200,168 @@ def tile_list_stereo_disparity_cost_kernel(tc, tab_words, tab_scales, offs, pos1
             nc.scalar.activation(out=cost[:, n0:n1, :], in_=mag[:, n0:n1, :], func=ACT.Sqrt)
             nc.sync.dma_start(out=out_rows[:, n0:n1, q * QUARTER : (q + 1) * QUARTER], in_=cost[:, n0:n1, :])
 
-        nc.scalar.copy(out=lane0[:, :PACK, :], in_=gain_sb[:, :PACK].unsqueeze(2).to_broadcast([PART, PACK, P]))
-        for lane, (i0, i1) in zip(lane1, SPANS):
-            nc.scalar.copy(out=lane[:, :PACK, :], in_=gain_sb[:, PACK:].unsqueeze(2).to_broadcast([PART, PACK, i1 - i0]))
+        for e in range(2):
+            half = slice(HALF * e, HALF * (e + 1))
+            nc.scalar.copy(out=gain_sb[half, :PACK].rearrange("p (c u) -> p c u", u=2), in_=gain_raw[half, 0:2, e:PACK:2])
+            nc.scalar.copy(out=gain_sb[half, PACK:], in_=gain_raw[half, 2 + e, :])
+        gains = [gain_wide[:, 0, :], z0_late[:, 0, :GAIN_W]] + [gain_wide[:, k, :] for k in range(1, R_PASSES * PACK - 1)]
+        for k in range(2):
+            nc.scalar.copy(out=gains[k], in_=gain_sb[:, k : k + 1].to_broadcast([PART, GAIN_W]))
+        nc.scalar.copy(out=gain_wide[:, 1:, :], in_=gain_sb[:, 2:].unsqueeze(2).to_broadcast([PART, R_PASSES * PACK - 2, GAIN_W]))
         gather_words(0, 0, S)
-        gather_words(1, 0, S)
         nc.vector.tensor_copy(v_sc[:], table_sc[:].bitcast(U8).indirect(offs_sb[:]))
         cast_w1(0, 0, "scalar")
-        cast_w1(0, 1, "vector")
         quant_w1(0, 0)
+        gather_words(1, 0, S)
+        cast_w1(0, 1, "scalar")
         quant_w1(0, 1)
-        cast_w1(0, 2, "vector", 0, 72)
-        cast_w1(0, 2, "scalar", 72, PART)
-        quant_w1(0, 2)
-        first_w = 256
-        first = [psum.tile([PART, BANK], F32, name="bank") for s in range(S // first_w)]
-        for s in range(S // first_w):
-            x_pass(first[s][:, :first_w], 0, 0, 0, s * first_w, (s + 1) * first_w)
-        for s in range(S // first_w):
-            x_pass(first[s][:, :first_w], 0, 0, 1, s * first_w, (s + 1) * first_w)
-        h[0, 0] = resp.tile([PART, S], F32, name="h")
-        sq = new_sq()
-        for s in range(S // first_w):
-            cols = slice(s * first_w, (s + 1) * first_w)
-            gather_words(2, s * first_w, (s + 1) * first_w)
-            x_pass(first[s][:, :first_w], 0, 0, 2, s * first_w, (s + 1) * first_w)
-            nc.scalar.activation(out=sq[:, cols], in_=first[s][:, :first_w], func=ACT.Square)
-            nc.scalar.activation(out=h[0, 0][:, cols], in_=sq[:, cols], func=ACT.Exp, scale=-1.0)
+        opened = [[psum.tile([PART, BANK], F32, name="bank") for j0 in range(0, S, BANK)] for u in range(2)]
+        for a in range(K_PASSES - 1):
+            for u in range(2):
+                for j0 in range(0, S, BANK):
+                    x_pass(opened[u][j0 // BANK][:], 0, u, a, j0, j0 + BANK)
+        for j0 in range(0, S, BANK):
+            gather_words(2, j0, j0 + BANK)
+        cast_w1(0, 2, "scalar")
+        quant_w1(0, 2, 0, 128)
+        quant_w1(0, 2, 128, 256)
+        respond(0, 0, new_sq(), opened[0])
+        respond(0, 1, new_sq(), opened[1])
+        def flat(raw):
+            return raw.rearrange("p j c -> p (j c)")
 
-        for t in range(1, PACK):
-            respond(0, t, new_sq())
-        lefts = [w1_raw[1, 1][:, 0, :]] + [w1_raw[1, 2][:, j, :] for j in range(PACK - 1)]
-        cast_w1(1, 0, "vector")
-        quant_w1(1, 0)
+        def match_left(k, left, lo=0, hi=P):
+            c, u = divmod(k, 2)
+            for i0 in range(lo, hi, GAIN_W):
+                gather_left(c, u, i0, i0 + GAIN_W, left[:, i0 : i0 + GAIN_W], gains[k])
+
+        def match_right(k, left):
+            c, u = divmod(k, 2)
+            if c == 0:
+                gather_right(c, u, 0, P, left, z0[:, 2 * u, :])
+                nc.sync.dma_start(out=z0[:HALF, 2 * u + 1, :], in_=z0[HALF:, 2 * u, :])
+            else:
+                gather_right(c, u, 0, P, left, z0_late[:, u, :])
+                nc.sync.dma_start(out=z0[HALF:, 2 * u, :], in_=z0_late[:HALF, u, :])
+                nc.sync.dma_start(out=z0[HALF:, 2 * u + 1, :], in_=z0_late[HALF:, u, :])
+
+        cast_w1(1, 0, "vector", "raw02")
         cast_w1(1, 1, "vector")
-        gather_left(0, 0, 0, P, lefts[0], lane0[:, 0, :])
-        quant_w1(1, 1)
+        quant_w1(1, 0, place="raw11")
         cast_w1(1, 2, "vector")
-        quant_w1(1, 2, 0, 128)
-        gather_left(0, 1, 0, P, lefts[1], lane0[:, 1, :])
-        quant_w1(1, 2, 128, 256)
-        quant_w1(1, 2, 256, 512)
-        for t in range(PACK - 1):
-            respond(1, t, new_sq())
-        respond(1, PACK - 1, ring.tile([PART, S], F32, name="sq_last", tag="z0", bufs=1, align_bytes=64))
-        for t in range(PACK):
-            if t + 2 < PACK:
-                gather_left(0, t + 2, 0, P, lefts[t + 2], lane0[:, t + 2, :])
-            gather_right(0, t, 0, P, lefts[t], lane0[:, t + 1, :])
-        nc.scalar.activation(out=warm[:], in_=h[1, PACK - 1][:, S - 1 : S], func=ACT.Sqrt)
-        z0_bf = ring.tile([PART, P * PACK], BF16, name="z0_bf", tag="z0", bufs=1, align_bytes=64)
-        cast_z(z0_bf[:], lane0[:, 1:, :], "scalar")
+        quant_w1(1, 1)
+        quant_w1(1, 2)
+        respond(1, 0, new_sq())
+        stage0 = keep.tile([PART, S], F32, name="stage0", tag="table2", align_bytes=64)
+        respond(1, 1, stage0)
+        left0 = keep.tile([PART, P], F32, name="left0")
+        z0 = keep.tile([PART, PACK, P], F32, name="z0", tag="table0", align_bytes=64)
+        cast_w1(2, 0, "vector")
+        match_left(0, left0, 0, GAIN_W)
+        quant_w1(2, 0)
+        match_left(0, left0, GAIN_W, P)
+        cast_w1(2, 1, "vector")
+        match_right(0, left0[:])
+        quant_w1(2, 1)
+        cast_w1(2, 2, "scalar", None, 0, 2)
+        cast_w1(2, 2, "scalar", None, 2, PACK)
+        quant_w1(2, 2, 0, 128)
+        quant_w1(2, 2, 128, 256)
+        lefts = [left0[:], w1_stage[2, 2][:, :P], w1_stage[2, 1][:, :P], w1_raw[2, 2][:, 0, :]]
+        match_left(2, lefts[2])
+        match_left(1, lefts[1])
+        quant_w1(2, 2, 256, 512)
+        match_right(1, lefts[1])
+        late = keep.tile([PART, S], F32, name="late", tag="table1", align_bytes=64)
+        respond(2, 0, late)
+        for t in range(1, PACK):
+            respond(2, t, rows[:, t - 1, :])
+        match_left(3, lefts[3])
+        match_right(2, lefts[2])
+        match_right(3, lefts[3])
+        cast_z(late[:, BANK:].bitcast(BF16), z0[:, :, :GAIN_W], "scalar")
+        nc.scalar.activation(out=warm[:], in_=h[2, PACK - 1][:, S - 1 : S], func=ACT.Sqrt, scale=late[:, 0:1], bias=stage0[:, 0:1])
 
-        steps = len(SPANS) * PACK
-        used = {}
-        z1_bf = {}
+        stage1 = keep.tile([PART, QUARTER * PACK], BF16, name="stage1", align_bytes=64)
+        stage2 = keep.tile([PART, QUARTER * PACK], BF16, name="stage2", align_bytes=64)
+        z0_bf = [late[:, BANK:].bitcast(BF16), late[:, :BANK].bitcast(BF16)]
+        z1 = [rows[:, :, S - GAIN_W :], late[:, BANK:].rearrange("p (t i) -> p t i", t=PACK), z_last[:]]
+        z1_bf = [stage0[:, :BANK].bitcast(BF16), stage1[:], stage2[:]]
+        places = [place[:, :GAIN_W] for place in lefts]
+        places += [lefts[1][:, :QUARTER], lefts[1][:, QUARTER : 2 * QUARTER], lefts[0][:, :QUARTER]]
+        places += [lefts[0][:, QUARTER : 2 * QUARTER], places[4], stage0[:, :QUARTER]]
+        places += [late[:, j * QUARTER : (j + 1) * QUARTER] for j in range(2)]
 
         def left_step(k):
             c, t = divmod(k, PACK)
             i0, i1 = SPANS[c]
-            used[k] = lefts[t][:, : i1 - i0]
-            gather_left(1, t, i0, i1, used[k], lane1[c][:, t, :])
+            gather_left(2, t, i0, i1, places[k], gains[PACK + t][:, : i1 - i0])
 
         def right_step(k, c0=0, c1=None):
             c, t = divmod(k, PACK)
             i0, i1 = SPANS[c]
             if c1 is None:
                 c1 = i1 - i0
-            gather_right(1, t, i0 + c0, i0 + c1, used[k][:, c0:c1], lane1[c][:, t + 1, c0:c1])
-
-        def advance(k0, k1):
-            for k in range(k0, k1):
-                if k < steps:
-                    left_step(k)
-                right_step(k - 2)
-
-        def cast_chunk(c):
-            i0, i1 = SPANS[c]
-            z1_bf[c] = ring.tile([PART, (i1 - i0) * PACK], BF16, name="z1_bf", tag="c%d" % c, bufs=1, align_bytes=64)
-            cast_z(z1_bf[c][:], lane1[c][:, 1:, :], "scalar")
-
-        def quant_chunk(c):
-            quant_z(1, SPANS[c][0], SPANS[c][1], z1_bf[c][:])
-
-        def move_lefts(tag):
-            place = ring.tile([PART, 2, QUARTER], F32, name="left", tag=tag, bufs=1, align_bytes=64)
-            lefts[0] = place[:, 0, :]
-            lefts[1] = place[:, 1, :]
+            gather_right(2, t, i0 + c0, i0 + c1, places[k][:, c0:c1], z1[c][:, t, c0:c1])
 
         def finish(q):
             mag = ring.tile([PART, N // PART, QUARTER], F32, name="mag", bufs=2)
             magnitude(q, 0, 4, mag)
-            return mag
+            root_and_store(q, 0, 4, mag)
 
         left_step(0)
-        left_step(1)
-        advance(2, 4)
-        right_step(2)
+        for k in range(1, PACK):
+            left_step(k)
+            right_step(k - 1)
         right_step(3)
-        quant_z(0, 0, P, z0_bf[:])
-        cast_chunk(0)
-        move_lefts("z0")
+        cast_z(z1_bf[0], z1[0], "scalar")
+        cast_z(z0_bf[1], z0[:, :, GAIN_W:], "scalar")
         left_step(4)
         left_step(5)
-        advance(6, 8)
-        quant_chunk(0)
-        for q in (0, 1):
-            open_y(q, 0, 4)
-            close_y(q, 0, 4)
+        quant_z(0, 0, GAIN_W, z0_bf[0])
+        open_y(0, 0, 4)
+        open_y(1, 0, 4)
+        left_step(6)
+        left_step(7)
+        right_step(4)
+        right_step(5)
+        right_step(6)
+        right_step(7)
+        left_step(8)
+        cast_z(z1_bf[1], z1[1], "vector")
+        quant_z(1, 0, GAIN_W, z1_bf[0])
+        close_y(0, 0, 4)
+        close_y(1, 0, 4)
+        finish(0)
+        finish(1)
+        right_step(8)
+        quant_z(1, SPANS[1][0], SPANS[1][1], z1_bf[1])
+        left_step(9)
+        quant_z(0, GAIN_W, P, z0_bf[1])
         open_y(2, 0, 4)
+        close_y(2, 0, 4)
+        finish(2)
         open_y(3, 0, 2)
         open_y(3, 2, 4)
-        move_lefts("c0")
-        advance(8, 10)
-        cast_chunk(1)
-        mags = [finish(0), finish(1)]
-        root_and_store(0, 0, 4, mags[0])
-        root_and_store(1, 0, 4, mags[1])
-        advance(10, 13)
-        quant_chunk(1)
-        close_y(2, 0, 4)
-        root_and_store(2, 0, 4, finish(2))
+        right_step(9)
+        left_step(10)
+        left_step(11)
+        right_step(10)
         last = CHUNKS - 1
         half = QUARTER // 2
-        z_last = ring.tile([PART, QUARTER * PACK], BF16, name="z1_last", bufs=1, align_bytes=64)
         for c0 in (0, half):
-            right_step(steps - 1, c0, c0 + half)
+            right_step(11, c0, c0 + half)
         for c0 in (0, half):
-            cast_z(z_last[:, PACK * c0 : PACK * (c0 + half)], lane1[-1][:, 1:, c0 : c0 + half], "vector")
+            cast_z(z1_bf[2][:, PACK * c0 : PACK * (c0 + half)], z1[2][:, :, c0 : c0 + half], "vector")
         for c0 in (0, half):
-            quant_z(1, last * QUARTER + c0, last * QUARTER + c0 + half, z_last[:, PACK * c0 : PACK * (c0 + half)])
+            quant_z(1, last * QUARTER + c0, last * QUARTER + c0 + half, z1_bf[2][:, PACK * c0 : PACK * (c0 + half)])
         close_y(last, 0, 2)
         close_y(last, 2, 4)
         mag_last = ring.tile([PART, N // PART, QUARTER], F32, name="mag_last", bufs=1)
         magnitude(last, 0, 2, mag_last)
-        magnitude(last, 2, 4, mag_last)
+        neg = ring.tile([PART, 2, QUARTER], F32, name="neg", bufs=1)
+        mag_v = ring.tile([PART, N // PART, QUARTER], F32, name="mag_v", bufs=1)
+        nc.vector.tensor_scalar(out=neg[:], in0=y_acc[last, 2][:, :2, :], scalar1=-1.0, scalar2=None, op0=MULT)
+        nc.vector.tensor_tensor(mag_v[:, 2:, :], y_acc[last, 2][:, :2, :], neg[:], mybir.AluOpType.max)
         root_and_store(last, 0, 2, mag_last)
-        root_and_store(last, 2, 4, mag_last)
+        root_and_store(last, 2, 4, mag_v)

@@ -37,7 +37,7 @@ def tile_list_stereo_disparity_cost_kernel(tc, tab_words, tab_scales, offs, pos1
         keep = ctx.enter_context(tc.tile_pool(name="keep", bufs=1))
         ring = ctx.enter_context(tc.tile_pool(name="ring", bufs=3))
         resp = ctx.enter_context(tc.tile_pool(name="resp", bufs=8))
-        psum = ctx.enter_context(tc.psum_pool(name="psum", bufs=8))
+        psum = ctx.enter_context(tc.psum_pool(name="psum", bufs=4))
 
         offs_sb = keep.tile([PART, S // STRIPE], U16, name="offs_sb")
         pos1_sb = keep.tile([PART, P // STRIPE], U16, name="pos1_sb")
@@ -47,7 +47,6 @@ def tile_list_stereo_disparity_cost_kernel(tc, tab_words, tab_scales, offs, pos1
         gain_wide = keep.tile([PART, R_PASSES * PACK - 1, GAIN_W], F32, name="gain_wide")
         z0_late = keep.tile([PART, 2, P], F32, name="z0_late")
         rows = keep.tile([PART, PACK, S], F32, name="rows", align_bytes=64)
-        z_last = keep.tile([PART, PACK, QUARTER], F32, name="z_last")
         table = [keep.tile([PART, T], I32, name="table", tag="table%d" % a, align_bytes=64) for a in range(K_PASSES)]
         table_sc = keep.tile([PART, T // 4], I32, name="table_sc", align_bytes=64)
         v_words = [keep.tile([PART, S], U32, name="v_words%d" % a, align_bytes=64) for a in range(K_PASSES)]
@@ -77,15 +76,15 @@ def tile_list_stereo_disparity_cost_kernel(tc, tab_words, tab_scales, offs, pos1
         def load_scales(queue, q):
             queue.dma_start(out=table_sc[32 * q : 32 * q + 12, :], in_=tab_scales[:, 4 * q : 4 * q + 4, :].bitcast(I32))
 
-        nc.gpsimd.memset(table_sc[:], 0)
+        nc.vector.memset(table_sc[:], 0)
         nc.vector.memset(w2_sc[:], 0)
         nc.sync.dma_start(offs_sb[:], offs)
         for e in range(2):
             nc.scalar.dma_start(out=gain_raw[HALF * e : HALF * (e + 1)], in_=gain.rearrange("(k m t) -> m k t", k=PACK, t=PACK))
         load_table(0)
+        load_w1(0, 0)
         for q in range(4):
             load_scales(nc.sync if q < 2 else nc.scalar, q)
-        load_w1(0, 0)
         load_table(1)
         load_w1(0, 1)
         load_table(2)
@@ -107,14 +106,15 @@ def tile_list_stereo_disparity_cost_kernel(tc, tab_words, tab_scales, offs, pos1
             else:
                 nc.vector.tensor_copy(out=dst, in_=src)
 
-        def cast_w1(b, a, engine, place=None, t0=0, t1=PACK):
+        def cast_w1(b, a, engine, place=None):
             width = GROUPS[b][1] - GROUPS[b][0]
             if (b, a) not in w1_bf:
                 w1_stage[b, a] = keep.tile([PART, width * PACK // 2], F32, name="w1_bf", tag=place or "bf%d%d" % (b, a), align_bytes=64)
                 w1_bf[b, a] = w1_stage[b, a][:].bitcast(BF16)
-            dst = w1_bf[b, a].rearrange("p (t m j) -> p m j t", t=PACK, j=PACK)[:, :, :, t0:t1]
-            src = w1_raw[b, a][:].rearrange("p j (m t) -> p m j t", t=PACK)[:, :, :, t0:t1]
-            copy_on(engine, dst, src)
+            dst = w1_bf[b, a].rearrange("p (t m j) -> p m j t", t=PACK, j=PACK)
+            src = w1_raw[b, a][:].rearrange("p j (m t) -> p m j t", t=PACK)
+            for t in range(0, PACK, 2):
+                copy_on(engine, dst[:, :, :, t : t + 2], src[:, :, :, t : t + 2])
 
         def quant_w1(b, a, c0=0, c1=None, place=None):
             width = GROUPS[b][1] - GROUPS[b][0]
@@ -184,7 +184,7 @@ def tile_list_stereo_disparity_cost_kernel(tc, tab_words, tab_scales, offs, pos1
         y_acc = {}
 
         def open_y(q, n0, n1):
-            y_acc[q, n0] = psum.tile([PART, N // PART, QUARTER], F32, name="bank")
+            y_acc[q, n0] = psum.tile([PART, N // PART, QUARTER], F32, name="y_acc", tag="bank" if n0 else "y_bank")
             for nt in range(n0, n1):
                 y_pass(y_acc[q, n0][:, nt - n0, :], nt, 0, q, nt == n0, False)
 
@@ -241,9 +241,12 @@ def tile_list_stereo_disparity_cost_kernel(tc, tab_words, tab_scales, offs, pos1
                 gather_right(c, u, 0, P, left, z0[:, 2 * u, :])
                 nc.sync.dma_start(out=z0[:HALF, 2 * u + 1, :], in_=z0[HALF:, 2 * u, :])
             else:
-                gather_right(c, u, 0, P, left, z0_late[:, u, :])
-                nc.sync.dma_start(out=z0[HALF:, 2 * u, :], in_=z0_late[:HALF, u, :])
-                nc.sync.dma_start(out=z0[HALF:, 2 * u + 1, :], in_=z0_late[HALF:, u, :])
+                step = P if u == 0 else GAIN_W
+                for i0 in range(0, P, step):
+                    cols = slice(i0, i0 + step)
+                    gather_right(c, u, i0, i0 + step, left[:, cols], z0_late[:, u, cols])
+                    nc.sync.dma_start(out=z0[HALF:, 2 * u, cols], in_=z0_late[:HALF, u, cols])
+                    nc.sync.dma_start(out=z0[HALF:, 2 * u + 1, cols], in_=z0_late[HALF:, u, cols])
 
         cast_w1(1, 0, "vector", "raw02")
         cast_w1(1, 1, "vector")
@@ -263,8 +266,7 @@ def tile_list_stereo_disparity_cost_kernel(tc, tab_words, tab_scales, offs, pos1
         cast_w1(2, 1, "vector")
         match_right(0, left0[:])
         quant_w1(2, 1)
-        cast_w1(2, 2, "scalar", None, 0, 2)
-        cast_w1(2, 2, "scalar", None, 2, PACK)
+        cast_w1(2, 2, "scalar")
         quant_w1(2, 2, 0, 128)
         quant_w1(2, 2, 128, 256)
         lefts = [left0[:], w1_stage[2, 2][:, :P], w1_stage[2, 1][:, :P], w1_raw[2, 2][:, 0, :]]
@@ -280,16 +282,15 @@ def tile_list_stereo_disparity_cost_kernel(tc, tab_words, tab_scales, offs, pos1
         match_right(2, lefts[2])
         match_right(3, lefts[3])
         cast_z(late[:, BANK:].bitcast(BF16), z0[:, :, :GAIN_W], "scalar")
-        nc.scalar.activation(out=warm[:], in_=h[2, PACK - 1][:, S - 1 : S], func=ACT.Sqrt, scale=late[:, 0:1], bias=stage0[:, 0:1])
+        nc.scalar.activation(out=warm[:], in_=h[2, PACK - 1][:, S - 1 : S], func=ACT.Sqrt, scale=late[:, 0:1])
 
-        stage1 = keep.tile([PART, QUARTER * PACK], BF16, name="stage1", align_bytes=64)
         stage2 = keep.tile([PART, QUARTER * PACK], BF16, name="stage2", align_bytes=64)
         z0_bf = [late[:, BANK:].bitcast(BF16), late[:, :BANK].bitcast(BF16)]
-        z1 = [rows[:, :, S - GAIN_W :], late[:, BANK:].rearrange("p (t i) -> p t i", t=PACK), z_last[:]]
-        z1_bf = [stage0[:, :BANK].bitcast(BF16), stage1[:], stage2[:]]
+        z1 = [rows[:, :, S - GAIN_W :], late[:, BANK:].rearrange("p (t i) -> p t i", t=PACK), stage0[:, GAIN_W : GAIN_W + BANK].rearrange("p (t i) -> p t i", t=PACK)]
+        z1_bf = [stage0[:, :BANK].bitcast(BF16), stage0[:, :GAIN_W].bitcast(BF16), stage2[:]]
         places = [place[:, :GAIN_W] for place in lefts]
         places += [lefts[1][:, :QUARTER], lefts[1][:, QUARTER : 2 * QUARTER], lefts[0][:, :QUARTER]]
-        places += [lefts[0][:, QUARTER : 2 * QUARTER], places[4], stage0[:, :QUARTER]]
+        places += [lefts[0][:, QUARTER : 2 * QUARTER], places[4], places[5]]
         places += [late[:, j * QUARTER : (j + 1) * QUARTER] for j in range(2)]
 
         def left_step(k):
@@ -308,6 +309,7 @@ def tile_list_stereo_disparity_cost_kernel(tc, tab_words, tab_scales, offs, pos1
             mag = ring.tile([PART, N // PART, QUARTER], F32, name="mag", bufs=2)
             magnitude(q, 0, 4, mag)
             root_and_store(q, 0, 4, mag)
+            return mag
 
         left_step(0)
         for k in range(1, PACK):
@@ -328,22 +330,22 @@ def tile_list_stereo_disparity_cost_kernel(tc, tab_words, tab_scales, offs, pos1
         right_step(6)
         right_step(7)
         left_step(8)
-        cast_z(z1_bf[1], z1[1], "vector")
+        left_step(9)
         quant_z(1, 0, GAIN_W, z1_bf[0])
         close_y(0, 0, 4)
         close_y(1, 0, 4)
         finish(0)
         finish(1)
+        cast_z(z1_bf[1], z1[1], "vector")
         right_step(8)
+        right_step(9)
         quant_z(1, SPANS[1][0], SPANS[1][1], z1_bf[1])
-        left_step(9)
         quant_z(0, GAIN_W, P, z0_bf[1])
         open_y(2, 0, 4)
         close_y(2, 0, 4)
-        finish(2)
+        mag_last = finish(2)
         open_y(3, 0, 2)
         open_y(3, 2, 4)
-        right_step(9)
         left_step(10)
         left_step(11)
         right_step(10)
@@ -357,11 +359,7 @@ def tile_list_stereo_disparity_cost_kernel(tc, tab_words, tab_scales, offs, pos1
             quant_z(1, last * QUARTER + c0, last * QUARTER + c0 + half, z1_bf[2][:, PACK * c0 : PACK * (c0 + half)])
         close_y(last, 0, 2)
         close_y(last, 2, 4)
-        mag_last = ring.tile([PART, N // PART, QUARTER], F32, name="mag_last", bufs=1)
         magnitude(last, 0, 2, mag_last)
-        neg = ring.tile([PART, 2, QUARTER], F32, name="neg", bufs=1)
-        mag_v = ring.tile([PART, N // PART, QUARTER], F32, name="mag_v", bufs=1)
-        nc.vector.tensor_scalar(out=neg[:], in0=y_acc[last, 2][:, :2, :], scalar1=-1.0, scalar2=None, op0=MULT)
-        nc.vector.tensor_tensor(mag_v[:, 2:, :], y_acc[last, 2][:, :2, :], neg[:], mybir.AluOpType.max)
+        magnitude(last, 2, 4, mag_last)
         root_and_store(last, 0, 2, mag_last)
-        root_and_store(last, 2, 4, mag_v)
+        root_and_store(last, 2, 4, mag_last)

@@ -73,8 +73,6 @@ def tile_list_stereo_disparity_cost_kernel(tc, tab_words, tab_scales, offs, pos1
         def load_table(a):
             nc.sync.dma_start(out=table[a][:], in_=tab_words[a].rearrange("p t i -> p (t i)").bitcast(I32))
 
-        def load_scales(queue, q):
-            queue.dma_start(out=table_sc[32 * q : 32 * q + 12, :], in_=tab_scales[:, 4 * q : 4 * q + 4, :].bitcast(I32))
 
         nc.vector.memset(table_sc[:], 0)
         nc.vector.memset(w2_sc[:], 0)
@@ -82,10 +80,12 @@ def tile_list_stereo_disparity_cost_kernel(tc, tab_words, tab_scales, offs, pos1
         for e in range(2):
             nc.scalar.dma_start(out=gain_raw[HALF * e : HALF * (e + 1)], in_=gain.rearrange("(k m t) -> m k t", k=PACK, t=PACK))
         load_table(0)
-        load_w1(0, 0)
-        for q in range(4):
-            load_scales(nc.sync if q < 2 else nc.scalar, q)
+        for a in range(K_PASSES):
+            for r in range(4):
+                queue = nc.gpsimd if a == K_PASSES - 1 else nc.scalar
+                queue.dma_start(out=table_sc[4 * a + r : PART : 32, :], in_=tab_scales[a, r:16:4, :].bitcast(I32))
         load_table(1)
+        load_w1(0, 0)
         load_w1(0, 1)
         load_table(2)
         load_w1(0, 2)
@@ -202,17 +202,17 @@ def tile_list_stereo_disparity_cost_kernel(tc, tab_words, tab_scales, offs, pos1
 
         for e in range(2):
             half = slice(HALF * e, HALF * (e + 1))
-            nc.scalar.copy(out=gain_sb[half, :PACK].rearrange("p (c u) -> p c u", u=2), in_=gain_raw[half, 0:2, e:PACK:2])
-            nc.scalar.copy(out=gain_sb[half, PACK:], in_=gain_raw[half, 2 + e, :])
+            nc.vector.tensor_copy(out=gain_sb[half, :PACK].rearrange("p (c u) -> p c u", u=2), in_=gain_raw[half, 0:2, e:PACK:2])
+            nc.vector.tensor_copy(out=gain_sb[half, PACK:], in_=gain_raw[half, 2 + e, :])
         gains = [gain_wide[:, 0, :], z0_late[:, 0, :GAIN_W]] + [gain_wide[:, k, :] for k in range(1, R_PASSES * PACK - 1)]
         for k in range(2):
-            nc.scalar.copy(out=gains[k], in_=gain_sb[:, k : k + 1].to_broadcast([PART, GAIN_W]))
-        nc.scalar.copy(out=gain_wide[:, 1:, :], in_=gain_sb[:, 2:].unsqueeze(2).to_broadcast([PART, R_PASSES * PACK - 2, GAIN_W]))
+            nc.vector.tensor_copy(out=gains[k], in_=gain_sb[:, k : k + 1].to_broadcast([PART, GAIN_W]))
+        nc.vector.tensor_copy(out=gain_wide[:, 1:, :], in_=gain_sb[:, 2:].unsqueeze(2).to_broadcast([PART, R_PASSES * PACK - 2, GAIN_W]))
         gather_words(0, 0, S)
+        gather_words(1, 0, S)
         nc.vector.tensor_copy(v_sc[:], table_sc[:].bitcast(U8).indirect(offs_sb[:]))
         cast_w1(0, 0, "scalar")
         quant_w1(0, 0)
-        gather_words(1, 0, S)
         cast_w1(0, 1, "scalar")
         quant_w1(0, 1)
         opened = [[psum.tile([PART, BANK], F32, name="bank") for j0 in range(0, S, BANK)] for u in range(2)]
@@ -238,15 +238,20 @@ def tile_list_stereo_disparity_cost_kernel(tc, tab_words, tab_scales, offs, pos1
         def match_right(k, left):
             c, u = divmod(k, 2)
             if c == 0:
-                gather_right(c, u, 0, P, left, z0[:, 2 * u, :])
-                nc.sync.dma_start(out=z0[:HALF, 2 * u + 1, :], in_=z0[HALF:, 2 * u, :])
+                for g in range(2):
+                    gather_right(c, u, g * GAIN_W, (g + 1) * GAIN_W, left[:, g * GAIN_W : (g + 1) * GAIN_W], z0[:, g, 2 * u, :])
+                nc.sync.dma_start(out=z0[:HALF, :, 2 * u + 1, :], in_=z0[HALF:, :, 2 * u, :])
+            elif u == 0:
+                gather_right(c, u, 0, P, left, z0_late[:, u, :])
+                by_half = z0_late[:, u, :].rearrange("p (g i) -> p g i", g=2)
+                nc.sync.dma_start(out=z0[HALF:, :, 0, :], in_=by_half[:HALF])
+                nc.sync.dma_start(out=z0[HALF:, :, 1, :], in_=by_half[HALF:])
             else:
-                step = P if u == 0 else GAIN_W
-                for i0 in range(0, P, step):
-                    cols = slice(i0, i0 + step)
-                    gather_right(c, u, i0, i0 + step, left[:, cols], z0_late[:, u, cols])
-                    nc.sync.dma_start(out=z0[HALF:, 2 * u, cols], in_=z0_late[:HALF, u, cols])
-                    nc.sync.dma_start(out=z0[HALF:, 2 * u + 1, cols], in_=z0_late[HALF:, u, cols])
+                for g in range(2):
+                    cols = slice(g * GAIN_W, (g + 1) * GAIN_W)
+                    gather_right(c, u, g * GAIN_W, (g + 1) * GAIN_W, left[:, cols], z0_late[:, u, cols])
+                    nc.sync.dma_start(out=z0[HALF:, g, 2, :], in_=z0_late[:HALF, u, cols])
+                    nc.sync.dma_start(out=z0[HALF:, g, 3, :], in_=z0_late[HALF:, u, cols])
 
         cast_w1(1, 0, "vector", "raw02")
         cast_w1(1, 1, "vector")
@@ -258,7 +263,7 @@ def tile_list_stereo_disparity_cost_kernel(tc, tab_words, tab_scales, offs, pos1
         stage0 = keep.tile([PART, S], F32, name="stage0", tag="table2", align_bytes=64)
         respond(1, 1, stage0)
         left0 = keep.tile([PART, P], F32, name="left0")
-        z0 = keep.tile([PART, PACK, P], F32, name="z0", tag="table0", align_bytes=64)
+        z0 = keep.tile([PART, 2, PACK, GAIN_W], F32, name="z0", tag="table0", align_bytes=64)
         cast_w1(2, 0, "vector")
         match_left(0, left0, 0, GAIN_W)
         quant_w1(2, 0)
@@ -281,17 +286,17 @@ def tile_list_stereo_disparity_cost_kernel(tc, tab_words, tab_scales, offs, pos1
         match_left(3, lefts[3])
         match_right(2, lefts[2])
         match_right(3, lefts[3])
-        cast_z(late[:, BANK:].bitcast(BF16), z0[:, :, :GAIN_W], "scalar")
+        cast_z(late[:, BANK:].bitcast(BF16), z0[:, 0], "scalar")
         nc.scalar.activation(out=warm[:], in_=h[2, PACK - 1][:, S - 1 : S], func=ACT.Sqrt, scale=late[:, 0:1])
 
         stage2 = keep.tile([PART, QUARTER * PACK], BF16, name="stage2", align_bytes=64)
         z0_bf = [late[:, BANK:].bitcast(BF16), late[:, :BANK].bitcast(BF16)]
-        z1 = [rows[:, :, S - GAIN_W :], late[:, BANK:].rearrange("p (t i) -> p t i", t=PACK), stage0[:, GAIN_W : GAIN_W + BANK].rearrange("p (t i) -> p t i", t=PACK)]
-        z1_bf = [stage0[:, :BANK].bitcast(BF16), stage0[:, :GAIN_W].bitcast(BF16), stage2[:]]
+        z1 = [rows[:, :, S - GAIN_W :], z0[:, 0, :, :QUARTER], rows[:, :, S - QUARTER :]]
+        z1_bf = [stage0[:, :BANK].bitcast(BF16), rows[:, 0, S - 3 * QUARTER : S - QUARTER].bitcast(BF16), stage2[:]]
         places = [place[:, :GAIN_W] for place in lefts]
         places += [lefts[1][:, :QUARTER], lefts[1][:, QUARTER : 2 * QUARTER], lefts[0][:, :QUARTER]]
-        places += [lefts[0][:, QUARTER : 2 * QUARTER], places[4], places[5]]
-        places += [late[:, j * QUARTER : (j + 1) * QUARTER] for j in range(2)]
+        places += [z0[:, 0, 0, QUARTER:], rows[:, 1, S - GAIN_W : S - QUARTER], rows[:, 2, S - GAIN_W : S - QUARTER]]
+        places += [z0[:, 1, j, :QUARTER] for j in range(2)]
 
         def left_step(k):
             c, t = divmod(k, PACK)
@@ -317,7 +322,7 @@ def tile_list_stereo_disparity_cost_kernel(tc, tab_words, tab_scales, offs, pos1
             right_step(k - 1)
         right_step(3)
         cast_z(z1_bf[0], z1[0], "scalar")
-        cast_z(z0_bf[1], z0[:, :, GAIN_W:], "scalar")
+        cast_z(z0_bf[1], z0[:, 1], "scalar")
         left_step(4)
         left_step(5)
         quant_z(0, 0, GAIN_W, z0_bf[0])
@@ -329,18 +334,18 @@ def tile_list_stereo_disparity_cost_kernel(tc, tab_words, tab_scales, offs, pos1
         right_step(5)
         right_step(6)
         right_step(7)
-        left_step(8)
-        left_step(9)
         quant_z(1, 0, GAIN_W, z1_bf[0])
         close_y(0, 0, 4)
         close_y(1, 0, 4)
         finish(0)
         finish(1)
         cast_z(z1_bf[1], z1[1], "vector")
-        right_step(8)
-        right_step(9)
+        left_step(8)
+        left_step(9)
         quant_z(1, SPANS[1][0], SPANS[1][1], z1_bf[1])
         quant_z(0, GAIN_W, P, z0_bf[1])
+        right_step(8)
+        right_step(9)
         open_y(2, 0, 4)
         close_y(2, 0, 4)
         mag_last = finish(2)

@@ -23,47 +23,43 @@ K_PASSES = K // PASS
 R_PASSES = H // PASS
 BANK = 512
 STRIPE = 16
-QUARTER = 128
-GAIN_W = 256
+CHUNK = 128
+WIDE = 256
 HALF = 64
 GROUPS = [(0, 256), (256, 512), (512, 1024)]
-CHUNKS = P // QUARTER
-SPANS = [(0, 256), (256, 384), (384, 512)]
+TILES = H // PART
 
 
 def tile_list_stereo_disparity_cost_kernel(tc, tab_words, tab_scales, offs, pos1, pos2, w1, gain, w2_words, w2_scales, out):
     nc = tc.nc
     with ExitStack() as ctx:
         keep = ctx.enter_context(tc.tile_pool(name="keep", bufs=1))
-        ring = ctx.enter_context(tc.tile_pool(name="ring", bufs=3))
-        resp = ctx.enter_context(tc.tile_pool(name="resp", bufs=8))
+        ring = ctx.enter_context(tc.tile_pool(name="ring", bufs=2))
         psum = ctx.enter_context(tc.psum_pool(name="psum", bufs=4))
 
         offs_sb = keep.tile([PART, S // STRIPE], U16, name="offs_sb")
         pos1_sb = keep.tile([PART, P // STRIPE], U16, name="pos1_sb")
         pos2_sb = keep.tile([PART, P // STRIPE], U16, name="pos2_sb")
         gain_raw = keep.tile([PART, PACK, PACK], F32, name="gain_raw")
-        gain_sb = keep.tile([PART, R_PASSES * PACK], F32, name="gain_sb")
-        gain_wide = keep.tile([PART, R_PASSES * PACK - 1, GAIN_W], F32, name="gain_wide")
-        z0_late = keep.tile([PART, 2, P], F32, name="z0_late")
-        rows = keep.tile([PART, PACK, S], F32, name="rows", align_bytes=64)
+        gain_sb = keep.tile([PART, TILES], F32, name="gain_sb")
+        gain_wide = keep.tile([PART, TILES, WIDE], F32, name="gain_wide")
         table = [keep.tile([PART, T], I32, name="table", tag="table%d" % a, align_bytes=64) for a in range(K_PASSES)]
         table_sc = keep.tile([PART, T // 4], I32, name="table_sc", align_bytes=64)
-        v_words = [keep.tile([PART, S], U32, name="v_words%d" % a, align_bytes=64) for a in range(K_PASSES)]
         v_sc = keep.tile([PART, S], U8, name="v_sc", align_bytes=64)
-        w1_raw = {}
-        w1_bf = {}
-        w1_stage = {}
-        w1_words = {}
-        w1_sc = {}
+        v_words = {}
+        w1_raw, w1_bf, w1_words, w1_sc = {}, {}, {}, {}
         for b, (r0, r1) in enumerate(GROUPS):
             for a in range(K_PASSES):
-                w1_raw[b, a] = keep.tile([PART, PACK, r1 - r0], F32, name="w1_raw", tag="raw%d%d" % (b, a), align_bytes=64)
-                w1_sc[b, a] = keep.tile([PART, r1 - r0], U8, name="w1_sc%d%d" % (b, a), align_bytes=64)
+                width = r1 - r0
+                w1_raw[b, a] = keep.tile([PART, PACK, width], F32, name="w1_raw", tag="raw%d%d" % (b, a), align_bytes=64)
+                w1_bf[b, a] = keep.tile([PART, PACK * width], BF16, name="w1_bf%d%d" % (b, a), align_bytes=64)
+                w1_words[b, a] = keep.tile([PART, width], U32, name="w1_words%d%d" % (b, a), align_bytes=64)
+                w1_sc[b, a] = keep.tile([PART, width], U8, name="w1_sc%d%d" % (b, a), align_bytes=64)
         w2_sb = keep.tile([PART, R_PASSES, N // 2], I32, name="w2_sb", align_bytes=64)
         w2_sc = keep.tile([PART, R_PASSES, N // 4], I32, name="w2_sc", align_bytes=64)
         z_words = [keep.tile([PART, P], U32, name="z_words%d" % b, align_bytes=64) for b in range(R_PASSES)]
         z_sc = [keep.tile([PART, P], U8, name="z_sc%d" % b, align_bytes=64) for b in range(R_PASSES)]
+        h = [keep.tile([PART, S], F32, name="h%d" % k) for k in range(TILES)]
         warm = keep.tile([PART, 1], F32, name="warm")
 
         def load_w1(b, a):
@@ -73,29 +69,28 @@ def tile_list_stereo_disparity_cost_kernel(tc, tab_words, tab_scales, offs, pos1
         def load_table(a):
             nc.sync.dma_start(out=table[a][:], in_=tab_words[a].rearrange("p t i -> p (t i)").bitcast(I32))
 
-
         nc.vector.memset(table_sc[:], 0)
         nc.vector.memset(w2_sc[:], 0)
         nc.sync.dma_start(offs_sb[:], offs)
-        for e in range(2):
-            nc.scalar.dma_start(out=gain_raw[HALF * e : HALF * (e + 1)], in_=gain.rearrange("(k m t) -> m k t", k=PACK, t=PACK))
         load_table(0)
-        for a in range(K_PASSES):
-            for r in range(4):
-                queue = nc.gpsimd if a == K_PASSES - 1 else nc.scalar
-                queue.dma_start(out=table_sc[4 * a + r : PART : 32, :], in_=tab_scales[a, r:16:4, :].bitcast(I32))
+        for r in range(4):
+            nc.gpsimd.dma_start(out=table_sc[8 + r : PART : 32, :], in_=tab_scales[2, r:16:4, :].bitcast(I32))
         load_table(1)
+        for q in range(4):
+            nc.sync.dma_start(out=table_sc[32 * q : 32 * q + 8, :], in_=tab_scales[:2, 4 * q : 4 * q + 4, :].bitcast(I32))
         load_w1(0, 0)
         load_w1(0, 1)
+        for e in range(2):
+            nc.sync.dma_start(out=gain_raw[HALF * e : HALF * (e + 1)], in_=gain.rearrange("(k m t) -> m k t", k=PACK, t=PACK))
         load_table(2)
         load_w1(0, 2)
-        for a in range(K_PASSES):
-            load_w1(1, a)
-        load_w1(2, 0)
+        load_w1(1, 0)
         nc.sync.dma_start(pos1_sb[:], pos1)
-        load_w1(2, 1)
+        load_w1(1, 1)
         nc.sync.dma_start(pos2_sb[:], pos2)
-        load_w1(2, 2)
+        load_w1(1, 2)
+        for a in range(K_PASSES):
+            load_w1(2, a)
         nc.sync.dma_start(out=w2_sb[:], in_=w2_words.rearrange("b p c -> p b c").bitcast(I32))
         for r in range(4):
             nc.sync.dma_start(out=w2_sc[r:PART:32, :, :], in_=w2_scales[:, r:16:4, :].rearrange("b q n -> q b n").bitcast(I32))
@@ -106,61 +101,55 @@ def tile_list_stereo_disparity_cost_kernel(tc, tab_words, tab_scales, offs, pos1
             else:
                 nc.vector.tensor_copy(out=dst, in_=src)
 
-        def cast_w1(b, a, engine, place=None):
-            width = GROUPS[b][1] - GROUPS[b][0]
-            if (b, a) not in w1_bf:
-                w1_stage[b, a] = keep.tile([PART, width * PACK // 2], F32, name="w1_bf", tag=place or "bf%d%d" % (b, a), align_bytes=64)
-                w1_bf[b, a] = w1_stage[b, a][:].bitcast(BF16)
-            dst = w1_bf[b, a].rearrange("p (t m j) -> p m j t", t=PACK, j=PACK)
+        def cast_w1(b, a, half, engine):
+            dst = w1_bf[b, a][:].rearrange("p (t m j) -> p m j t", t=PACK, j=PACK)
             src = w1_raw[b, a][:].rearrange("p j (m t) -> p m j t", t=PACK)
-            for t in range(0, PACK, 2):
-                copy_on(engine, dst[:, :, :, t : t + 2], src[:, :, :, t : t + 2])
+            copy_on(engine, dst[:, :, :, 2 * half : 2 * half + 2], src[:, :, :, 2 * half : 2 * half + 2])
 
-        def quant_w1(b, a, c0=0, c1=None, place=None):
-            width = GROUPS[b][1] - GROUPS[b][0]
-            if c1 is None:
-                c1 = width
-            if (b, a) not in w1_words:
-                w1_words[b, a] = keep.tile([PART, width], U32, name="w1_words", tag=place or "words%d%d" % (b, a), align_bytes=64)
+        def quant_w1(b, a, c0, c1):
             nc.vector.quantize_mx(
                 out=w1_words[b, a][:, c0:c1].bitcast(FP8X4), scales=w1_sc[b, a][:, c0:c1], in_=w1_bf[b, a][:, PACK * c0 : PACK * c1]
             )
 
-        def gather_words(a, j0, j1):
-            nc.vector.tensor_copy(v_words[a][:, j0:j1], table[a][:].bitcast(U32).indirect(offs_sb[:, j0 // STRIPE : j1 // STRIPE]))
+        def gather_words(a, j0, place=None):
+            v_words[a, j0] = keep.tile([PART, BANK], U32, name="v_words", tag=place or "v%d%d" % (a, j0), align_bytes=64)
+            nc.vector.tensor_copy(v_words[a, j0][:], table[a][:].bitcast(U32).indirect(offs_sb[:, j0 // STRIPE : (j0 + BANK) // STRIPE]))
 
-        def x_pass(acc, b, t, a, j0, j1):
+        def x_pass(acc, k, a, j0):
+            b, t = (2, k - 4) if k >= 4 else divmod(k, 2)
             cols = slice(t * PART, (t + 1) * PART)
             nc.tensor.matmul_mx(
                 out=acc,
                 lhsT=w1_words[b, a][:, cols].bitcast(FP8X4),
                 lhsT_scale=w1_sc[b, a][:, cols],
-                rhs=v_words[a][:, j0:j1].bitcast(FP8X4),
-                rhs_scale=v_sc[4 * a : PART, j0:j1],
+                rhs=v_words[a, j0][:].bitcast(FP8X4),
+                rhs_scale=v_sc[4 * a : PART, j0 : j0 + BANK],
                 start=(a == 0),
                 stop=(a == K_PASSES - 1),
             )
 
-        h = {}
-
-        def respond(b, t, sq, opened=None):
-            h[b, t] = resp.tile([PART, S], F32, name="h")
+        def respond(k, sq=None, opened=None):
+            if sq is None:
+                sq = ring.tile([PART, S], F32, name="sq")
             for j0 in range(0, S, BANK):
                 acc = psum.tile([PART, BANK], F32, name="bank") if opened is None else opened[j0 // BANK]
                 for a in range(0 if opened is None else K_PASSES - 1, K_PASSES):
-                    x_pass(acc[:], b, t, a, j0, j0 + BANK)
+                    x_pass(acc[:], k, a, j0)
                 nc.scalar.activation(out=sq[:, j0 : j0 + BANK], in_=acc[:], func=ACT.Square)
             for j0 in range(0, S, BANK):
-                nc.scalar.activation(out=h[b, t][:, j0 : j0 + BANK], in_=sq[:, j0 : j0 + BANK], func=ACT.Exp, scale=-1.0)
+                nc.scalar.activation(out=h[k][:, j0 : j0 + BANK], in_=sq[:, j0 : j0 + BANK], func=ACT.Exp, scale=-1.0)
 
-        def new_sq():
-            return ring.tile([PART, S], F32, name="sq", bufs=2)
+        def gather_left(k, i0, i1, left, gains):
+            nc.vector.tensor_tensor(left, h[k][:].indirect(pos1_sb[:, i0 // STRIPE : i1 // STRIPE]), gains, MULT)
 
-        def gather_left(b, t, i0, i1, left, gains):
-            nc.vector.tensor_tensor(left, h[b, t][:].indirect(pos1_sb[:, i0 // STRIPE : i1 // STRIPE]), gains, MULT)
+        def gather_right(k, i0, i1, left, z):
+            nc.vector.tensor_tensor(z, h[k][:].indirect(pos2_sb[:, i0 // STRIPE : i1 // STRIPE]), left, MULT)
 
-        def gather_right(b, t, i0, i1, left, z):
-            nc.vector.tensor_tensor(z, h[b, t][:].indirect(pos2_sb[:, i0 // STRIPE : i1 // STRIPE]), left, MULT)
+        def match(k, left, z):
+            for i0 in range(0, P, WIDE):
+                gather_left(k, i0, i0 + WIDE, left[:, i0 : i0 + WIDE], gain_wide[:, k, :])
+            for i0 in range(0, P, WIDE):
+                gather_right(k, i0, i0 + WIDE, left[:, i0 : i0 + WIDE], z[:, i0 : i0 + WIDE])
 
         def cast_z(dst, src, engine):
             copy_on(engine, dst.rearrange("p (c i t) -> p c t i", i=4, t=PACK), src.rearrange("p t (c i) -> p c t i", i=4))
@@ -169,7 +158,7 @@ def tile_list_stereo_disparity_cost_kernel(tc, tab_words, tab_scales, offs, pos1
             nc.vector.quantize_mx(out=z_words[b][:, i0:i1].bitcast(FP8X4), scales=z_sc[b][:, i0:i1], in_=src)
 
         def y_pass(acc, nt, b, q, start, stop):
-            cols = slice(q * QUARTER, (q + 1) * QUARTER)
+            cols = slice(q * CHUNK, (q + 1) * CHUNK)
             nc.tensor.matmul_mx(
                 out=acc,
                 lhsT=w2_sb[:, b, :].bitcast(U8)[:, 2 * PART * nt : 2 * PART * (nt + 1)].bitcast(FP4X4),
@@ -184,7 +173,7 @@ def tile_list_stereo_disparity_cost_kernel(tc, tab_words, tab_scales, offs, pos1
         y_acc = {}
 
         def open_y(q, n0, n1):
-            y_acc[q, n0] = psum.tile([PART, N // PART, QUARTER], F32, name="y_acc", tag="bank" if n0 else "y_bank")
+            y_acc[q, n0] = psum.tile([PART, N // PART, CHUNK], F32, name="y_acc", tag="bank" if n0 else "y_bank", bufs=4 if n0 else 2)
             for nt in range(n0, n1):
                 y_pass(y_acc[q, n0][:, nt - n0, :], nt, 0, q, nt == n0, False)
 
@@ -192,179 +181,150 @@ def tile_list_stereo_disparity_cost_kernel(tc, tab_words, tab_scales, offs, pos1
             for nt in range(n0, n1):
                 y_pass(y_acc[q, n0][:, nt - n0, :], nt, 1, q, False, nt == n1 - 1)
 
-        def magnitude(q, n0, n1, mag):
-            nc.scalar.activation(out=mag[:, n0:n1, :], in_=y_acc[q, n0][:, : n1 - n0, :], func=ACT.Abs)
+        mag = keep.tile([PART, 3, N // PART, CHUNK], F32, name="mag", tag="table2", align_bytes=64)
 
-        def root_and_store(q, n0, n1, mag):
-            cost = ring.tile([PART, N // PART, QUARTER], F32, name="cost", bufs=5)
-            nc.scalar.activation(out=cost[:, n0:n1, :], in_=mag[:, n0:n1, :], func=ACT.Sqrt)
-            nc.sync.dma_start(out=out_rows[:, n0:n1, q * QUARTER : (q + 1) * QUARTER], in_=cost[:, n0:n1, :])
+        def magnitude(q, n0, n1):
+            nc.scalar.activation(out=mag[:, min(q, 2), n0:n1, :], in_=y_acc[q, n0][:, : n1 - n0, :], func=ACT.Abs)
 
+        def root_and_store(q, n0, n1):
+            cost = ring.tile([PART, n1 - n0, CHUNK], F32, name="cost", bufs=5)
+            nc.scalar.activation(out=cost[:], in_=mag[:, min(q, 2), n0:n1, :], func=ACT.Sqrt)
+            nc.sync.dma_start(out=out_rows[:, n0:n1, q * CHUNK : (q + 1) * CHUNK], in_=cost[:])
+
+        gather_words(0, 0)
+        gather_words(0, BANK)
+        gather_words(1, 0)
+        gather_words(1, BANK)
+        nc.vector.tensor_copy(v_sc[:], table_sc[:].bitcast(U8).indirect(offs_sb[:]))
+        for half in range(2):
+            cast_w1(0, 0, half, "scalar")
+        quant_w1(0, 0, 0, 2 * PART)
+        for half in range(2):
+            cast_w1(0, 1, half, "scalar")
+        quant_w1(0, 1, 0, 2 * PART)
         for e in range(2):
             half = slice(HALF * e, HALF * (e + 1))
-            nc.vector.tensor_copy(out=gain_sb[half, :PACK].rearrange("p (c u) -> p c u", u=2), in_=gain_raw[half, 0:2, e:PACK:2])
-            nc.vector.tensor_copy(out=gain_sb[half, PACK:], in_=gain_raw[half, 2 + e, :])
-        gains = [gain_wide[:, 0, :], z0_late[:, 0, :GAIN_W]] + [gain_wide[:, k, :] for k in range(1, R_PASSES * PACK - 1)]
-        for k in range(2):
-            nc.vector.tensor_copy(out=gains[k], in_=gain_sb[:, k : k + 1].to_broadcast([PART, GAIN_W]))
-        nc.vector.tensor_copy(out=gain_wide[:, 1:, :], in_=gain_sb[:, 2:].unsqueeze(2).to_broadcast([PART, R_PASSES * PACK - 2, GAIN_W]))
-        gather_words(0, 0, S)
-        gather_words(1, 0, S)
-        nc.vector.tensor_copy(v_sc[:], table_sc[:].bitcast(U8).indirect(offs_sb[:]))
-        cast_w1(0, 0, "scalar")
-        quant_w1(0, 0)
-        cast_w1(0, 1, "scalar")
-        quant_w1(0, 1)
-        opened = [[psum.tile([PART, BANK], F32, name="bank") for j0 in range(0, S, BANK)] for u in range(2)]
+            nc.scalar.copy(out=gain_sb[half, :PACK].rearrange("p (c u) -> p c u", u=2), in_=gain_raw[half, 0:2, e:PACK:2])
+            nc.scalar.copy(out=gain_sb[half, PACK:], in_=gain_raw[half, 2 + e, :])
+        gain_last = keep.tile([PART, WIDE], F32, name="gain_last")
+        nc.scalar.copy(out=gain_wide[:, : TILES - 1, :], in_=gain_sb[:, : TILES - 1].unsqueeze(2).to_broadcast([PART, TILES - 1, WIDE]))
+        nc.scalar.copy(out=gain_wide[:, TILES - 1, :CHUNK], in_=gain_sb[:, TILES - 1 :].to_broadcast([PART, CHUNK]))
+        nc.scalar.copy(out=gain_last[:], in_=gain_sb[:, TILES - 1 :].to_broadcast([PART, WIDE]))
+        opened = [[psum.tile([PART, BANK], F32, name="bank") for j0 in range(0, S, BANK)] for k in range(2)]
         for a in range(K_PASSES - 1):
-            for u in range(2):
+            for k in range(2):
                 for j0 in range(0, S, BANK):
-                    x_pass(opened[u][j0 // BANK][:], 0, u, a, j0, j0 + BANK)
+                    x_pass(opened[k][j0 // BANK][:], k, a, j0)
         for j0 in range(0, S, BANK):
-            gather_words(2, j0, j0 + BANK)
-        cast_w1(0, 2, "scalar")
-        quant_w1(0, 2, 0, 128)
-        quant_w1(0, 2, 128, 256)
-        respond(0, 0, new_sq(), opened[0])
-        respond(0, 1, new_sq(), opened[1])
-        def flat(raw):
-            return raw.rearrange("p j c -> p (j c)")
+            gather_words(2, j0)
+        for half in range(2):
+            cast_w1(0, 2, half, "scalar")
+            quant_w1(0, 2, half * PART, (half + 1) * PART)
+        respond(0, None, opened[0])
+        respond(1, None, opened[1])
+        for a in range(K_PASSES):
+            for half in range(2):
+                cast_w1(1, a, half, "vector")
+            for half in range(2):
+                quant_w1(1, a, half * PART, (half + 1) * PART)
+        respond(2)
+        respond(3)
 
-        def match_left(k, left, lo=0, hi=P):
-            c, u = divmod(k, 2)
-            for i0 in range(lo, hi, GAIN_W):
-                gather_left(c, u, i0, i0 + GAIN_W, left[:, i0 : i0 + GAIN_W], gains[k])
+        z0 = keep.tile([PART, PACK, P], F32, name="z0", tag="table0", align_bytes=64)
+        z0_late = keep.tile([PART, 2, P], F32, name="z0_late")
+        for u in range(2):
+            match(u, w1_raw[1, 2][:].rearrange("p (u j) c -> p u (j c)", u=2)[:, u, :], z0[:, 2 * u, :])
+            nc.sync.dma_start(out=z0[:HALF, 2 * u + 1, :], in_=z0[HALF:, 2 * u, :])
+        for half in range(2):
+            cast_w1(2, 0, half, "vector")
+        for half in range(2):
+            quant_w1(2, 0, half * WIDE, (half + 1) * WIDE)
+        for half in range(2):
+            cast_w1(2, 1, half, "scalar")
+        cast_w1(2, 2, 0, "vector")
+        quant_w1(2, 1, 0, WIDE)
+        quant_w1(2, 2, 0, PART)
+        quant_w1(2, 2, PART, WIDE)
+        cast_w1(2, 2, 1, "scalar")
+        quant_w1(2, 1, WIDE, 2 * WIDE)
+        quant_w1(2, 2, WIDE, 2 * WIDE)
+        sq = {k: keep.tile([PART, S], F32, name="sq%d" % k, align_bytes=64) for k in (TILES - 2, TILES - 1)}
+        for k in range(4, TILES - 1):
+            respond(k, sq.get(k))
+        for u in range(2):
+            match(2 + u, w1_raw[2, 1][:, u, :], z0_late[:, u, :])
+            for i0 in range(0, P, WIDE if u else P):
+                cols = slice(i0, i0 + (WIDE if u else P))
+                nc.sync.dma_start(out=z0[HALF:, 2 * u, cols], in_=z0_late[:HALF, u, cols])
+                nc.sync.dma_start(out=z0[HALF:, 2 * u + 1, cols], in_=z0_late[HALF:, u, cols])
+        z1_bf = keep.tile([PART, PACK * P], BF16, name="z1_bf", align_bytes=64)
+        z1_first = keep.tile([PART, PACK, WIDE], F32, name="z1_first")
+        z1_next = keep.tile([PART, 2, PACK, CHUNK], F32, name="z1_next")
+        left_first = keep.tile([PART, PACK, WIDE], F32, name="left_first")
+        left_next = keep.tile([PART, PACK, CHUNK], F32, name="left_next")
+        left_end = [gain_last[:, :CHUNK], gain_last[:, CHUNK:], left_first[:, 3, :CHUNK], left_first[:, 3, CHUNK:]]
+        z0_bf = [sq[k][:, BANK:].bitcast(BF16) for k in (TILES - 2, TILES - 1)]
 
-        def match_right(k, left):
-            c, u = divmod(k, 2)
-            if c == 0:
-                for g in range(2):
-                    gather_right(c, u, g * GAIN_W, (g + 1) * GAIN_W, left[:, g * GAIN_W : (g + 1) * GAIN_W], z0[:, g, 2 * u, :])
-                nc.sync.dma_start(out=z0[:HALF, :, 2 * u + 1, :], in_=z0[HALF:, :, 2 * u, :])
-            elif u == 0:
-                gather_right(c, u, 0, P, left, z0_late[:, u, :])
-                by_half = z0_late[:, u, :].rearrange("p (g i) -> p g i", g=2)
-                nc.sync.dma_start(out=z0[HALF:, :, 0, :], in_=by_half[:HALF])
-                nc.sync.dma_start(out=z0[HALF:, :, 1, :], in_=by_half[HALF:])
-            else:
-                for g in range(2):
-                    cols = slice(g * GAIN_W, (g + 1) * GAIN_W)
-                    gather_right(c, u, g * GAIN_W, (g + 1) * GAIN_W, left[:, cols], z0_late[:, u, cols])
-                    nc.sync.dma_start(out=z0[HALF:, g, 2, :], in_=z0_late[:HALF, u, cols])
-                    nc.sync.dma_start(out=z0[HALF:, g, 3, :], in_=z0_late[HALF:, u, cols])
+        def round_z(c0, c1, src):
+            cast_z(z1_bf[:, PACK * c0 : PACK * c1], src, "vector")
 
-        cast_w1(1, 0, "vector", "raw02")
-        cast_w1(1, 1, "vector")
-        quant_w1(1, 0, place="raw11")
-        cast_w1(1, 2, "vector")
-        quant_w1(1, 1)
-        quant_w1(1, 2)
-        respond(1, 0, new_sq())
-        stage0 = keep.tile([PART, S], F32, name="stage0", tag="table2", align_bytes=64)
-        respond(1, 1, stage0)
-        left0 = keep.tile([PART, P], F32, name="left0")
-        z0 = keep.tile([PART, 2, PACK, GAIN_W], F32, name="z0", tag="table0", align_bytes=64)
-        cast_w1(2, 0, "vector")
-        match_left(0, left0, 0, GAIN_W)
-        quant_w1(2, 0)
-        match_left(0, left0, GAIN_W, P)
-        cast_w1(2, 1, "vector")
-        match_right(0, left0[:])
-        quant_w1(2, 1)
-        cast_w1(2, 2, "scalar")
-        quant_w1(2, 2, 0, 128)
-        quant_w1(2, 2, 128, 256)
-        lefts = [left0[:], w1_stage[2, 2][:, :P], w1_stage[2, 1][:, :P], w1_raw[2, 2][:, 0, :]]
-        match_left(2, lefts[2])
-        match_left(1, lefts[1])
-        quant_w1(2, 2, 256, 512)
-        match_right(1, lefts[1])
-        late = keep.tile([PART, S], F32, name="late", tag="table1", align_bytes=64)
-        respond(2, 0, late)
-        for t in range(1, PACK):
-            respond(2, t, rows[:, t - 1, :])
-        match_left(3, lefts[3])
-        match_right(2, lefts[2])
-        match_right(3, lefts[3])
-        cast_z(late[:, BANK:].bitcast(BF16), z0[:, 0], "scalar")
-        nc.scalar.activation(out=warm[:], in_=h[2, PACK - 1][:, S - 1 : S], func=ACT.Sqrt, scale=late[:, 0:1])
+        def quant_z1(c0, c1):
+            quant_z(1, c0, c1, z1_bf[:, PACK * c0 : PACK * c1])
 
-        stage2 = keep.tile([PART, QUARTER * PACK], BF16, name="stage2", align_bytes=64)
-        z0_bf = [late[:, BANK:].bitcast(BF16), late[:, :BANK].bitcast(BF16)]
-        z1 = [rows[:, :, S - GAIN_W :], z0[:, 0, :, :QUARTER], rows[:, :, S - QUARTER :]]
-        z1_bf = [stage0[:, :BANK].bitcast(BF16), rows[:, 0, S - 3 * QUARTER : S - QUARTER].bitcast(BF16), stage2[:]]
-        places = [place[:, :GAIN_W] for place in lefts]
-        places += [lefts[1][:, :QUARTER], lefts[1][:, QUARTER : 2 * QUARTER], lefts[0][:, :QUARTER]]
-        places += [z0[:, 0, 0, QUARTER:], rows[:, 1, S - GAIN_W : S - QUARTER], rows[:, 2, S - GAIN_W : S - QUARTER]]
-        places += [z0[:, 1, j, :QUARTER] for j in range(2)]
+        cast_z(z0_bf[0], z0[:, :, :WIDE], "scalar")
+        respond(TILES - 1, sq[TILES - 1])
+        cast_z(z0_bf[1], z0[:, :, WIDE:], "scalar")
+        nc.scalar.activation(out=warm[:], in_=z0_bf[1][:, PACK * WIDE - 1 :], func=ACT.Sqrt, scale=0.0)
 
-        def left_step(k):
-            c, t = divmod(k, PACK)
-            i0, i1 = SPANS[c]
-            gather_left(2, t, i0, i1, places[k], gains[PACK + t][:, : i1 - i0])
+        for t in range(PACK - 1):
+            gather_left(4 + t, 0, WIDE, left_first[:, t, :], gain_wide[:, 4 + t, :])
+            gather_right(4 + t, 0, WIDE, left_first[:, t, :], z1_first[:, t, :])
+        quant_z(0, 0, WIDE, z0_bf[0])
+        for q in range(2):
+            open_y(q, 0, 4)
+        for i0 in range(0, WIDE, CHUNK):
+            gather_left(7, i0, i0 + CHUNK, left_first[:, 3, i0 : i0 + CHUNK], gain_last[:, i0 : i0 + CHUNK])
+        for i0 in range(0, WIDE, CHUNK):
+            gather_right(7, i0, i0 + CHUNK, left_first[:, 3, i0 : i0 + CHUNK], z1_first[:, 3, i0 : i0 + CHUNK])
+        for i0 in range(0, WIDE, CHUNK):
+            round_z(i0, i0 + CHUNK, z1_first[:, :, i0 : i0 + CHUNK])
+        for q in range(2):
+            quant_z1(q * CHUNK, (q + 1) * CHUNK)
+            close_y(q, 0, 4)
+        for q in range(2):
+            magnitude(q, 0, 4)
+        for q in range(2):
+            root_and_store(q, 0, 4)
 
-        def right_step(k, c0=0, c1=None):
-            c, t = divmod(k, PACK)
-            i0, i1 = SPANS[c]
-            if c1 is None:
-                c1 = i1 - i0
-            gather_right(2, t, i0 + c0, i0 + c1, places[k][:, c0:c1], z1[c][:, t, c0:c1])
-
-        def finish(q):
-            mag = ring.tile([PART, N // PART, QUARTER], F32, name="mag", bufs=2)
-            magnitude(q, 0, 4, mag)
-            root_and_store(q, 0, 4, mag)
-            return mag
-
-        left_step(0)
-        for k in range(1, PACK):
-            left_step(k)
-            right_step(k - 1)
-        right_step(3)
-        cast_z(z1_bf[0], z1[0], "scalar")
-        cast_z(z0_bf[1], z0[:, 1], "scalar")
-        left_step(4)
-        left_step(5)
-        quant_z(0, 0, GAIN_W, z0_bf[0])
-        open_y(0, 0, 4)
-        open_y(1, 0, 4)
-        left_step(6)
-        left_step(7)
-        right_step(4)
-        right_step(5)
-        right_step(6)
-        right_step(7)
-        quant_z(1, 0, GAIN_W, z1_bf[0])
-        close_y(0, 0, 4)
-        close_y(1, 0, 4)
-        finish(0)
-        finish(1)
-        cast_z(z1_bf[1], z1[1], "vector")
-        left_step(8)
-        left_step(9)
-        quant_z(1, SPANS[1][0], SPANS[1][1], z1_bf[1])
-        quant_z(0, GAIN_W, P, z0_bf[1])
-        right_step(8)
-        right_step(9)
+        i0 = 2 * CHUNK
+        for t in range(PACK):
+            gather_left(4 + t, i0, i0 + CHUNK, left_next[:, t, :], gain_wide[:, 4 + t, :CHUNK])
+        for t in range(PACK):
+            gather_right(4 + t, i0, i0 + CHUNK, left_next[:, t, :], z1_next[:, 0, t, :])
+        quant_z(0, WIDE, P, z0_bf[1])
         open_y(2, 0, 4)
+        round_z(i0, i0 + CHUNK, z1_next[:, 0])
+        quant_z1(i0, i0 + CHUNK)
         close_y(2, 0, 4)
-        mag_last = finish(2)
         open_y(3, 0, 2)
         open_y(3, 2, 4)
-        left_step(10)
-        left_step(11)
-        right_step(10)
-        last = CHUNKS - 1
-        half = QUARTER // 2
-        for c0 in (0, half):
-            right_step(11, c0, c0 + half)
-        for c0 in (0, half):
-            cast_z(z1_bf[2][:, PACK * c0 : PACK * (c0 + half)], z1[2][:, :, c0 : c0 + half], "vector")
-        for c0 in (0, half):
-            quant_z(1, last * QUARTER + c0, last * QUARTER + c0 + half, z1_bf[2][:, PACK * c0 : PACK * (c0 + half)])
-        close_y(last, 0, 2)
-        close_y(last, 2, 4)
-        magnitude(last, 0, 2, mag_last)
-        magnitude(last, 2, 4, mag_last)
-        root_and_store(last, 0, 2, mag_last)
-        root_and_store(last, 2, 4, mag_last)
+        magnitude(2, 0, 4)
+        root_and_store(2, 0, 4)
+
+        i0 = 3 * CHUNK
+        for t in range(PACK):
+            gather_left(4 + t, i0, i0 + CHUNK, left_end[t], gain_wide[:, 4 + t, :CHUNK])
+        for t in range(PACK - 1):
+            gather_right(4 + t, i0, i0 + CHUNK, left_end[t], z1_next[:, 1, t, :])
+        for c0 in range(0, CHUNK, HALF):
+            gather_right(7, i0 + c0, i0 + c0 + HALF, left_end[3][:, c0 : c0 + HALF], z1_next[:, 1, 3, c0 : c0 + HALF])
+        for c0 in range(0, CHUNK, HALF):
+            round_z(i0 + c0, i0 + c0 + HALF, z1_next[:, 1, :, c0 : c0 + HALF])
+        for c0 in range(0, CHUNK, HALF):
+            quant_z1(i0 + c0, i0 + c0 + HALF)
+        close_y(3, 0, 2)
+        close_y(3, 2, 4)
+        magnitude(3, 0, 2)
+        magnitude(3, 2, 4)
+        root_and_store(3, 0, 2)
+        root_and_store(3, 2, 4)

@@ -40,9 +40,10 @@ def tile_list_stereo_disparity_cost_kernel(tc, tab_words, tab_scales, offs, pos1
         offs_sb = keep.tile([PART, S // STRIPE], U16, name="offs_sb")
         pos1_sb = keep.tile([PART, P // STRIPE], U16, name="pos1_sb")
         pos2_sb = keep.tile([PART, P // STRIPE], U16, name="pos2_sb")
-        gain_raw = keep.tile([PART, PACK, PACK], F32, name="gain_raw")
-        gain_sb = keep.tile([PART, TILES], F32, name="gain_sb")
-        gain_wide = keep.tile([PART, TILES, WIDE], F32, name="gain_wide")
+        gain_raw = keep.tile([PART, 2, PACK], F32, name="gain_raw")
+        gain_sb = keep.tile([PART, PACK], F32, name="gain_sb")
+        gain_dealt = keep.tile([PART, PACK], F32, name="gain_dealt")
+        spread = [keep.tile([PART, PACK, WIDE], F32, name="spread%d" % b) for b in range(R_PASSES)]
         table = [keep.tile([PART, T], I32, name="table", tag="table%d" % a, align_bytes=64) for a in range(K_PASSES)]
         table_sc = keep.tile([PART, T // 4], I32, name="table_sc", align_bytes=64)
         v_sc = keep.tile([PART, S], U8, name="v_sc", align_bytes=64)
@@ -51,10 +52,32 @@ def tile_list_stereo_disparity_cost_kernel(tc, tab_words, tab_scales, offs, pos1
         for b, (r0, r1) in enumerate(GROUPS):
             for a in range(K_PASSES):
                 width = r1 - r0
-                w1_raw[b, a] = keep.tile([PART, PACK, width], F32, name="w1_raw", tag="raw%d%d" % (b, a), align_bytes=64)
-                w1_bf[b, a] = keep.tile([PART, PACK * width], BF16, name="w1_bf%d%d" % (b, a), align_bytes=64)
-                w1_words[b, a] = keep.tile([PART, width], U32, name="w1_words%d%d" % (b, a), align_bytes=64)
-                w1_sc[b, a] = keep.tile([PART, width], U8, name="w1_sc%d%d" % (b, a), align_bytes=64)
+                if (b, a) != (1, 2):
+                    w1_raw[b, a] = keep.tile([PART, PACK, width], F32, name="w1_raw", tag="raw%d%d" % (b, a), align_bytes=64)
+        ahead = keep.tile([PART, (PACK + 1) * WIDE], F32, name="ahead", align_bytes=64)
+        w1_raw[1, 2] = ahead[:, WIDE:].rearrange("p (j c) -> p j c", j=PACK)
+
+        def stage(name, halves):
+            width = (GROUPS[halves[0][0]][1] - GROUPS[halves[0][0]][0]) // 2
+            rounded = keep.tile([PART, len(halves) * width * 2], F32, name="bf" + name, align_bytes=64)
+            words = keep.tile([PART, len(halves) * width], U32, name="words" + name, align_bytes=64)
+            scales = keep.tile([PART, len(halves) * width], U8, name="sc" + name, align_bytes=64)
+            for n, half in enumerate(halves):
+                w1_bf[half] = rounded[:].bitcast(BF16)[:, PACK * n * width : PACK * (n + 1) * width]
+                w1_words[half] = words[:, n * width : (n + 1) * width]
+                w1_sc[half] = scales[:, n * width : (n + 1) * width]
+            return rounded, words, scales
+
+        early = {(b, a): stage("%d%d" % (b, a), [(b, a, 0), (b, a, 1)]) for b in range(2) for a in range(K_PASSES) if (b, a) not in ((0, 1), (0, 2))}
+        for a in range(1, K_PASSES):
+            stage("0%da" % a, [(0, a, 0)])
+        second_tile = stage("0b", [(0, 1, 1), (0, 2, 1)])
+        stage("20a", [(2, 0, 0)])
+        stage("21a", [(2, 1, 0)])
+        firsts = stage("22a", [(2, 2, 0)])
+        seconds = stage("2b", [(2, 0, 1), (2, 1, 1)])
+        stage("22b", [(2, 2, 1)])
+        left_1 = keep.tile([PART, P], F32, name="left_1")
         w2_sb = keep.tile([PART, R_PASSES, N // 2], I32, name="w2_sb", align_bytes=64)
         w2_sc = keep.tile([PART, R_PASSES, N // 4], I32, name="w2_sc", align_bytes=64)
         z_words = [keep.tile([PART, P], U32, name="z_words%d" % b, align_bytes=64) for b in range(R_PASSES)]
@@ -79,10 +102,11 @@ def tile_list_stereo_disparity_cost_kernel(tc, tab_words, tab_scales, offs, pos1
         for q in range(4):
             nc.sync.dma_start(out=table_sc[32 * q : 32 * q + 8, :], in_=tab_scales[:2, 4 * q : 4 * q + 4, :].bitcast(I32))
         load_w1(0, 0)
-        load_w1(0, 1)
         for e in range(2):
-            nc.sync.dma_start(out=gain_raw[HALF * e : HALF * (e + 1)], in_=gain.rearrange("(k m t) -> m k t", k=PACK, t=PACK))
+            nc.sync.dma_start(out=gain_raw[HALF * e : HALF * (e + 1)], in_=gain[:PASS].rearrange("(c m t) -> m c t", c=2, t=PACK))
+        nc.sync.dma_start(out=gain_dealt[:], in_=gain[PASS:].rearrange("(p t) -> p t", t=PACK))
         load_table(2)
+        load_w1(0, 1)
         load_w1(0, 2)
         load_w1(1, 0)
         nc.sync.dma_start(pos1_sb[:], pos1)
@@ -102,27 +126,35 @@ def tile_list_stereo_disparity_cost_kernel(tc, tab_words, tab_scales, offs, pos1
                 nc.vector.tensor_copy(out=dst, in_=src)
 
         def cast_w1(b, a, half, engine):
-            dst = w1_bf[b, a][:].rearrange("p (t m j) -> p m j t", t=PACK, j=PACK)
+            dst = w1_bf[b, a, half].rearrange("p (t m j) -> p m j t", t=2, j=PACK)
             src = w1_raw[b, a][:].rearrange("p j (m t) -> p m j t", t=PACK)
-            copy_on(engine, dst[:, :, :, 2 * half : 2 * half + 2], src[:, :, :, 2 * half : 2 * half + 2])
+            copy_on(engine, dst, src[:, :, :, 2 * half : 2 * half + 2])
 
-        def quant_w1(b, a, c0, c1):
-            nc.vector.quantize_mx(
-                out=w1_words[b, a][:, c0:c1].bitcast(FP8X4), scales=w1_sc[b, a][:, c0:c1], in_=w1_bf[b, a][:, PACK * c0 : PACK * c1]
-            )
+        def quantize(rounded, words, scales):
+            nc.vector.quantize_mx(out=words.bitcast(FP8X4), scales=scales, in_=rounded)
 
-        def gather_words(a, j0, place=None):
-            v_words[a, j0] = keep.tile([PART, BANK], U32, name="v_words", tag=place or "v%d%d" % (a, j0), align_bytes=64)
-            nc.vector.tensor_copy(v_words[a, j0][:], table[a][:].bitcast(U32).indirect(offs_sb[:, j0 // STRIPE : (j0 + BANK) // STRIPE]))
+        def quant_half(b, a, half, c0=0, c1=None):
+            if c1 is None:
+                c1 = w1_sc[b, a, half].shape[1]
+            quantize(w1_bf[b, a, half][:, PACK * c0 : PACK * c1], w1_words[b, a, half][:, c0:c1], w1_sc[b, a, half][:, c0:c1])
+
+        def quant_stage(staged):
+            quantize(staged[0][:].bitcast(BF16), staged[1][:], staged[2][:])
+
+        def gather_words(a, j0, count, place=None):
+            picked = keep.tile([PART, count], U32, name="v_words", tag=place or "v%d%d" % (a, j0), align_bytes=64)
+            nc.vector.tensor_copy(picked[:], table[a][:].bitcast(U32).indirect(offs_sb[:, j0 // STRIPE : (j0 + count) // STRIPE]))
+            for c0 in range(0, count, BANK):
+                v_words[a, j0 + c0] = picked[:, c0 : c0 + BANK]
 
         def x_pass(acc, k, a, j0):
-            b, t = (2, k - 4) if k >= 4 else divmod(k, 2)
+            b, half, t = (2, *divmod(k - 4, 2)) if k >= 4 else (*divmod(k, 2), 0)
             cols = slice(t * PART, (t + 1) * PART)
             nc.tensor.matmul_mx(
                 out=acc,
-                lhsT=w1_words[b, a][:, cols].bitcast(FP8X4),
-                lhsT_scale=w1_sc[b, a][:, cols],
-                rhs=v_words[a, j0][:].bitcast(FP8X4),
+                lhsT=w1_words[b, a, half][:, cols].bitcast(FP8X4),
+                lhsT_scale=w1_sc[b, a, half][:, cols],
+                rhs=v_words[a, j0].bitcast(FP8X4),
                 rhs_scale=v_sc[4 * a : PART, j0 : j0 + BANK],
                 start=(a == 0),
                 stop=(a == K_PASSES - 1),
@@ -133,7 +165,7 @@ def tile_list_stereo_disparity_cost_kernel(tc, tab_words, tab_scales, offs, pos1
                 sq = ring.tile([PART, S], F32, name="sq")
             for j0 in range(0, S, BANK):
                 acc = psum.tile([PART, BANK], F32, name="bank") if opened is None else opened[j0 // BANK]
-                for a in range(0 if opened is None else K_PASSES - 1, K_PASSES):
+                for a in range(0 if opened is None else 1, K_PASSES):
                     x_pass(acc[:], k, a, j0)
                 nc.scalar.activation(out=sq[:, j0 : j0 + BANK], in_=acc[:], func=ACT.Square)
             for j0 in range(0, S, BANK):
@@ -147,7 +179,7 @@ def tile_list_stereo_disparity_cost_kernel(tc, tab_words, tab_scales, offs, pos1
 
         def match(k, left, z):
             for i0 in range(0, P, WIDE):
-                gather_left(k, i0, i0 + WIDE, left[:, i0 : i0 + WIDE], gain_wide[:, k, :])
+                gather_left(k, i0, i0 + WIDE, left[:, i0 : i0 + WIDE], spread[0][:, k, :])
             for i0 in range(0, P, WIDE):
                 gather_right(k, i0, i0 + WIDE, left[:, i0 : i0 + WIDE], z[:, i0 : i0 + WIDE])
 
@@ -173,7 +205,7 @@ def tile_list_stereo_disparity_cost_kernel(tc, tab_words, tab_scales, offs, pos1
         y_acc = {}
 
         def open_y(q, n0, n1):
-            y_acc[q, n0] = psum.tile([PART, N // PART, CHUNK], F32, name="y_acc", tag="bank" if n0 else "y_bank", bufs=4 if n0 else 2)
+            y_acc[q, n0] = psum.tile([PART, N // PART, CHUNK], F32, name="y_acc", tag="bank" if n0 else "y_bank", bufs=4 if n0 else 3)
             for nt in range(n0, n1):
                 y_pass(y_acc[q, n0][:, nt - n0, :], nt, 0, q, nt == n0, False)
 
@@ -184,144 +216,152 @@ def tile_list_stereo_disparity_cost_kernel(tc, tab_words, tab_scales, offs, pos1
         mag = keep.tile([PART, 3, N // PART, CHUNK], F32, name="mag", tag="table2", align_bytes=64)
 
         def magnitude(q, n0, n1):
-            nc.scalar.activation(out=mag[:, min(q, 2), n0:n1, :], in_=y_acc[q, n0][:, : n1 - n0, :], func=ACT.Abs)
+            nc.scalar.activation(out=mag[:, q if q < 3 else 1 + n0 // 2, n0:n1, :], in_=y_acc[q, n0][:, : n1 - n0, :], func=ACT.Abs)
 
         def root_and_store(q, n0, n1):
             cost = ring.tile([PART, n1 - n0, CHUNK], F32, name="cost", bufs=5)
-            nc.scalar.activation(out=cost[:], in_=mag[:, min(q, 2), n0:n1, :], func=ACT.Sqrt)
+            nc.scalar.activation(out=cost[:], in_=mag[:, q if q < 3 else 1 + n0 // 2, n0:n1, :], func=ACT.Sqrt)
             nc.sync.dma_start(out=out_rows[:, n0:n1, q * CHUNK : (q + 1) * CHUNK], in_=cost[:])
 
-        gather_words(0, 0)
-        gather_words(0, BANK)
-        gather_words(1, 0)
-        gather_words(1, BANK)
+        for a in range(2):
+            for j0 in range(0, S, BANK):
+                gather_words(a, j0, BANK)
         nc.vector.tensor_copy(v_sc[:], table_sc[:].bitcast(U8).indirect(offs_sb[:]))
         for half in range(2):
             cast_w1(0, 0, half, "scalar")
-        quant_w1(0, 0, 0, 2 * PART)
-        for half in range(2):
-            cast_w1(0, 1, half, "scalar")
-        quant_w1(0, 1, 0, 2 * PART)
+        quant_stage(early[0, 0])
         for e in range(2):
             half = slice(HALF * e, HALF * (e + 1))
-            nc.scalar.copy(out=gain_sb[half, :PACK].rearrange("p (c u) -> p c u", u=2), in_=gain_raw[half, 0:2, e:PACK:2])
-            nc.scalar.copy(out=gain_sb[half, PACK:], in_=gain_raw[half, 2 + e, :])
-        gain_last = keep.tile([PART, WIDE], F32, name="gain_last")
-        nc.scalar.copy(out=gain_wide[:, : TILES - 1, :], in_=gain_sb[:, : TILES - 1].unsqueeze(2).to_broadcast([PART, TILES - 1, WIDE]))
-        nc.scalar.copy(out=gain_wide[:, TILES - 1, :CHUNK], in_=gain_sb[:, TILES - 1 :].to_broadcast([PART, CHUNK]))
-        nc.scalar.copy(out=gain_last[:], in_=gain_sb[:, TILES - 1 :].to_broadcast([PART, WIDE]))
+            nc.scalar.copy(out=gain_sb[half].rearrange("p (c u) -> p c u", u=2), in_=gain_raw[half, :, e:PACK:2])
+        for b, column in enumerate((gain_sb, gain_dealt)):
+            nc.scalar.copy(out=spread[b][:], in_=column[:].unsqueeze(2).to_broadcast([PART, PACK, WIDE]))
         opened = [[psum.tile([PART, BANK], F32, name="bank") for j0 in range(0, S, BANK)] for k in range(2)]
-        for a in range(K_PASSES - 1):
-            for k in range(2):
-                for j0 in range(0, S, BANK):
-                    x_pass(opened[k][j0 // BANK][:], k, a, j0)
-        for j0 in range(0, S, BANK):
-            gather_words(2, j0)
-        for half in range(2):
-            cast_w1(0, 2, half, "scalar")
-            quant_w1(0, 2, half * PART, (half + 1) * PART)
+        for k in range(2):
+            for j0 in range(0, S, BANK):
+                x_pass(opened[k][j0 // BANK][:], k, 0, j0)
+        gather_words(2, 0, S, "raw00")
+        cast_w1(0, 1, 0, "scalar")
+        quant_half(0, 1, 0)
+        cast_w1(0, 1, 1, "scalar")
+        cast_w1(0, 2, 0, "vector")
+        quant_half(0, 2, 0)
+        cast_w1(0, 2, 1, "scalar")
+        quant_stage(second_tile)
         respond(0, None, opened[0])
         respond(1, None, opened[1])
-        for a in range(K_PASSES):
+        for a in range(K_PASSES - 1):
             for half in range(2):
                 cast_w1(1, a, half, "vector")
             for half in range(2):
-                quant_w1(1, a, half * PART, (half + 1) * PART)
+                quant_half(1, a, half)
+        left_0 = ahead[:, :P]
+        gather_left(0, 0, WIDE, left_0[:, :WIDE], spread[0][:, 0, :])
+        for half in range(2):
+            cast_w1(1, 2, half, "vector")
+        quant_half(1, 2, 0)
+        gather_left(0, WIDE, P, left_0[:, WIDE:], spread[0][:, 0, :])
+        quant_half(1, 2, 1)
         respond(2)
         respond(3)
 
         z0 = keep.tile([PART, PACK, P], F32, name="z0", tag="table0", align_bytes=64)
         z0_late = keep.tile([PART, 2, P], F32, name="z0_late")
-        for u in range(2):
-            match(u, w1_raw[1, 2][:].rearrange("p (u j) c -> p u (j c)", u=2)[:, u, :], z0[:, 2 * u, :])
-            nc.sync.dma_start(out=z0[:HALF, 2 * u + 1, :], in_=z0[HALF:, 2 * u, :])
-        for half in range(2):
-            cast_w1(2, 0, half, "vector")
-        for half in range(2):
-            quant_w1(2, 0, half * WIDE, (half + 1) * WIDE)
-        for half in range(2):
-            cast_w1(2, 1, half, "scalar")
+        gather_right(0, 0, P, left_0, z0[:, 0, :])
+        nc.sync.dma_start(out=z0[:HALF, 1, :], in_=z0[HALF:, 0, :])
+        match(1, left_1[:], z0[:, 2, :])
+        nc.sync.dma_start(out=z0[:HALF, 3, :], in_=z0[HALF:, 2, :])
+        for a in range(K_PASSES - 1):
+            cast_w1(2, a, 0, "vector")
+            quant_half(2, a, 0)
         cast_w1(2, 2, 0, "vector")
-        quant_w1(2, 1, 0, WIDE)
-        quant_w1(2, 2, 0, PART)
-        quant_w1(2, 2, PART, WIDE)
-        cast_w1(2, 2, 1, "scalar")
-        quant_w1(2, 1, WIDE, 2 * WIDE)
-        quant_w1(2, 2, WIDE, 2 * WIDE)
-        sq = {k: keep.tile([PART, S], F32, name="sq%d" % k, align_bytes=64) for k in (TILES - 2, TILES - 1)}
-        for k in range(4, TILES - 1):
-            respond(k, sq.get(k))
+        quant_half(2, 2, 0, 0, PART)
+        quant_half(2, 2, 0, PART, WIDE)
+        for a in range(K_PASSES):
+            cast_w1(2, a, 1, "scalar")
+        last_sq = keep.tile([PART, S], F32, name="last_sq", align_bytes=64)
+        respond(4)
+        respond(5)
+        left_2 = firsts[0][:]
+        gather_left(2, 0, WIDE, left_2[:, :WIDE], spread[0][:, 2, :])
+        quant_stage(seconds)
+        quant_half(2, 2, 1)
+        respond(6)
+        respond(7, last_sq)
+        gather_left(2, WIDE, P, left_2[:, WIDE:], spread[0][:, 2, :])
         for u in range(2):
-            match(2 + u, w1_raw[2, 1][:, u, :], z0_late[:, u, :])
+            if u:
+                match(3, w1_raw[2, 1][:, 0, :], z0_late[:, 1, :])
+            else:
+                for i0 in range(0, P, WIDE):
+                    gather_right(2, i0, i0 + WIDE, left_2[:, i0 : i0 + WIDE], z0_late[:, 0, i0 : i0 + WIDE])
             for i0 in range(0, P, WIDE if u else P):
                 cols = slice(i0, i0 + (WIDE if u else P))
                 nc.sync.dma_start(out=z0[HALF:, 2 * u, cols], in_=z0_late[:HALF, u, cols])
                 nc.sync.dma_start(out=z0[HALF:, 2 * u + 1, cols], in_=z0_late[HALF:, u, cols])
         z1_bf = keep.tile([PART, PACK * P], BF16, name="z1_bf", align_bytes=64)
         z1_first = keep.tile([PART, PACK, WIDE], F32, name="z1_first")
-        z1_next = keep.tile([PART, 2, PACK, CHUNK], F32, name="z1_next")
         left_first = keep.tile([PART, PACK, WIDE], F32, name="left_first")
-        left_next = keep.tile([PART, PACK, CHUNK], F32, name="left_next")
-        left_end = [gain_last[:, :CHUNK], gain_last[:, CHUNK:], left_first[:, 3, :CHUNK], left_first[:, 3, CHUNK:]]
-        z0_bf = [sq[k][:, BANK:].bitcast(BF16) for k in (TILES - 2, TILES - 1)]
+        z0_bf = last_sq[:].bitcast(BF16)
 
-        def round_z(c0, c1, src):
-            cast_z(z1_bf[:, PACK * c0 : PACK * c1], src, "vector")
+        def round_z(c0, c1, src, engine):
+            cast_z(z1_bf[:, PACK * c0 : PACK * c1], src, engine)
 
         def quant_z1(c0, c1):
             quant_z(1, c0, c1, z1_bf[:, PACK * c0 : PACK * c1])
 
-        cast_z(z0_bf[0], z0[:, :, :WIDE], "scalar")
-        respond(TILES - 1, sq[TILES - 1])
-        cast_z(z0_bf[1], z0[:, :, WIDE:], "scalar")
-        nc.scalar.activation(out=warm[:], in_=z0_bf[1][:, PACK * WIDE - 1 :], func=ACT.Sqrt, scale=0.0)
+        for i0 in range(0, P, WIDE):
+            cast_z(z0_bf[:, PACK * i0 : PACK * (i0 + WIDE)], z0[:, :, i0 : i0 + WIDE], "scalar")
+        nc.scalar.activation(out=warm[:], in_=z0_bf[:, PACK * P - 1 :], func=ACT.Sqrt, scale=0.0)
 
-        for t in range(PACK - 1):
-            gather_left(4 + t, 0, WIDE, left_first[:, t, :], gain_wide[:, 4 + t, :])
+        for t in range(PACK):
+            gather_left(4 + t, 0, WIDE, left_first[:, t, :], spread[1][:, t, :])
+        for t in range(PACK):
             gather_right(4 + t, 0, WIDE, left_first[:, t, :], z1_first[:, t, :])
-        quant_z(0, 0, WIDE, z0_bf[0])
+        quant_z(0, 0, WIDE, z0_bf[:, : PACK * WIDE])
         for q in range(2):
             open_y(q, 0, 4)
         for i0 in range(0, WIDE, CHUNK):
-            gather_left(7, i0, i0 + CHUNK, left_first[:, 3, i0 : i0 + CHUNK], gain_last[:, i0 : i0 + CHUNK])
-        for i0 in range(0, WIDE, CHUNK):
-            gather_right(7, i0, i0 + CHUNK, left_first[:, 3, i0 : i0 + CHUNK], z1_first[:, 3, i0 : i0 + CHUNK])
-        for i0 in range(0, WIDE, CHUNK):
-            round_z(i0, i0 + CHUNK, z1_first[:, :, i0 : i0 + CHUNK])
+            round_z(i0, i0 + CHUNK, z1_first[:, :, i0 : i0 + CHUNK], "vector")
+
+        i0 = 2 * CHUNK
+        left_rest = keep.tile([PART, PACK, CHUNK], F32, name="left_rest")
+        left_next = [left_rest[:, t, :] for t in range(PACK)]
+        z1_next = keep.tile([PART, PACK, CHUNK], F32, name="z1_next")[:]
+        left_end = [left_first[:, 3, :CHUNK], left_first[:, 3, CHUNK:], z1_first[:, 0, :CHUNK], left_next[3]]
+        for t in range(PACK):
+            gather_left(4 + t, i0, i0 + CHUNK, left_next[t], spread[1][:, t, :CHUNK])
         for q in range(2):
             quant_z1(q * CHUNK, (q + 1) * CHUNK)
             close_y(q, 0, 4)
-        for q in range(2):
-            magnitude(q, 0, 4)
-        for q in range(2):
-            root_and_store(q, 0, 4)
-
-        i0 = 2 * CHUNK
         for t in range(PACK):
-            gather_left(4 + t, i0, i0 + CHUNK, left_next[:, t, :], gain_wide[:, 4 + t, :CHUNK])
-        for t in range(PACK):
-            gather_right(4 + t, i0, i0 + CHUNK, left_next[:, t, :], z1_next[:, 0, t, :])
-        quant_z(0, WIDE, P, z0_bf[1])
+            gather_right(4 + t, i0, i0 + CHUNK, left_next[t], z1_next[:, t, :])
+        i1 = 3 * CHUNK
+        gather_left(4, i1, P, left_end[0], spread[1][:, 0, :CHUNK])
+        round_z(i0, i1, z1_next, "vector")
+        quant_z(0, WIDE, P, z0_bf[:, PACK * WIDE :])
         open_y(2, 0, 4)
-        round_z(i0, i0 + CHUNK, z1_next[:, 0])
-        quant_z1(i0, i0 + CHUNK)
+        quant_z1(i0, i1)
         close_y(2, 0, 4)
         open_y(3, 0, 2)
         open_y(3, 2, 4)
+        magnitude(0, 0, 4)
+        magnitude(1, 0, 4)
+        root_and_store(0, 0, 4)
         magnitude(2, 0, 4)
+        root_and_store(1, 0, 4)
         root_and_store(2, 0, 4)
 
-        i0 = 3 * CHUNK
-        for t in range(PACK):
-            gather_left(4 + t, i0, i0 + CHUNK, left_end[t], gain_wide[:, 4 + t, :CHUNK])
+        z1_end = z1_first[:, :, CHUNK:]
+        for t in range(1, PACK):
+            gather_left(4 + t, i1, P, left_end[t], spread[1][:, t, :CHUNK])
         for t in range(PACK - 1):
-            gather_right(4 + t, i0, i0 + CHUNK, left_end[t], z1_next[:, 1, t, :])
+            gather_right(4 + t, i1, P, left_end[t], z1_end[:, t, :])
         for c0 in range(0, CHUNK, HALF):
-            gather_right(7, i0 + c0, i0 + c0 + HALF, left_end[3][:, c0 : c0 + HALF], z1_next[:, 1, 3, c0 : c0 + HALF])
+            gather_right(7, i1 + c0, i1 + c0 + HALF, left_end[3][:, c0 : c0 + HALF], z1_end[:, 3, c0 : c0 + HALF])
         for c0 in range(0, CHUNK, HALF):
-            round_z(i0 + c0, i0 + c0 + HALF, z1_next[:, 1, :, c0 : c0 + HALF])
+            round_z(i1 + c0, i1 + c0 + HALF, z1_end[:, :, c0 : c0 + HALF], "vector")
         for c0 in range(0, CHUNK, HALF):
-            quant_z1(i0 + c0, i0 + c0 + HALF)
+            quant_z1(i1 + c0, i1 + c0 + HALF)
         close_y(3, 0, 2)
         close_y(3, 2, 4)
         magnitude(3, 0, 2)

@@ -57,15 +57,16 @@ def tile_list_stereo_disparity_cost_kernel(tc, tab_words, tab_scales, offs, pos1
         ahead = keep.tile([PART, (PACK + 1) * WIDE], F32, name="ahead", align_bytes=64)
         w1_raw[1, 2] = ahead[:, WIDE:].rearrange("p (j c) -> p j c", j=PACK)
 
-        def stage(name, halves):
+        def stage(name, halves, by_tile=False):
             width = (GROUPS[halves[0][0]][1] - GROUPS[halves[0][0]][0]) // 2
             rounded = keep.tile([PART, len(halves) * width * 2], F32, name="bf" + name, align_bytes=64)
             words = keep.tile([PART, len(halves) * width], U32, name="words" + name, align_bytes=64)
             scales = keep.tile([PART, len(halves) * width], U8, name="sc" + name, align_bytes=64)
+            order = "p (t n c) -> p n t c" if by_tile else "p (n t c) -> p n t c"
             for n, half in enumerate(halves):
-                w1_bf[half] = rounded[:].bitcast(BF16)[:, PACK * n * width : PACK * (n + 1) * width]
-                w1_words[half] = words[:, n * width : (n + 1) * width]
-                w1_sc[half] = scales[:, n * width : (n + 1) * width]
+                w1_bf[half] = rounded[:].bitcast(BF16).rearrange(order, n=len(halves), t=2)[:, n]
+                w1_words[half] = words[:].rearrange(order, n=len(halves), t=2)[:, n]
+                w1_sc[half] = scales[:].rearrange(order, n=len(halves), t=2)[:, n]
             return rounded, words, scales
 
         early = {(b, a): stage("%d%d" % (b, a), [(b, a, 0), (b, a, 1)]) for b in range(2) for a in range(K_PASSES) if (b, a) not in ((0, 1), (0, 2))}
@@ -73,8 +74,7 @@ def tile_list_stereo_disparity_cost_kernel(tc, tab_words, tab_scales, offs, pos1
             stage("0%da" % a, [(0, a, 0)])
         second_tile = stage("0b", [(0, 1, 1), (0, 2, 1)])
         stage("20a", [(2, 0, 0)])
-        stage("21a", [(2, 1, 0)])
-        firsts = stage("22a", [(2, 2, 0)])
+        firsts = stage("2a", [(2, 1, 0), (2, 2, 0)], by_tile=True)
         seconds = stage("2b", [(2, 0, 1), (2, 1, 1)])
         stage("22b", [(2, 2, 1)])
         left_1 = keep.tile([PART, P], F32, name="left_1")
@@ -97,7 +97,7 @@ def tile_list_stereo_disparity_cost_kernel(tc, tab_words, tab_scales, offs, pos1
         nc.sync.dma_start(offs_sb[:], offs)
         load_table(0)
         for r in range(4):
-            nc.gpsimd.dma_start(out=table_sc[8 + r : PART : 32, :], in_=tab_scales[2, r:16:4, :].bitcast(I32))
+            nc.scalar.dma_start(out=table_sc[8 + r : PART : 32, :], in_=tab_scales[2, r:16:4, :].bitcast(I32))
         load_table(1)
         for q in range(4):
             nc.sync.dma_start(out=table_sc[32 * q : 32 * q + 8, :], in_=tab_scales[:2, 4 * q : 4 * q + 4, :].bitcast(I32))
@@ -126,17 +126,18 @@ def tile_list_stereo_disparity_cost_kernel(tc, tab_words, tab_scales, offs, pos1
                 nc.vector.tensor_copy(out=dst, in_=src)
 
         def cast_w1(b, a, half, engine):
-            dst = w1_bf[b, a, half].rearrange("p (t m j) -> p m j t", t=2, j=PACK)
+            dst = w1_bf[b, a, half].rearrange("p t (m j) -> p m j t", j=PACK)
             src = w1_raw[b, a][:].rearrange("p j (m t) -> p m j t", t=PACK)
             copy_on(engine, dst, src[:, :, :, 2 * half : 2 * half + 2])
 
         def quantize(rounded, words, scales):
             nc.vector.quantize_mx(out=words.bitcast(FP8X4), scales=scales, in_=rounded)
 
-        def quant_half(b, a, half, c0=0, c1=None):
-            if c1 is None:
-                c1 = w1_sc[b, a, half].shape[1]
-            quantize(w1_bf[b, a, half][:, PACK * c0 : PACK * c1], w1_words[b, a, half][:, c0:c1], w1_sc[b, a, half][:, c0:c1])
+        def flat(view):
+            return view.rearrange("p t c -> p (t c)")
+
+        def quant_half(b, a, half):
+            quantize(flat(w1_bf[b, a, half]), flat(w1_words[b, a, half]), flat(w1_sc[b, a, half]))
 
         def quant_stage(staged):
             quantize(staged[0][:].bitcast(BF16), staged[1][:], staged[2][:])
@@ -148,12 +149,15 @@ def tile_list_stereo_disparity_cost_kernel(tc, tab_words, tab_scales, offs, pos1
                 v_words[a, j0 + c0] = picked[:, c0 : c0 + BANK]
 
         def x_pass(acc, k, a, j0):
-            b, half, t = (2, *divmod(k - 4, 2)) if k >= 4 else (*divmod(k, 2), 0)
-            cols = slice(t * PART, (t + 1) * PART)
+            if k >= 4:
+                half, t = divmod(k - 4, 2)
+                words, scales = w1_words[2, a, half][:, t], w1_sc[2, a, half][:, t]
+            else:
+                words, scales = flat(w1_words[k // 2, a, k % 2]), flat(w1_sc[k // 2, a, k % 2])
             nc.tensor.matmul_mx(
                 out=acc,
-                lhsT=w1_words[b, a, half][:, cols].bitcast(FP8X4),
-                lhsT_scale=w1_sc[b, a, half][:, cols],
+                lhsT=words.bitcast(FP8X4),
+                lhsT_scale=scales,
                 rhs=v_words[a, j0].bitcast(FP8X4),
                 rhs_scale=v_sc[4 * a : PART, j0 : j0 + BANK],
                 start=(a == 0),
@@ -270,18 +274,19 @@ def tile_list_stereo_disparity_cost_kernel(tc, tab_words, tab_scales, offs, pos1
         nc.sync.dma_start(out=z0[:HALF, 1, :], in_=z0[HALF:, 0, :])
         match(1, left_1[:], z0[:, 2, :])
         nc.sync.dma_start(out=z0[:HALF, 3, :], in_=z0[HALF:, 2, :])
-        for a in range(K_PASSES - 1):
-            cast_w1(2, a, 0, "vector")
-            quant_half(2, a, 0)
+        cast_w1(2, 0, 0, "vector")
+        quant_half(2, 0, 0)
+        cast_w1(2, 1, 0, "vector")
         cast_w1(2, 2, 0, "vector")
-        quant_half(2, 2, 0, 0, PART)
-        quant_half(2, 2, 0, PART, WIDE)
+        for t in range(2):
+            cols = slice(t * WIDE, (t + 1) * WIDE)
+            quantize(firsts[0][:].bitcast(BF16)[:, PACK * cols.start : PACK * cols.stop], firsts[1][:, cols], firsts[2][:, cols])
         for a in range(K_PASSES):
             cast_w1(2, a, 1, "scalar")
         last_sq = keep.tile([PART, S], F32, name="last_sq", align_bytes=64)
         respond(4)
         respond(5)
-        left_2 = firsts[0][:]
+        left_2 = firsts[0][:, :P]
         gather_left(2, 0, WIDE, left_2[:, :WIDE], spread[0][:, 2, :])
         quant_stage(seconds)
         quant_half(2, 2, 1)

@@ -17,17 +17,28 @@ ACT = mybir.ActivationFunctionType
 MULT = mybir.AluOpType.mult
 
 PART = 128
+HALF = PART // 2
+QUAD = 32
+QUADS = PART // QUAD
+ROWS = 4
 PACK = 4
 PASS = PART * PACK
 K_PASSES = K // PASS
 R_PASSES = H // PASS
+LAST = K_PASSES - 1
 BANK = 512
 STRIPE = 16
-CHUNK = 128
-WIDE = 256
-HALF = 64
-GROUPS = [(0, 256), (256, 512), (512, 1024)]
+ALIGN = 64
 TILES = H // PART
+BLOCKS = N // PART
+GROUPS = [(0, 256), (256, 512), (512, 1024)]
+DEALT = len(GROUPS) - 1
+FIRST_DEALT = GROUPS[DEALT][0] // PART
+WIDE = P // 2
+CHUNK = 128
+SLIVER = CHUNK // 2
+X_BANKS = 4
+Y_BANKS = 3
 
 
 def tile_list_stereo_disparity_cost_kernel(tc, tab_words, tab_scales, offs, pos1, pos2, w1, gain, w2_words, w2_scales, out):
@@ -35,53 +46,57 @@ def tile_list_stereo_disparity_cost_kernel(tc, tab_words, tab_scales, offs, pos1
     with ExitStack() as ctx:
         keep = ctx.enter_context(tc.tile_pool(name="keep", bufs=1))
         ring = ctx.enter_context(tc.tile_pool(name="ring", bufs=2))
-        psum = ctx.enter_context(tc.psum_pool(name="psum", bufs=4))
+        psum = ctx.enter_context(tc.psum_pool(name="psum", bufs=X_BANKS))
 
         offs_sb = keep.tile([PART, S // STRIPE], U16, name="offs_sb")
         pos1_sb = keep.tile([PART, P // STRIPE], U16, name="pos1_sb")
         pos2_sb = keep.tile([PART, P // STRIPE], U16, name="pos2_sb")
         gain_raw = keep.tile([PART, 2, PACK], F32, name="gain_raw")
-        gain_sb = keep.tile([PART, PACK], F32, name="gain_sb")
+        gain_early = keep.tile([PART, FIRST_DEALT], F32, name="gain_early")
         gain_dealt = keep.tile([PART, PACK], F32, name="gain_dealt")
-        spread = [keep.tile([PART, PACK, WIDE], F32, name="spread%d" % b) for b in range(R_PASSES)]
-        table = [keep.tile([PART, T], I32, name="table", tag="table%d" % a, align_bytes=64) for a in range(K_PASSES)]
-        table_sc = keep.tile([PART, T // 4], I32, name="table_sc", align_bytes=64)
-        v_sc = keep.tile([PART, S], U8, name="v_sc", align_bytes=64)
+        spread_halves = keep.tile([PART, FIRST_DEALT - 1, WIDE], F32, name="spread_halves")
+        spread_whole = keep.tile([PART, P], F32, name="spread_whole")
+        spread_dealt = keep.tile([PART, PACK, WIDE], F32, name="spread_dealt")
+        gains = [spread_halves[:, k, :] for k in range(FIRST_DEALT - 1)] + [spread_whole[:]] + [spread_dealt[:, j, :] for j in range(PACK)]
+        table = [keep.tile([PART, T], I32, name="table", tag="table%d" % a, align_bytes=ALIGN) for a in range(K_PASSES)]
+        table_sc = keep.tile([PART, T // 4], I32, name="table_sc", align_bytes=ALIGN)
+        v_sc = keep.tile([PART, S], U8, name="v_sc", align_bytes=ALIGN)
         v_words = {}
-        w1_raw, w1_bf, w1_words, w1_sc = {}, {}, {}, {}
-        for b, (r0, r1) in enumerate(GROUPS):
-            for a in range(K_PASSES):
-                width = r1 - r0
-                if (b, a) != (1, 2):
-                    w1_raw[b, a] = keep.tile([PART, PACK, width], F32, name="w1_raw", tag="raw%d%d" % (b, a), align_bytes=64)
-        ahead = keep.tile([PART, (PACK + 1) * WIDE], F32, name="ahead", align_bytes=64)
-        w1_raw[1, 2] = ahead[:, WIDE:].rearrange("p (j c) -> p j c", j=PACK)
+        w1_raw = {
+            (b, a): keep.tile([PART, PACK, c1 - c0], F32, name="w1_raw", tag="raw%d%d" % (b, a), align_bytes=ALIGN)
+            for b, (c0, c1) in enumerate(GROUPS)
+            for a in range(K_PASSES)
+        }
 
-        def stage(name, halves, by_tile=False):
+        w1_bf, w1_words, w1_sc = {}, {}, {}
+
+        def stage(name, halves, by_place=False):
             width = (GROUPS[halves[0][0]][1] - GROUPS[halves[0][0]][0]) // 2
-            rounded = keep.tile([PART, len(halves) * width * 2], F32, name="bf" + name, align_bytes=64)
-            words = keep.tile([PART, len(halves) * width], U32, name="words" + name, align_bytes=64)
-            scales = keep.tile([PART, len(halves) * width], U8, name="sc" + name, align_bytes=64)
-            order = "p (t n c) -> p n t c" if by_tile else "p (n t c) -> p n t c"
+            rounded = keep.tile([PART, len(halves) * width * PACK // 2], F32, name="bf" + name, align_bytes=ALIGN)
+            words = keep.tile([PART, len(halves) * width], U32, name="words" + name, align_bytes=ALIGN)
+            scales = keep.tile([PART, len(halves) * width], U8, name="sc" + name, align_bytes=ALIGN)
+            order = "p (t n c) -> p n t c" if by_place else "p (n t c) -> p n t c"
             for n, half in enumerate(halves):
                 w1_bf[half] = rounded[:].bitcast(BF16).rearrange(order, n=len(halves), t=2)[:, n]
                 w1_words[half] = words[:].rearrange(order, n=len(halves), t=2)[:, n]
                 w1_sc[half] = scales[:].rearrange(order, n=len(halves), t=2)[:, n]
             return rounded, words, scales
 
-        early = {(b, a): stage("%d%d" % (b, a), [(b, a, 0), (b, a, 1)]) for b in range(2) for a in range(K_PASSES) if (b, a) not in ((0, 1), (0, 2))}
+        opening = stage("00", [(0, 0, 0), (0, 0, 1)])
+        for a in range(K_PASSES):
+            stage("1%d" % a, [(1, a, 0), (1, a, 1)])
         for a in range(1, K_PASSES):
             stage("0%da" % a, [(0, a, 0)])
         second_tile = stage("0b", [(0, 1, 1), (0, 2, 1)])
-        stage("20a", [(2, 0, 0)])
-        firsts = stage("2a", [(2, 1, 0), (2, 2, 0)], by_tile=True)
-        seconds = stage("2b", [(2, 0, 1), (2, 1, 1)])
-        stage("22b", [(2, 2, 1)])
+        stage("20a", [(DEALT, 0, 0)])
+        firsts = stage("2a", [(DEALT, 1, 0), (DEALT, 2, 0)], by_place=True)
+        seconds = stage("2b", [(DEALT, 0, 1), (DEALT, 1, 1)])
+        stage("22b", [(DEALT, 2, 1)])
         left_1 = keep.tile([PART, P], F32, name="left_1")
-        w2_sb = keep.tile([PART, R_PASSES, N // 2], I32, name="w2_sb", align_bytes=64)
-        w2_sc = keep.tile([PART, R_PASSES, N // 4], I32, name="w2_sc", align_bytes=64)
-        z_words = [keep.tile([PART, P], U32, name="z_words%d" % b, align_bytes=64) for b in range(R_PASSES)]
-        z_sc = [keep.tile([PART, P], U8, name="z_sc%d" % b, align_bytes=64) for b in range(R_PASSES)]
+        w2_sb = keep.tile([PART, R_PASSES, N // 2], I32, name="w2_sb", align_bytes=ALIGN)
+        w2_sc = keep.tile([PART, R_PASSES, N // 4], I32, name="w2_sc", align_bytes=ALIGN)
+        z_words = [keep.tile([PART, P], U32, name="z_words%d" % b, align_bytes=ALIGN) for b in range(R_PASSES)]
+        z_sc = [keep.tile([PART, P], U8, name="z_sc%d" % b, align_bytes=ALIGN) for b in range(R_PASSES)]
         h = [keep.tile([PART, S], F32, name="h%d" % k) for k in range(TILES)]
         warm = keep.tile([PART, 1], F32, name="warm")
 
@@ -96,15 +111,14 @@ def tile_list_stereo_disparity_cost_kernel(tc, tab_words, tab_scales, offs, pos1
         nc.vector.memset(w2_sc[:], 0)
         nc.sync.dma_start(offs_sb[:], offs)
         load_table(0)
-        for r in range(4):
-            nc.scalar.dma_start(out=table_sc[8 + r : PART : 32, :], in_=tab_scales[2, r:16:4, :].bitcast(I32))
-        load_table(1)
-        for q in range(4):
-            nc.sync.dma_start(out=table_sc[32 * q : 32 * q + 8, :], in_=tab_scales[:2, 4 * q : 4 * q + 4, :].bitcast(I32))
-        load_w1(0, 0)
         for e in range(2):
-            nc.sync.dma_start(out=gain_raw[HALF * e : HALF * (e + 1)], in_=gain[:PASS].rearrange("(c m t) -> m c t", c=2, t=PACK))
-        nc.sync.dma_start(out=gain_dealt[:], in_=gain[PASS:].rearrange("(p t) -> p t", t=PACK))
+            nc.sync.dma_start(out=gain_raw[HALF * e : HALF * (e + 1)], in_=gain[:PASS].rearrange("(c m j) -> m c j", c=2, j=PACK))
+        nc.sync.dma_start(out=gain_dealt[:], in_=gain[PASS:].rearrange("(p j) -> p j", j=PACK))
+        load_table(1)
+        for quad in range(QUADS):
+            rows = tab_scales[:, ROWS * quad : ROWS * (quad + 1), :]
+            nc.sync.dma_start(out=table_sc[QUAD * quad : QUAD * quad + ROWS * K_PASSES, :], in_=rows.bitcast(I32))
+        load_w1(0, 0)
         load_table(2)
         load_w1(0, 1)
         load_w1(0, 2)
@@ -114,21 +128,22 @@ def tile_list_stereo_disparity_cost_kernel(tc, tab_words, tab_scales, offs, pos1
         nc.sync.dma_start(pos2_sb[:], pos2)
         load_w1(1, 2)
         for a in range(K_PASSES):
-            load_w1(2, a)
+            load_w1(DEALT, a)
         nc.sync.dma_start(out=w2_sb[:], in_=w2_words.rearrange("b p c -> p b c").bitcast(I32))
-        for r in range(4):
-            nc.sync.dma_start(out=w2_sc[r:PART:32, :, :], in_=w2_scales[:, r:16:4, :].rearrange("b q n -> q b n").bitcast(I32))
+        for s in range(ROWS):
+            rows = w2_scales[:, s : ROWS * QUADS : ROWS, :].rearrange("b q n -> q b n")
+            nc.sync.dma_start(out=w2_sc[s:PART:QUAD, :, :], in_=rows.bitcast(I32))
 
-        def copy_on(engine, dst, src):
-            if engine == "scalar":
-                nc.scalar.copy(out=dst, in_=src)
-            else:
-                nc.vector.tensor_copy(out=dst, in_=src)
+        def on_scalar(dst, src):
+            nc.scalar.copy(out=dst, in_=src)
 
-        def cast_w1(b, a, half, engine):
+        def on_vector(dst, src):
+            nc.vector.tensor_copy(out=dst, in_=src)
+
+        def round_w1(b, a, half, copy):
             dst = w1_bf[b, a, half].rearrange("p t (m j) -> p m j t", j=PACK)
             src = w1_raw[b, a][:].rearrange("p j (m t) -> p m j t", t=PACK)
-            copy_on(engine, dst, src[:, :, :, 2 * half : 2 * half + 2])
+            copy(dst, src[:, :, :, 2 * half : 2 * half + 2])
 
         def quantize(rounded, words, scales):
             nc.vector.quantize_mx(out=words.bitcast(FP8X4), scales=scales, in_=rounded)
@@ -139,32 +154,32 @@ def tile_list_stereo_disparity_cost_kernel(tc, tab_words, tab_scales, offs, pos1
         def quant_half(b, a, half):
             quantize(flat(w1_bf[b, a, half]), flat(w1_words[b, a, half]), flat(w1_sc[b, a, half]))
 
-        def quant_stage(staged):
-            quantize(staged[0][:].bitcast(BF16), staged[1][:], staged[2][:])
+        def quant_stage(staged, c0, c1):
+            quantize(staged[0][:].bitcast(BF16)[:, PACK * c0 : PACK * c1], staged[1][:, c0:c1], staged[2][:, c0:c1])
 
-        def gather_words(a, j0, count, place=None):
-            picked = keep.tile([PART, count], U32, name="v_words", tag=place or "v%d%d" % (a, j0), align_bytes=64)
-            nc.vector.tensor_copy(picked[:], table[a][:].bitcast(U32).indirect(offs_sb[:, j0 // STRIPE : (j0 + count) // STRIPE]))
-            for c0 in range(0, count, BANK):
-                v_words[a, j0 + c0] = picked[:, c0 : c0 + BANK]
+        def gather_words(a, place):
+            picked = keep.tile([PART, S], U32, name="v_words", tag=place, align_bytes=ALIGN)
+            nc.vector.tensor_copy(picked[:], table[a][:].bitcast(U32).indirect(offs_sb[:]))
+            v_words[a] = picked
 
         def x_pass(acc, k, a, j0):
-            if k >= 4:
-                half, t = divmod(k - 4, 2)
-                words, scales = w1_words[2, a, half][:, t], w1_sc[2, a, half][:, t]
+            if k >= FIRST_DEALT:
+                half, t = divmod(k - FIRST_DEALT, 2)
+                words, scales = w1_words[DEALT, a, half][:, t], w1_sc[DEALT, a, half][:, t]
             else:
-                words, scales = flat(w1_words[k // 2, a, k % 2]), flat(w1_sc[k // 2, a, k % 2])
+                b, half = divmod(k, 2)
+                words, scales = flat(w1_words[b, a, half]), flat(w1_sc[b, a, half])
             nc.tensor.matmul_mx(
                 out=acc,
                 lhsT=words.bitcast(FP8X4),
                 lhsT_scale=scales,
-                rhs=v_words[a, j0].bitcast(FP8X4),
-                rhs_scale=v_sc[4 * a : PART, j0 : j0 + BANK],
+                rhs=v_words[a][:, j0 : j0 + BANK].bitcast(FP8X4),
+                rhs_scale=v_sc[ROWS * a : PART, j0 : j0 + BANK],
                 start=(a == 0),
-                stop=(a == K_PASSES - 1),
+                stop=(a == LAST),
             )
 
-        def respond(k, sq=None, opened=None):
+        def respond(k, step, sq=None, opened=None):
             if sq is None:
                 sq = ring.tile([PART, S], F32, name="sq")
             for j0 in range(0, S, BANK):
@@ -172,26 +187,26 @@ def tile_list_stereo_disparity_cost_kernel(tc, tab_words, tab_scales, offs, pos1
                 for a in range(0 if opened is None else 1, K_PASSES):
                     x_pass(acc[:], k, a, j0)
                 nc.scalar.activation(out=sq[:, j0 : j0 + BANK], in_=acc[:], func=ACT.Square)
-            for j0 in range(0, S, BANK):
-                nc.scalar.activation(out=h[k][:, j0 : j0 + BANK], in_=sq[:, j0 : j0 + BANK], func=ACT.Exp, scale=-1.0)
+            for j0 in range(0, S, step):
+                nc.scalar.activation(out=h[k][:, j0 : j0 + step], in_=sq[:, j0 : j0 + step], func=ACT.Exp, scale=-1.0)
 
-        def gather_left(k, i0, i1, left, gains):
-            nc.vector.tensor_tensor(left, h[k][:].indirect(pos1_sb[:, i0 // STRIPE : i1 // STRIPE]), gains, MULT)
+        def gather_left(k, i0, i1, left):
+            nc.vector.tensor_tensor(left, h[k][:].indirect(pos1_sb[:, i0 // STRIPE : i1 // STRIPE]), gains[k][:, : i1 - i0], MULT)
 
         def gather_right(k, i0, i1, left, z):
             nc.vector.tensor_tensor(z, h[k][:].indirect(pos2_sb[:, i0 // STRIPE : i1 // STRIPE]), left, MULT)
 
         def match(k, left, z):
             for i0 in range(0, P, WIDE):
-                gather_left(k, i0, i0 + WIDE, left[:, i0 : i0 + WIDE], spread[0][:, k, :])
+                gather_left(k, i0, i0 + WIDE, left[:, i0 : i0 + WIDE])
             for i0 in range(0, P, WIDE):
                 gather_right(k, i0, i0 + WIDE, left[:, i0 : i0 + WIDE], z[:, i0 : i0 + WIDE])
 
-        def cast_z(dst, src, engine):
-            copy_on(engine, dst.rearrange("p (c i t) -> p c t i", i=4, t=PACK), src.rearrange("p t (c i) -> p c t i", i=4))
+        def round_z(dst, src, copy):
+            copy(dst.rearrange("p (c i j) -> p c j i", i=4, j=PACK), src.rearrange("p j (c i) -> p c j i", i=4))
 
-        def quant_z(b, i0, i1, src):
-            nc.vector.quantize_mx(out=z_words[b][:, i0:i1].bitcast(FP8X4), scales=z_sc[b][:, i0:i1], in_=src)
+        def quant_z(b, i0, i1, rounded):
+            quantize(rounded[:, PACK * i0 : PACK * i1], z_words[b][:, i0:i1], z_sc[b][:, i0:i1])
 
         def y_pass(acc, nt, b, q, start, stop):
             cols = slice(q * CHUNK, (q + 1) * CHUNK)
@@ -207,9 +222,10 @@ def tile_list_stereo_disparity_cost_kernel(tc, tab_words, tab_scales, offs, pos1
 
         out_rows = out.rearrange("(nt p) i -> p nt i", p=PART)
         y_acc = {}
+        mag = keep.tile([PART, Y_BANKS, BLOCKS, CHUNK], F32, name="mag", tag="table%d" % LAST, align_bytes=ALIGN)
 
-        def open_y(q, n0, n1):
-            y_acc[q, n0] = psum.tile([PART, N // PART, CHUNK], F32, name="y_acc", tag="bank" if n0 else "y_bank", bufs=4 if n0 else 3)
+        def open_y(q, n0, n1, tag, bufs):
+            y_acc[q, n0] = psum.tile([PART, BLOCKS, CHUNK], F32, name="y_acc", tag=tag, bufs=bufs)
             for nt in range(n0, n1):
                 y_pass(y_acc[q, n0][:, nt - n0, :], nt, 0, q, nt == n0, False)
 
@@ -217,159 +233,150 @@ def tile_list_stereo_disparity_cost_kernel(tc, tab_words, tab_scales, offs, pos1
             for nt in range(n0, n1):
                 y_pass(y_acc[q, n0][:, nt - n0, :], nt, 1, q, False, nt == n1 - 1)
 
-        mag = keep.tile([PART, 3, N // PART, CHUNK], F32, name="mag", tag="table2", align_bytes=64)
+        def magnitude(q, n0, n1, slot):
+            nc.scalar.activation(out=mag[:, slot, n0:n1, :], in_=y_acc[q, n0][:, : n1 - n0, :], func=ACT.Abs)
 
-        def magnitude(q, n0, n1):
-            nc.scalar.activation(out=mag[:, q if q < 3 else 1 + n0 // 2, n0:n1, :], in_=y_acc[q, n0][:, : n1 - n0, :], func=ACT.Abs)
-
-        def root_and_store(q, n0, n1):
-            cost = ring.tile([PART, n1 - n0, CHUNK], F32, name="cost", bufs=5)
-            nc.scalar.activation(out=cost[:], in_=mag[:, q if q < 3 else 1 + n0 // 2, n0:n1, :], func=ACT.Sqrt)
+        def root_and_store(q, n0, n1, slot):
+            cost = keep.tile([PART, n1 - n0, CHUNK], F32, name="cost%d%d" % (q, n0))
+            nc.scalar.activation(out=cost[:], in_=mag[:, slot, n0:n1, :], func=ACT.Sqrt)
             nc.sync.dma_start(out=out_rows[:, n0:n1, q * CHUNK : (q + 1) * CHUNK], in_=cost[:])
 
-        for a in range(2):
-            for j0 in range(0, S, BANK):
-                gather_words(a, j0, BANK)
+        for a in range(LAST):
+            gather_words(a, "v%d" % a)
         nc.vector.tensor_copy(v_sc[:], table_sc[:].bitcast(U8).indirect(offs_sb[:]))
         for half in range(2):
-            cast_w1(0, 0, half, "scalar")
-        quant_stage(early[0, 0])
+            round_w1(0, 0, half, on_scalar)
+        quant_stage(opening, 0, WIDE)
         for e in range(2):
-            half = slice(HALF * e, HALF * (e + 1))
-            nc.scalar.copy(out=gain_sb[half].rearrange("p (c u) -> p c u", u=2), in_=gain_raw[half, :, e:PACK:2])
-        for b, column in enumerate((gain_sb, gain_dealt)):
-            nc.scalar.copy(out=spread[b][:], in_=column[:].unsqueeze(2).to_broadcast([PART, PACK, WIDE]))
+            rows = slice(HALF * e, HALF * (e + 1))
+            on_scalar(gain_early[rows].rearrange("p (c u) -> p c u", u=2), gain_raw[rows, :, e:PACK:2])
+        on_scalar(spread_halves[:], gain_early[:, : FIRST_DEALT - 1].unsqueeze(2).to_broadcast([PART, FIRST_DEALT - 1, WIDE]))
+        on_scalar(spread_whole[:], gain_early[:, FIRST_DEALT - 1 :].to_broadcast([PART, P]))
+        on_scalar(spread_dealt[:], gain_dealt[:].unsqueeze(2).to_broadcast([PART, PACK, WIDE]))
         opened = [[psum.tile([PART, BANK], F32, name="bank") for j0 in range(0, S, BANK)] for k in range(2)]
         for k in range(2):
             for j0 in range(0, S, BANK):
                 x_pass(opened[k][j0 // BANK][:], k, 0, j0)
-        gather_words(2, 0, S, "raw00")
-        cast_w1(0, 1, 0, "scalar")
-        quant_half(0, 1, 0)
-        cast_w1(0, 1, 1, "scalar")
-        cast_w1(0, 2, 0, "vector")
-        quant_half(0, 2, 0)
-        cast_w1(0, 2, 1, "scalar")
-        quant_stage(second_tile)
-        respond(0, None, opened[0])
-        respond(1, None, opened[1])
-        for a in range(K_PASSES - 1):
+        gather_words(LAST, "raw00")
+        for a in range(1, K_PASSES):
+            round_w1(0, a, 0, on_scalar)
+            quant_half(0, a, 0)
+            round_w1(0, a, 1, on_scalar)
+        quant_stage(second_tile, 0, WIDE)
+        for k in range(2):
+            respond(k, BANK, opened=opened[k])
+
+        for a in range(K_PASSES):
             for half in range(2):
-                cast_w1(1, a, half, "vector")
+                round_w1(1, a, half, on_vector)
             for half in range(2):
                 quant_half(1, a, half)
-        left_0 = ahead[:, :P]
-        gather_left(0, 0, WIDE, left_0[:, :WIDE], spread[0][:, 0, :])
-        for half in range(2):
-            cast_w1(1, 2, half, "vector")
-        quant_half(1, 2, 0)
-        gather_left(0, WIDE, P, left_0[:, WIDE:], spread[0][:, 0, :])
-        quant_half(1, 2, 1)
-        respond(2)
-        respond(3)
+        respond(2, S)
+        respond(3, S)
 
-        z0 = keep.tile([PART, PACK, P], F32, name="z0", tag="table0", align_bytes=64)
+        z0 = keep.tile([PART, PACK, P], F32, name="z0", tag="table0", align_bytes=ALIGN)
         z0_late = keep.tile([PART, 2, P], F32, name="z0_late")
-        gather_right(0, 0, P, left_0, z0[:, 0, :])
+        match(0, w1_raw[1, LAST][:].rearrange("p j c -> p (j c)")[:, :P], z0[:, 0, :])
         nc.sync.dma_start(out=z0[:HALF, 1, :], in_=z0[HALF:, 0, :])
+        left_2 = keep.tile([PART, WIDE], F32, name="left_2")
         match(1, left_1[:], z0[:, 2, :])
         nc.sync.dma_start(out=z0[:HALF, 3, :], in_=z0[HALF:, 2, :])
-        cast_w1(2, 0, 0, "vector")
-        quant_half(2, 0, 0)
-        cast_w1(2, 1, 0, "vector")
-        cast_w1(2, 2, 0, "vector")
-        for t in range(2):
-            cols = slice(t * WIDE, (t + 1) * WIDE)
-            quantize(firsts[0][:].bitcast(BF16)[:, PACK * cols.start : PACK * cols.stop], firsts[1][:, cols], firsts[2][:, cols])
+        round_w1(DEALT, 0, 0, on_vector)
+        quant_half(DEALT, 0, 0)
+        round_w1(DEALT, 1, 0, on_vector)
+        gather_left(2, 0, WIDE, left_2[:])
+        gather_right(2, 0, WIDE, left_2[:], z0_late[:, 0, :WIDE])
+        round_w1(DEALT, LAST, 0, on_vector)
+        quant_stage(firsts, 0, PART)
+        quant_stage(firsts, PART, 2 * PART)
+        quant_stage(firsts, 2 * PART, 4 * PART)
         for a in range(K_PASSES):
-            cast_w1(2, a, 1, "scalar")
-        last_sq = keep.tile([PART, S], F32, name="last_sq", align_bytes=64)
-        respond(4)
-        respond(5)
-        left_2 = firsts[0][:, :P]
-        gather_left(2, 0, WIDE, left_2[:, :WIDE], spread[0][:, 2, :])
-        quant_stage(seconds)
-        quant_half(2, 2, 1)
-        respond(6)
-        respond(7, last_sq)
-        gather_left(2, WIDE, P, left_2[:, WIDE:], spread[0][:, 2, :])
-        for u in range(2):
-            if u:
-                match(3, w1_raw[2, 1][:, 0, :], z0_late[:, 1, :])
-            else:
-                for i0 in range(0, P, WIDE):
-                    gather_right(2, i0, i0 + WIDE, left_2[:, i0 : i0 + WIDE], z0_late[:, 0, i0 : i0 + WIDE])
-            for i0 in range(0, P, WIDE if u else P):
-                cols = slice(i0, i0 + (WIDE if u else P))
-                nc.sync.dma_start(out=z0[HALF:, 2 * u, cols], in_=z0_late[:HALF, u, cols])
-                nc.sync.dma_start(out=z0[HALF:, 2 * u + 1, cols], in_=z0_late[HALF:, u, cols])
-        z1_bf = keep.tile([PART, PACK * P], BF16, name="z1_bf", align_bytes=64)
+            round_w1(DEALT, a, 1, on_scalar)
+        last_sq = keep.tile([PART, S], F32, name="last_sq", align_bytes=ALIGN)
+        respond(4, S)
+        respond(5, S)
+        left_2_rest, left_3 = firsts[0][:, WIDE:P], firsts[0][:, P:]
+        gather_left(2, WIDE, P, left_2_rest)
+        gather_left(3, 0, P, left_3)
+        quant_stage(seconds, 0, P)
+        quant_half(DEALT, LAST, 1)
+        respond(6, S)
+        respond(7, BANK, sq=last_sq)
+
+        def lift(u):
+            nc.sync.dma_start(out=z0[HALF:, 2 * u, :], in_=z0_late[:HALF, u, :])
+            nc.sync.dma_start(out=z0[HALF:, 2 * u + 1, :], in_=z0_late[HALF:, u, :])
+
+        gather_right(2, WIDE, P, left_2_rest, z0_late[:, 0, WIDE:])
+        lift(0)
+        gather_right(3, 0, P, left_3, z0_late[:, 1, :])
+        lift(1)
+
+        z1_bf = keep.tile([PART, PACK * P], BF16, name="z1_bf", align_bytes=ALIGN)
         z1_first = keep.tile([PART, PACK, WIDE], F32, name="z1_first")
         left_first = keep.tile([PART, PACK, WIDE], F32, name="left_first")
+        dealt = range(FIRST_DEALT, TILES)
+
+        def round_z1(i0, i1, src):
+            round_z(z1_bf[:, PACK * i0 : PACK * i1], src, on_vector)
+
         z0_bf = last_sq[:].bitcast(BF16)
-
-        def round_z(c0, c1, src, engine):
-            cast_z(z1_bf[:, PACK * c0 : PACK * c1], src, engine)
-
-        def quant_z1(c0, c1):
-            quant_z(1, c0, c1, z1_bf[:, PACK * c0 : PACK * c1])
-
         for i0 in range(0, P, WIDE):
-            cast_z(z0_bf[:, PACK * i0 : PACK * (i0 + WIDE)], z0[:, :, i0 : i0 + WIDE], "scalar")
+            round_z(z0_bf[:, PACK * i0 : PACK * (i0 + WIDE)], z0[:, :, i0 : i0 + WIDE], on_scalar)
         nc.scalar.activation(out=warm[:], in_=z0_bf[:, PACK * P - 1 :], func=ACT.Sqrt, scale=0.0)
 
-        for t in range(PACK):
-            gather_left(4 + t, 0, WIDE, left_first[:, t, :], spread[1][:, t, :])
-        for t in range(PACK):
-            gather_right(4 + t, 0, WIDE, left_first[:, t, :], z1_first[:, t, :])
-        quant_z(0, 0, WIDE, z0_bf[:, : PACK * WIDE])
+        for j, k in enumerate(dealt):
+            gather_left(k, 0, WIDE, left_first[:, j, :])
+        for j, k in enumerate(dealt):
+            gather_right(k, 0, WIDE, left_first[:, j, :], z1_first[:, j, :])
+        quant_z(0, 0, WIDE, z0_bf)
         for q in range(2):
-            open_y(q, 0, 4)
+            open_y(q, 0, BLOCKS, "y_bank", Y_BANKS)
         for i0 in range(0, WIDE, CHUNK):
-            round_z(i0, i0 + CHUNK, z1_first[:, :, i0 : i0 + CHUNK], "vector")
+            round_z1(i0, i0 + CHUNK, z1_first[:, :, i0 : i0 + CHUNK])
 
-        i0 = 2 * CHUNK
-        left_rest = keep.tile([PART, PACK, CHUNK], F32, name="left_rest")
-        left_next = [left_rest[:, t, :] for t in range(PACK)]
-        z1_next = keep.tile([PART, PACK, CHUNK], F32, name="z1_next")[:]
-        left_end = [left_first[:, 3, :CHUNK], left_first[:, 3, CHUNK:], z1_first[:, 0, :CHUNK], left_next[3]]
-        for t in range(PACK):
-            gather_left(4 + t, i0, i0 + CHUNK, left_next[t], spread[1][:, t, :CHUNK])
+        third, fourth = 2 * CHUNK, 3 * CHUNK
+        left_third = keep.tile([PART, PACK, CHUNK], F32, name="left_third")
+        z1_third = keep.tile([PART, PACK, CHUNK], F32, name="z1_third")
+        left_fourth = [left_first[:, PACK - 1, :CHUNK], left_first[:, PACK - 1, CHUNK:], z1_first[:, 0, :CHUNK], left_third[:, PACK - 1, :]]
+        z1_fourth = z1_first[:, :, CHUNK:]
+        for j, k in enumerate(dealt):
+            gather_left(k, third, fourth, left_third[:, j, :])
         for q in range(2):
-            quant_z1(q * CHUNK, (q + 1) * CHUNK)
-            close_y(q, 0, 4)
-        for t in range(PACK):
-            gather_right(4 + t, i0, i0 + CHUNK, left_next[t], z1_next[:, t, :])
-        i1 = 3 * CHUNK
-        gather_left(4, i1, P, left_end[0], spread[1][:, 0, :CHUNK])
-        round_z(i0, i1, z1_next, "vector")
-        quant_z(0, WIDE, P, z0_bf[:, PACK * WIDE :])
-        open_y(2, 0, 4)
-        quant_z1(i0, i1)
-        close_y(2, 0, 4)
-        open_y(3, 0, 2)
-        open_y(3, 2, 4)
-        magnitude(0, 0, 4)
-        magnitude(1, 0, 4)
-        root_and_store(0, 0, 4)
-        magnitude(2, 0, 4)
-        root_and_store(1, 0, 4)
-        root_and_store(2, 0, 4)
+            quant_z(1, q * CHUNK, (q + 1) * CHUNK, z1_bf)
+            close_y(q, 0, BLOCKS)
+        for j, k in enumerate(dealt):
+            gather_right(k, third, fourth, left_third[:, j, :], z1_third[:, j, :])
+        gather_left(FIRST_DEALT, fourth, P, left_fourth[0])
+        round_z1(third, fourth, z1_third[:])
+        quant_z(0, WIDE, P, z0_bf)
+        open_y(2, 0, BLOCKS, "y_bank", Y_BANKS)
+        quant_z(1, third, fourth, z1_bf)
+        close_y(2, 0, BLOCKS)
+        parts = [(0, BLOCKS // 2), (BLOCKS // 2, BLOCKS)]
+        open_y(3, *parts[0], "y_bank", Y_BANKS)
+        open_y(3, *parts[1], "bank", X_BANKS)
+        magnitude(0, 0, BLOCKS, 0)
+        magnitude(1, 0, BLOCKS, 1)
+        root_and_store(0, 0, BLOCKS, 0)
+        magnitude(2, 0, BLOCKS, 2)
+        root_and_store(1, 0, BLOCKS, 1)
+        root_and_store(2, 0, BLOCKS, 2)
 
-        z1_end = z1_first[:, :, CHUNK:]
-        for t in range(1, PACK):
-            gather_left(4 + t, i1, P, left_end[t], spread[1][:, t, :CHUNK])
-        for t in range(PACK - 1):
-            gather_right(4 + t, i1, P, left_end[t], z1_end[:, t, :])
-        for c0 in range(0, CHUNK, HALF):
-            gather_right(7, i1 + c0, i1 + c0 + HALF, left_end[3][:, c0 : c0 + HALF], z1_end[:, 3, c0 : c0 + HALF])
-        for c0 in range(0, CHUNK, HALF):
-            round_z(i1 + c0, i1 + c0 + HALF, z1_end[:, :, c0 : c0 + HALF], "vector")
-        for c0 in range(0, CHUNK, HALF):
-            quant_z1(i1 + c0, i1 + c0 + HALF)
-        close_y(3, 0, 2)
-        close_y(3, 2, 4)
-        magnitude(3, 0, 2)
-        magnitude(3, 2, 4)
-        root_and_store(3, 0, 2)
-        root_and_store(3, 2, 4)
+        for j in range(1, PACK):
+            gather_left(dealt[j], fourth, P, left_fourth[j])
+        for j in range(PACK - 1):
+            gather_right(dealt[j], fourth, P, left_fourth[j], z1_fourth[:, j, :])
+        slivers = [slice(c0, c0 + SLIVER) for c0 in range(0, CHUNK, SLIVER)]
+        for cols in slivers:
+            gather_right(TILES - 1, fourth + cols.start, fourth + cols.stop, left_fourth[PACK - 1][:, cols], z1_fourth[:, PACK - 1, cols])
+        for cols in slivers:
+            round_z1(fourth + cols.start, fourth + cols.stop, z1_fourth[:, :, cols])
+        for cols in slivers:
+            quant_z(1, fourth + cols.start, fourth + cols.stop, z1_bf)
+        for part in parts:
+            close_y(3, *part)
+        for slot, part in enumerate(parts, 1):
+            magnitude(3, *part, slot)
+        for slot, part in enumerate(parts, 1):
+            root_and_store(3, *part, slot)

@@ -1,6 +1,7 @@
 from contextlib import ExitStack
 
 import concourse.mybir as mybir
+from concourse.masks import make_identity
 
 K, H, N, T, S, P = 1536, 1024, 512, 2048, 1024, 512
 FLOPS = 2 * K * H * S + 2 * H * N * P
@@ -31,13 +32,13 @@ STRIPE = 16
 ALIGN = 64
 TILES = H // PART
 BLOCKS = N // PART
-GROUPS = [(0, 256), (256, 512), (512, 1024)]
+GROUPS = [(0, 128), (128, 256), (256, 512), (512, 1024)]
 DEALT = len(GROUPS) - 1
 FIRST_DEALT = GROUPS[DEALT][0] // PART
 WIDE = P // 2
 CHUNK = 128
 SLIVER = CHUNK // 2
-X_BANKS = 4
+X_BANKS = 3
 Y_BANKS = 3
 
 
@@ -45,54 +46,45 @@ def tile_list_stereo_disparity_cost_kernel(tc, tab_words, tab_scales, offs, pos1
     nc = tc.nc
     with ExitStack() as ctx:
         keep = ctx.enter_context(tc.tile_pool(name="keep", bufs=1))
-        ring = ctx.enter_context(tc.tile_pool(name="ring", bufs=2))
         psum = ctx.enter_context(tc.psum_pool(name="psum", bufs=X_BANKS))
 
         offs_sb = keep.tile([PART, S // STRIPE], U16, name="offs_sb")
         pos1_sb = keep.tile([PART, P // STRIPE], U16, name="pos1_sb")
         pos2_sb = keep.tile([PART, P // STRIPE], U16, name="pos2_sb")
-        gain_raw = keep.tile([PART, 2, PACK], F32, name="gain_raw")
-        gain_early = keep.tile([PART, FIRST_DEALT], F32, name="gain_early")
-        gain_dealt = keep.tile([PART, PACK], F32, name="gain_dealt")
-        spread_halves = keep.tile([PART, FIRST_DEALT - 1, WIDE], F32, name="spread_halves")
-        spread_whole = keep.tile([PART, P], F32, name="spread_whole")
-        spread_dealt = keep.tile([PART, PACK, WIDE], F32, name="spread_dealt")
-        gains = [spread_halves[:, k, :] for k in range(FIRST_DEALT - 1)] + [spread_whole[:]] + [spread_dealt[:, j, :] for j in range(PACK)]
+        gain_rows = keep.tile([PART, PASS], F32, name="gain_rows")
+        identity = keep.tile([PART, PART], F32, name="identity")
+        spread_early = keep.tile([PART, FIRST_DEALT, P], F32, name="spread_early")
+        spread_dealt = keep.tile([PART, PACK, P], F32, name="spread_dealt")
+        gains = [spread_early[:, k, :] for k in range(FIRST_DEALT)] + [spread_dealt[:, j, :] for j in range(PACK)]
         table = [keep.tile([PART, T], I32, name="table", tag="table%d" % a, align_bytes=ALIGN) for a in range(K_PASSES)]
         table_sc = keep.tile([PART, T // 4], I32, name="table_sc", align_bytes=ALIGN)
         v_sc = keep.tile([PART, S], U8, name="v_sc", align_bytes=ALIGN)
         v_words = {}
-        w1_raw = {
-            (b, a): keep.tile([PART, PACK, c1 - c0], F32, name="w1_raw", tag="raw%d%d" % (b, a), align_bytes=ALIGN)
-            for b, (c0, c1) in enumerate(GROUPS)
-            for a in range(K_PASSES)
-        }
+        late = keep.tile([PART, 6 * S], F32, name="late", align_bytes=ALIGN)
+        late_rows = late[:, : PACK * S].rearrange("p (j c) -> p j c", j=PACK)
+        z0_rows = late[:, 3 * S + P : 5 * S + P].rearrange("p (j i) -> p j i", j=PACK)
+        sq_0 = keep.tile([PART, S], F32, name="sq_0", align_bytes=ALIGN)
+        second = keep.tile([PART, 2 * PACK * WIDE + P - PART], F32, name="second", align_bytes=ALIGN)
+        padded = keep.tile([PART, WIDE + PACK * PASS], F32, name="padded", align_bytes=ALIGN)
+        raw = {}
+        for b, (c0, c1) in enumerate(GROUPS):
+            for a in range(K_PASSES):
+                if (b, a) == (1, LAST):
+                    raw[b, a] = sq_0[:, WIDE : WIDE + BANK]
+                elif (b, a) == (2, LAST):
+                    raw[b, a] = second[:, PACK * WIDE : 2 * PACK * WIDE]
+                elif (b, a) == (DEALT, 0):
+                    raw[b, a] = padded[:, WIDE:]
+                elif (b, a) != (DEALT, LAST):
+                    raw[b, a] = keep.tile([PART, PACK * (c1 - c0)], F32, name="raw", tag="raw%d%d" % (b, a), align_bytes=ALIGN)[:]
+        last = keep.tile([PART, PACK * PASS], F32, name="last", align_bytes=ALIGN)
+        last_left, last_right = last[:, : PACK * WIDE], last[:, PACK * WIDE :]
 
-        w1_bf, w1_words, w1_sc = {}, {}, {}
-
-        def stage(name, halves, by_place=False):
-            width = (GROUPS[halves[0][0]][1] - GROUPS[halves[0][0]][0]) // 2
-            rounded = keep.tile([PART, len(halves) * width * PACK // 2], F32, name="bf" + name, align_bytes=ALIGN)
-            words = keep.tile([PART, len(halves) * width], U32, name="words" + name, align_bytes=ALIGN)
-            scales = keep.tile([PART, len(halves) * width], U8, name="sc" + name, align_bytes=ALIGN)
-            order = "p (t n c) -> p n t c" if by_place else "p (n t c) -> p n t c"
-            for n, half in enumerate(halves):
-                w1_bf[half] = rounded[:].bitcast(BF16).rearrange(order, n=len(halves), t=2)[:, n]
-                w1_words[half] = words[:].rearrange(order, n=len(halves), t=2)[:, n]
-                w1_sc[half] = scales[:].rearrange(order, n=len(halves), t=2)[:, n]
-            return rounded, words, scales
-
-        opening = stage("00", [(0, 0, 0), (0, 0, 1)])
-        for a in range(K_PASSES):
-            stage("1%d" % a, [(1, a, 0), (1, a, 1)])
-        for a in range(1, K_PASSES):
-            stage("0%da" % a, [(0, a, 0)])
-        second_tile = stage("0b", [(0, 1, 1), (0, 2, 1)])
-        stage("20a", [(DEALT, 0, 0)])
-        firsts = stage("2a", [(DEALT, 1, 0), (DEALT, 2, 0)], by_place=True)
-        seconds = stage("2b", [(DEALT, 0, 1), (DEALT, 1, 1)])
-        stage("22b", [(DEALT, 2, 1)])
-        left_1 = keep.tile([PART, P], F32, name="left_1")
+        rounded, w1_words, w1_sc = [], [], []
+        for b, (c0, c1) in enumerate(GROUPS):
+            rounded.append(keep.tile([PART, K_PASSES * PACK * (c1 - c0)], BF16, name="bf%d" % b, align_bytes=ALIGN))
+            w1_words.append(keep.tile([PART, K_PASSES * (c1 - c0)], U32, name="words%d" % b, align_bytes=ALIGN))
+            w1_sc.append(keep.tile([PART, K_PASSES * (c1 - c0)], U8, name="sc%d" % b, align_bytes=ALIGN))
         w2_sb = keep.tile([PART, R_PASSES, N // 2], I32, name="w2_sb", align_bytes=ALIGN)
         w2_sc = keep.tile([PART, R_PASSES, N // 4], I32, name="w2_sc", align_bytes=ALIGN)
         z_words = [keep.tile([PART, P], U32, name="z_words%d" % b, align_bytes=ALIGN) for b in range(R_PASSES)]
@@ -100,35 +92,42 @@ def tile_list_stereo_disparity_cost_kernel(tc, tab_words, tab_scales, offs, pos1
         h = [keep.tile([PART, S], F32, name="h%d" % k) for k in range(TILES)]
         warm = keep.tile([PART, 1], F32, name="warm")
 
-        def load_w1(b, a):
-            rows = w1[a * PASS : (a + 1) * PASS, GROUPS[b][0] : GROUPS[b][1]]
-            nc.sync.dma_start(out=w1_raw[b, a][:], in_=rows.rearrange("(p j) c -> p j c", j=PACK))
+        def load_w1(dst, a, c0, c1):
+            rows = w1[a * PASS : (a + 1) * PASS, c0:c1]
+            nc.sync.dma_start(out=dst.rearrange("p (j c) -> p j c", j=PACK), in_=rows.rearrange("(p j) c -> p j c", j=PACK))
+
+        def load_piece(b, a):
+            load_w1(raw[b, a], a, *GROUPS[b])
 
         def load_table(a):
             nc.sync.dma_start(out=table[a][:], in_=tab_words[a].rearrange("p t i -> p (t i)").bitcast(I32))
 
+        nc.gpsimd.memset(gain_rows[:], 0.0)
+        make_identity(nc, identity[:])
         nc.vector.memset(table_sc[:], 0)
         nc.vector.memset(w2_sc[:], 0)
         nc.sync.dma_start(offs_sb[:], offs)
         load_table(0)
-        for e in range(2):
-            nc.sync.dma_start(out=gain_raw[HALF * e : HALF * (e + 1)], in_=gain[:PASS].rearrange("(c m j) -> m c j", c=2, j=PACK))
-        nc.sync.dma_start(out=gain_dealt[:], in_=gain[PASS:].rearrange("(p j) -> p j", j=PACK))
+        nc.sync.dma_start(out=gain_rows[:R_PASSES], in_=gain.rearrange("(b r) -> b r", b=R_PASSES))
         load_table(1)
         for quad in range(QUADS):
             rows = tab_scales[:, ROWS * quad : ROWS * (quad + 1), :]
             nc.sync.dma_start(out=table_sc[QUAD * quad : QUAD * quad + ROWS * K_PASSES, :], in_=rows.bitcast(I32))
-        load_w1(0, 0)
+        load_piece(0, 0)
+        load_piece(0, 1)
         load_table(2)
-        load_w1(0, 1)
-        load_w1(0, 2)
-        load_w1(1, 0)
-        nc.sync.dma_start(pos1_sb[:], pos1)
-        load_w1(1, 1)
-        nc.sync.dma_start(pos2_sb[:], pos2)
-        load_w1(1, 2)
+        load_piece(0, 2)
         for a in range(K_PASSES):
-            load_w1(DEALT, a)
+            load_piece(1, a)
+        load_piece(2, 0)
+        nc.sync.dma_start(pos1_sb[:], pos1)
+        load_piece(2, 1)
+        nc.sync.dma_start(pos2_sb[:], pos2)
+        load_piece(2, 2)
+        for a in range(LAST):
+            load_piece(DEALT, a)
+        load_w1(last_left, LAST, PASS, PASS + WIDE)
+        load_w1(last_right, LAST, PASS + WIDE, H)
         nc.sync.dma_start(out=w2_sb[:], in_=w2_words.rearrange("b p c -> p b c").bitcast(I32))
         for s in range(ROWS):
             rows = w2_scales[:, s : ROWS * QUADS : ROWS, :].rearrange("b q n -> q b n")
@@ -140,22 +139,31 @@ def tile_list_stereo_disparity_cost_kernel(tc, tab_words, tab_scales, offs, pos1
         def on_vector(dst, src):
             nc.vector.tensor_copy(out=dst, in_=src)
 
-        def round_w1(b, a, half, copy):
-            dst = w1_bf[b, a, half].rearrange("p t (m j) -> p m j t", j=PACK)
-            src = w1_raw[b, a][:].rearrange("p j (m t) -> p m j t", t=PACK)
-            copy(dst, src[:, :, :, 2 * half : 2 * half + 2])
+        def piece(b, a):
+            width = PACK * (GROUPS[b][1] - GROUPS[b][0])
+            return rounded[b][:, a * width : (a + 1) * width]
 
-        def quantize(rounded, words, scales):
-            nc.vector.quantize_mx(out=words.bitcast(FP8X4), scales=scales, in_=rounded)
+        def interleave(dst, src, copy):
+            copy(dst.rearrange("p (c i j) -> p c j i", i=4, j=PACK), src.rearrange("p j (c i) -> p c j i", i=4))
 
-        def flat(view):
-            return view.rearrange("p t c -> p (t c)")
+        def round_plain(b, a, copy):
+            interleave(piece(b, a), raw[b, a].rearrange("p (j c) -> p j c", j=PACK), copy)
 
-        def quant_half(b, a, half):
-            quantize(flat(w1_bf[b, a, half]), flat(w1_words[b, a, half]), flat(w1_sc[b, a, half]))
+        def round_dealt(a):
+            dst = piece(DEALT, a).rearrange("p (t m j) -> p m j t", t=PACK, j=PACK)
+            src = raw[DEALT, a].rearrange("p (j m t) -> p m j t", j=PACK, t=PACK)
+            for m0 in range(0, PART, HALF):
+                on_vector(dst[:, m0 : m0 + HALF], src[:, m0 : m0 + HALF])
 
-        def quant_stage(staged, c0, c1):
-            quantize(staged[0][:].bitcast(BF16)[:, PACK * c0 : PACK * c1], staged[1][:, c0:c1], staged[2][:, c0:c1])
+        def round_last(src, m0):
+            dst = piece(DEALT, LAST).rearrange("p (t m j) -> p m j t", t=PACK, j=PACK)
+            on_scalar(dst[:, m0 : m0 + HALF], src.rearrange("p (j m t) -> p m j t", j=PACK, t=PACK))
+
+        def quantize(src, words, scales):
+            nc.vector.quantize_mx(out=words.bitcast(FP8X4), scales=scales, in_=src)
+
+        def quant_w1(b, c0, c1):
+            quantize(rounded[b][:, PACK * c0 : PACK * c1], w1_words[b][:, c0:c1], w1_sc[b][:, c0:c1])
 
         def gather_words(a, place):
             picked = keep.tile([PART, S], U32, name="v_words", tag=place, align_bytes=ALIGN)
@@ -163,50 +171,46 @@ def tile_list_stereo_disparity_cost_kernel(tc, tab_words, tab_scales, offs, pos1
             v_words[a] = picked
 
         def x_pass(acc, k, a, j0):
-            if k >= FIRST_DEALT:
-                half, t = divmod(k - FIRST_DEALT, 2)
-                words, scales = w1_words[DEALT, a, half][:, t], w1_sc[DEALT, a, half][:, t]
-            else:
-                b, half = divmod(k, 2)
-                words, scales = flat(w1_words[b, a, half]), flat(w1_sc[b, a, half])
+            b = max(n for n, group in enumerate(GROUPS) if group[0] <= k * PART)
+            c0 = a * (GROUPS[b][1] - GROUPS[b][0]) + k * PART - GROUPS[b][0]
             nc.tensor.matmul_mx(
                 out=acc,
-                lhsT=words.bitcast(FP8X4),
-                lhsT_scale=scales,
+                lhsT=w1_words[b][:, c0 : c0 + PART].bitcast(FP8X4),
+                lhsT_scale=w1_sc[b][:, c0 : c0 + PART],
                 rhs=v_words[a][:, j0 : j0 + BANK].bitcast(FP8X4),
                 rhs_scale=v_sc[ROWS * a : PART, j0 : j0 + BANK],
                 start=(a == 0),
                 stop=(a == LAST),
             )
 
-        def respond(k, step, sq=None, opened=None):
-            if sq is None:
-                sq = ring.tile([PART, S], F32, name="sq")
+        def x_bank(k, j0):
+            acc = psum.tile([PART, BANK], F32, name="bank")
+            for a in range(K_PASSES):
+                x_pass(acc[:], k, a, j0)
+            return acc
+
+        def square(acc, sq):
+            nc.scalar.activation(out=sq, in_=acc, func=ACT.Square)
+
+        def exponent(k, j0, j1, sq):
+            nc.scalar.activation(out=h[k][:, j0:j1], in_=sq, func=ACT.Exp, scale=-1.0)
+
+        def respond(k, step, sq):
             for j0 in range(0, S, BANK):
-                acc = psum.tile([PART, BANK], F32, name="bank") if opened is None else opened[j0 // BANK]
-                for a in range(0 if opened is None else 1, K_PASSES):
-                    x_pass(acc[:], k, a, j0)
-                nc.scalar.activation(out=sq[:, j0 : j0 + BANK], in_=acc[:], func=ACT.Square)
+                square(x_bank(k, j0)[:], sq[:, j0 : j0 + BANK])
             for j0 in range(0, S, step):
-                nc.scalar.activation(out=h[k][:, j0 : j0 + step], in_=sq[:, j0 : j0 + step], func=ACT.Exp, scale=-1.0)
+                exponent(k, j0, j0 + step, sq[:, j0 : j0 + step])
 
-        def gather_left(k, i0, i1, left):
-            nc.vector.tensor_tensor(left, h[k][:].indirect(pos1_sb[:, i0 // STRIPE : i1 // STRIPE]), gains[k][:, : i1 - i0], MULT)
+        left = {}
 
-        def gather_right(k, i0, i1, left, z):
-            nc.vector.tensor_tensor(z, h[k][:].indirect(pos2_sb[:, i0 // STRIPE : i1 // STRIPE]), left, MULT)
+        def gather_left(k, i0, i1):
+            nc.vector.tensor_tensor(left[k][:, i0:i1], h[k][:].indirect(pos1_sb[:, i0 // STRIPE : i1 // STRIPE]), gains[k][:, i0:i1], MULT)
 
-        def match(k, left, z):
-            for i0 in range(0, P, WIDE):
-                gather_left(k, i0, i0 + WIDE, left[:, i0 : i0 + WIDE])
-            for i0 in range(0, P, WIDE):
-                gather_right(k, i0, i0 + WIDE, left[:, i0 : i0 + WIDE], z[:, i0 : i0 + WIDE])
+        def gather_right(k, i0, i1, z):
+            nc.vector.tensor_tensor(z, h[k][:].indirect(pos2_sb[:, i0 // STRIPE : i1 // STRIPE]), left[k][:, i0:i1], MULT)
 
-        def round_z(dst, src, copy):
-            copy(dst.rearrange("p (c i j) -> p c j i", i=4, j=PACK), src.rearrange("p j (c i) -> p c j i", i=4))
-
-        def quant_z(b, i0, i1, rounded):
-            quantize(rounded[:, PACK * i0 : PACK * i1], z_words[b][:, i0:i1], z_sc[b][:, i0:i1])
+        def quant_z(b, i0, i1, src):
+            quantize(src, z_words[b][:, i0:i1], z_sc[b][:, i0:i1])
 
         def y_pass(acc, nt, b, q, start, stop):
             cols = slice(q * CHUNK, (q + 1) * CHUNK)
@@ -222,7 +226,8 @@ def tile_list_stereo_disparity_cost_kernel(tc, tab_words, tab_scales, offs, pos1
 
         out_rows = out.rearrange("(nt p) i -> p nt i", p=PART)
         y_acc = {}
-        mag = keep.tile([PART, Y_BANKS, BLOCKS, CHUNK], F32, name="mag", tag="table%d" % LAST, align_bytes=ALIGN)
+        mag = keep.tile([PART, PACK, BLOCKS, CHUNK], F32, name="mag", tag="table2", align_bytes=ALIGN)
+        cost = keep.tile([PART, PACK, BLOCKS, CHUNK], F32, name="cost", tag="table1", align_bytes=ALIGN)
 
         def open_y(q, n0, n1, tag, bufs):
             y_acc[q, n0] = psum.tile([PART, BLOCKS, CHUNK], F32, name="y_acc", tag=tag, bufs=bufs)
@@ -237,121 +242,134 @@ def tile_list_stereo_disparity_cost_kernel(tc, tab_words, tab_scales, offs, pos1
             nc.scalar.activation(out=mag[:, slot, n0:n1, :], in_=y_acc[q, n0][:, : n1 - n0, :], func=ACT.Abs)
 
         def root_and_store(q, n0, n1, slot):
-            cost = keep.tile([PART, n1 - n0, CHUNK], F32, name="cost%d%d" % (q, n0))
-            nc.scalar.activation(out=cost[:], in_=mag[:, slot, n0:n1, :], func=ACT.Sqrt)
-            nc.sync.dma_start(out=out_rows[:, n0:n1, q * CHUNK : (q + 1) * CHUNK], in_=cost[:])
+            nc.scalar.activation(out=cost[:, q, n0:n1, :], in_=mag[:, slot, n0:n1, :], func=ACT.Sqrt)
+            nc.sync.dma_start(out=out_rows[:, n0:n1, q * CHUNK : (q + 1) * CHUNK], in_=cost[:, q, n0:n1, :])
 
         for a in range(LAST):
             gather_words(a, "v%d" % a)
         nc.vector.tensor_copy(v_sc[:], table_sc[:].bitcast(U8).indirect(offs_sb[:]))
-        for half in range(2):
-            round_w1(0, 0, half, on_scalar)
-        quant_stage(opening, 0, WIDE)
-        for e in range(2):
-            rows = slice(HALF * e, HALF * (e + 1))
-            on_scalar(gain_early[rows].rearrange("p (c u) -> p c u", u=2), gain_raw[rows, :, e:PACK:2])
-        on_scalar(spread_halves[:], gain_early[:, : FIRST_DEALT - 1].unsqueeze(2).to_broadcast([PART, FIRST_DEALT - 1, WIDE]))
-        on_scalar(spread_whole[:], gain_early[:, FIRST_DEALT - 1 :].to_broadcast([PART, P]))
-        on_scalar(spread_dealt[:], gain_dealt[:].unsqueeze(2).to_broadcast([PART, PACK, WIDE]))
-        opened = [[psum.tile([PART, BANK], F32, name="bank") for j0 in range(0, S, BANK)] for k in range(2)]
-        for k in range(2):
-            for j0 in range(0, S, BANK):
-                x_pass(opened[k][j0 // BANK][:], k, 0, j0)
-        gather_words(LAST, "raw00")
-        for a in range(1, K_PASSES):
-            round_w1(0, a, 0, on_scalar)
-            quant_half(0, a, 0)
-            round_w1(0, a, 1, on_scalar)
-        quant_stage(second_tile, 0, WIDE)
-        for k in range(2):
-            respond(k, BANK, opened=opened[k])
-
+        for a in range(LAST):
+            round_plain(0, a, on_scalar)
+        for b, spread in enumerate((spread_early, spread_dealt)):
+            turned = psum.tile([PART, BLOCKS, CHUNK], F32, name="turned", tag="y_bank", bufs=Y_BANKS)
+            for n in range(PACK):
+                columns = gain_rows[:, n:PASS:PACK] if b else gain_rows[:, n * PART : (n + 1) * PART]
+                nc.tensor.transpose(turned[:, n, :], columns, identity[:])
+            on_scalar(spread[:], turned[:, :, b : b + 1].to_broadcast([PART, PACK, P]))
+        quant_w1(0, 0, LAST * PART)
+        gather_words(LAST, "raw01")
+        round_plain(0, LAST, on_scalar)
+        quant_w1(0, LAST * PART, K_PASSES * PART)
         for a in range(K_PASSES):
-            for half in range(2):
-                round_w1(1, a, half, on_vector)
-            for half in range(2):
-                quant_half(1, a, half)
-        respond(2, S)
-        respond(3, S)
+            round_plain(1, a, on_scalar)
+        quant_w1(1, 0, LAST * PART)
+        quant_w1(1, LAST * PART, K_PASSES * PART)
+        sq_even = keep.tile([PART, 2 * S], F32, name="sq_even", tag="table0", align_bytes=ALIGN)
+        respond(0, BANK, sq_0[:])
 
-        z0 = keep.tile([PART, PACK, P], F32, name="z0", tag="table0", align_bytes=ALIGN)
-        z0_late = keep.tile([PART, 2, P], F32, name="z0_late")
-        match(0, w1_raw[1, LAST][:].rearrange("p j c -> p (j c)")[:, :P], z0[:, 0, :])
-        nc.sync.dma_start(out=z0[:HALF, 1, :], in_=z0[HALF:, 0, :])
-        left_2 = keep.tile([PART, WIDE], F32, name="left_2")
-        match(1, left_1[:], z0[:, 2, :])
-        nc.sync.dma_start(out=z0[:HALF, 3, :], in_=z0[HALF:, 2, :])
-        round_w1(DEALT, 0, 0, on_vector)
-        quant_half(DEALT, 0, 0)
-        round_w1(DEALT, 1, 0, on_vector)
-        gather_left(2, 0, WIDE, left_2[:])
-        gather_right(2, 0, WIDE, left_2[:], z0_late[:, 0, :WIDE])
-        round_w1(DEALT, LAST, 0, on_vector)
-        quant_stage(firsts, 0, PART)
-        quant_stage(firsts, PART, 2 * PART)
-        quant_stage(firsts, 2 * PART, 4 * PART)
-        for a in range(K_PASSES):
-            round_w1(DEALT, a, 1, on_scalar)
-        last_sq = keep.tile([PART, S], F32, name="last_sq", align_bytes=ALIGN)
-        respond(4, S)
-        respond(5, S)
-        left_2_rest, left_3 = firsts[0][:, WIDE:P], firsts[0][:, P:]
-        gather_left(2, WIDE, P, left_2_rest)
-        gather_left(3, 0, P, left_3)
-        quant_stage(seconds, 0, P)
-        quant_half(DEALT, LAST, 1)
-        respond(6, S)
-        respond(7, BANK, sq=last_sq)
+        left[0], left[1] = raw[2, 1][:, P:], padded[:, :P]
+        left[3], left[4] = raw[1, 0], raw[1, 1]
+        left[5], left[6] = raw[2, 0][:, :P], raw[2, 0][:, P:]
 
-        def lift(u):
-            nc.sync.dma_start(out=z0[HALF:, 2 * u, :], in_=z0_late[:HALF, u, :])
-            nc.sync.dma_start(out=z0[HALF:, 2 * u + 1, :], in_=z0_late[HALF:, u, :])
+        def carry(k, z):
+            for j in range(PACK):
+                nc.sync.dma_start(out=z0_rows[QUAD * k : QUAD * (k + 1), j, :], in_=z[j:PART:PACK])
 
-        gather_right(2, WIDE, P, left_2_rest, z0_late[:, 0, WIDE:])
-        lift(0)
-        gather_right(3, 0, P, left_3, z0_late[:, 1, :])
-        lift(1)
+        def match(k, z):
+            gather_right(k, 0, P, z)
+            carry(k, z)
+
+        for a in range(LAST):
+            round_plain(2, a, on_vector)
+            quant_w1(2, a * WIDE, (a + 1) * WIDE)
+        sq_1 = second[:, : 2 * PACK * WIDE].rearrange("p (r c) -> p r c", c=WIDE)[:, :, :PART]
+        banks_1 = [x_bank(1, j0) for j0 in range(0, S, BANK)]
+        square(banks_1[0][:].rearrange("p (r c) -> p r c", c=PART), sq_1[:, :PACK])
+        for c0 in range(0, WIDE, PART):
+            src = raw[2, LAST].rearrange("p (j c) -> p j c", j=PACK)[:, :, c0 : c0 + PART]
+            interleave(piece(2, LAST)[:, PACK * c0 : PACK * (c0 + PART)], src, on_scalar)
+        square(banks_1[1][:].rearrange("p (r c) -> p r c", c=PART), sq_1[:, PACK:])
+        nc.scalar.activation(out=h[1][:].rearrange("p (r c) -> p r c", c=PART), in_=sq_1, func=ACT.Exp, scale=-1.0)
+        gather_left(0, 0, P)
+        quant_w1(2, LAST * WIDE, LAST * WIDE + PART)
+        match(0, second[:, 2 * PACK * WIDE - PART :])
+        quant_w1(2, LAST * WIDE + PART, K_PASSES * WIDE)
+        respond(2, S, sq_even[:, S:])
+        third_banks = [x_bank(3, j0) for j0 in range(0, S, BANK)]
+        sq_3a = keep.tile([PART, BANK], F32, name="sq_3a")
+        sq_3b = last[:, WIDE : WIDE + BANK]
+        square(third_banks[0][:], sq_3a[:])
+        exponent(3, 0, BANK, sq_3a[:])
+        left[2] = last[:, 3 * WIDE : 5 * WIDE]
+
+        round_dealt(0)
+        gather_left(1, 0, P)
+        quant_w1(DEALT, 0, PASS)
+        round_dealt(1)
+        z_1 = raw[DEALT, 1][:, :P]
+        gather_right(1, 0, WIDE, z_1[:, :WIDE])
+        quant_w1(DEALT, PASS, 2 * PASS)
+        gather_right(1, WIDE, P, z_1[:, WIDE:])
+        carry(1, z_1)
+        round_last(last_left, 0)
+        round_last(last_right, HALF)
+        quant_w1(DEALT, 2 * PASS, 2 * PASS + PART)
+        quant_w1(DEALT, 2 * PASS + PART, 3 * PASS)
+        square(third_banks[1][:], sq_3b)
+        exponent(3, BANK, S, sq_3b)
+        gather_left(2, 0, P)
+        gather_left(3, 0, P)
+        match(2, sq_3b)
+        match(3, last[:, 5 * WIDE : 7 * WIDE])
+        respond(4, S, sq_even[:, :S])
+        gather_left(4, 0, P)
+
+        z1_first = late_rows[:, :, BANK : BANK + WIDE]
+        for k in range(FIRST_DEALT + 1, TILES - 1):
+            j = k - FIRST_DEALT
+            respond(k, S, late_rows[:, j - 1, :])
+            gather_left(k, 0, P)
+            gather_right(k - 1, 0, WIDE, z1_first[:, j - 1, :])
+        respond(TILES - 1, BANK, late_rows[:, 2, :])
+        left[TILES - 1] = raw[2, 1][:, :P]
+        gather_left(TILES - 1, 0, WIDE)
+        gather_right(TILES - 2, 0, WIDE, z1_first[:, 2, :])
+
+        z0_bf = [late[:, 2 * S : 2 * S + BANK].bitcast(BF16), late[:, 3 * S - WIDE : 3 * S + WIDE].bitcast(BF16)]
+        for n in range(2):
+            interleave(z0_bf[n], z0_rows[:, :, n * WIDE : (n + 1) * WIDE], on_scalar)
+        nc.scalar.activation(out=warm[:], in_=z0_bf[1][:, PACK * WIDE - 1 :], func=ACT.Sqrt, scale=0.0)
 
         z1_bf = keep.tile([PART, PACK * P], BF16, name="z1_bf", align_bytes=ALIGN)
-        z1_first = keep.tile([PART, PACK, WIDE], F32, name="z1_first")
-        left_first = keep.tile([PART, PACK, WIDE], F32, name="left_first")
+        z1_third = late[:, S : 5 * S].rearrange("p (j c) -> p j c", j=PACK)[:, :, BANK : BANK + CHUNK]
+        slant = S - SLIVER
+        z1_fourth = late[:, BANK + 3 * SLIVER : BANK + 3 * SLIVER + PACK * slant].rearrange("p (j c) -> p j c", j=PACK)[:, :, :CHUNK]
         dealt = range(FIRST_DEALT, TILES)
 
         def round_z1(i0, i1, src):
-            round_z(z1_bf[:, PACK * i0 : PACK * i1], src, on_vector)
+            interleave(z1_bf[:, PACK * i0 : PACK * i1], src, on_vector)
 
-        z0_bf = last_sq[:].bitcast(BF16)
-        for i0 in range(0, P, WIDE):
-            round_z(z0_bf[:, PACK * i0 : PACK * (i0 + WIDE)], z0[:, :, i0 : i0 + WIDE], on_scalar)
-        nc.scalar.activation(out=warm[:], in_=z0_bf[:, PACK * P - 1 :], func=ACT.Sqrt, scale=0.0)
+        def quant_z1(i0, i1):
+            quant_z(1, i0, i1, z1_bf[:, PACK * i0 : PACK * i1])
 
-        for j, k in enumerate(dealt):
-            gather_left(k, 0, WIDE, left_first[:, j, :])
-        for j, k in enumerate(dealt):
-            gather_right(k, 0, WIDE, left_first[:, j, :], z1_first[:, j, :])
-        quant_z(0, 0, WIDE, z0_bf)
+        quant_z(0, 0, WIDE, z0_bf[0])
+        gather_right(TILES - 1, 0, WIDE, z1_first[:, 3, :])
+        left[TILES - 1] = late[:, 2 * S - WIDE : 2 * S + WIDE]
+        gather_left(TILES - 1, WIDE, P)
         for q in range(2):
             open_y(q, 0, BLOCKS, "y_bank", Y_BANKS)
         for i0 in range(0, WIDE, CHUNK):
             round_z1(i0, i0 + CHUNK, z1_first[:, :, i0 : i0 + CHUNK])
-
-        third, fourth = 2 * CHUNK, 3 * CHUNK
-        left_third = keep.tile([PART, PACK, CHUNK], F32, name="left_third")
-        z1_third = keep.tile([PART, PACK, CHUNK], F32, name="z1_third")
-        left_fourth = [left_first[:, PACK - 1, :CHUNK], left_first[:, PACK - 1, CHUNK:], z1_first[:, 0, :CHUNK], left_third[:, PACK - 1, :]]
-        z1_fourth = z1_first[:, :, CHUNK:]
-        for j, k in enumerate(dealt):
-            gather_left(k, third, fourth, left_third[:, j, :])
         for q in range(2):
-            quant_z(1, q * CHUNK, (q + 1) * CHUNK, z1_bf)
+            quant_z1(q * CHUNK, (q + 1) * CHUNK)
             close_y(q, 0, BLOCKS)
+        third, fourth = 2 * CHUNK, 3 * CHUNK
         for j, k in enumerate(dealt):
-            gather_right(k, third, fourth, left_third[:, j, :], z1_third[:, j, :])
-        gather_left(FIRST_DEALT, fourth, P, left_fourth[0])
-        round_z1(third, fourth, z1_third[:])
-        quant_z(0, WIDE, P, z0_bf)
+            gather_right(k, third, fourth, z1_third[:, j, :])
+        quant_z(0, WIDE, P, z0_bf[1])
         open_y(2, 0, BLOCKS, "y_bank", Y_BANKS)
-        quant_z(1, third, fourth, z1_bf)
+        round_z1(third, fourth, z1_third)
+        quant_z1(third, fourth)
         close_y(2, 0, BLOCKS)
         parts = [(0, BLOCKS // 2), (BLOCKS // 2, BLOCKS)]
         open_y(3, *parts[0], "y_bank", Y_BANKS)
@@ -359,24 +377,22 @@ def tile_list_stereo_disparity_cost_kernel(tc, tab_words, tab_scales, offs, pos1
         magnitude(0, 0, BLOCKS, 0)
         magnitude(1, 0, BLOCKS, 1)
         root_and_store(0, 0, BLOCKS, 0)
-        magnitude(2, 0, BLOCKS, 2)
         root_and_store(1, 0, BLOCKS, 1)
+        magnitude(2, 0, BLOCKS, 2)
         root_and_store(2, 0, BLOCKS, 2)
 
-        for j in range(1, PACK):
-            gather_left(dealt[j], fourth, P, left_fourth[j])
         for j in range(PACK - 1):
-            gather_right(dealt[j], fourth, P, left_fourth[j], z1_fourth[:, j, :])
+            gather_right(dealt[j], fourth, P, z1_fourth[:, j, :])
         slivers = [slice(c0, c0 + SLIVER) for c0 in range(0, CHUNK, SLIVER)]
         for cols in slivers:
-            gather_right(TILES - 1, fourth + cols.start, fourth + cols.stop, left_fourth[PACK - 1][:, cols], z1_fourth[:, PACK - 1, cols])
+            gather_right(TILES - 1, fourth + cols.start, fourth + cols.stop, z1_fourth[:, PACK - 1, cols])
         for cols in slivers:
             round_z1(fourth + cols.start, fourth + cols.stop, z1_fourth[:, :, cols])
         for cols in slivers:
-            quant_z(1, fourth + cols.start, fourth + cols.stop, z1_bf)
+            quant_z1(fourth + cols.start, fourth + cols.stop)
         for part in parts:
             close_y(3, *part)
-        for slot, part in enumerate(parts, 1):
-            magnitude(3, *part, slot)
-        for slot, part in enumerate(parts, 1):
-            root_and_store(3, *part, slot)
+        for part in parts:
+            magnitude(3, *part, 2)
+        for part in parts:
+            root_and_store(3, *part, 2)

@@ -38,7 +38,7 @@ FIRST_DEALT = GROUPS[DEALT][0] // PART
 WIDE = P // 2
 CHUNK = 128
 SLIVER = CHUNK // 2
-X_BANKS = 3
+X_BANKS = 4
 Y_BANKS = 3
 
 
@@ -63,16 +63,16 @@ def tile_list_stereo_disparity_cost_kernel(tc, tab_words, tab_scales, offs, pos1
         late = keep.tile([PART, 6 * S], F32, name="late", align_bytes=ALIGN)
         late_rows = late[:, : PACK * S].rearrange("p (j c) -> p j c", j=PACK)
         z0_rows = late[:, 3 * S + P : 5 * S + P].rearrange("p (j i) -> p j i", j=PACK)
-        sq_0 = keep.tile([PART, S], F32, name="sq_0", align_bytes=ALIGN)
-        second = keep.tile([PART, 2 * PACK * WIDE + P - PART], F32, name="second", align_bytes=ALIGN)
+        second = keep.tile([PART, PACK * WIDE], F32, name="second", align_bytes=ALIGN)
+        joint = [keep.tile([PART, PACK * 3 * PART], F32, name="joint%d" % a, align_bytes=ALIGN) for a in range(LAST)]
         padded = keep.tile([PART, WIDE + PACK * PASS], F32, name="padded", align_bytes=ALIGN)
         raw = {}
         for b, (c0, c1) in enumerate(GROUPS):
             for a in range(K_PASSES):
-                if (b, a) == (1, LAST):
-                    raw[b, a] = sq_0[:, WIDE : WIDE + BANK]
-                elif (b, a) == (2, LAST):
-                    raw[b, a] = second[:, PACK * WIDE : 2 * PACK * WIDE]
+                if b in (1, 2) and a < LAST:
+                    continue
+                if (b, a) == (2, LAST):
+                    raw[b, a] = second[:, : PACK * WIDE]
                 elif (b, a) == (DEALT, 0):
                     raw[b, a] = padded[:, WIDE:]
                 elif (b, a) != (DEALT, LAST):
@@ -106,10 +106,12 @@ def tile_list_stereo_disparity_cost_kernel(tc, tab_words, tab_scales, offs, pos1
         make_identity(nc, identity[:])
         nc.vector.memset(table_sc[:], 0)
         nc.vector.memset(w2_sc[:], 0)
-        nc.sync.dma_start(offs_sb[:], offs)
         load_table(0)
+        nc.sync.dma_start(offs_sb[:], offs)
         nc.sync.dma_start(out=gain_rows[:R_PASSES], in_=gain.rearrange("(b r) -> b r", b=R_PASSES))
         load_table(1)
+        nc.sync.dma_start(pos1_sb[:], pos1)
+        nc.sync.dma_start(pos2_sb[:], pos2)
         for quad in range(QUADS):
             rows = tab_scales[:, ROWS * quad : ROWS * (quad + 1), :]
             nc.sync.dma_start(out=table_sc[QUAD * quad : QUAD * quad + ROWS * K_PASSES, :], in_=rows.bitcast(I32))
@@ -117,13 +119,10 @@ def tile_list_stereo_disparity_cost_kernel(tc, tab_words, tab_scales, offs, pos1
         load_piece(0, 1)
         load_table(2)
         load_piece(0, 2)
-        for a in range(K_PASSES):
-            load_piece(1, a)
-        load_piece(2, 0)
-        nc.sync.dma_start(pos1_sb[:], pos1)
-        load_piece(2, 1)
-        nc.sync.dma_start(pos2_sb[:], pos2)
-        load_piece(2, 2)
+        for a in range(LAST):
+            load_w1(joint[a][:], a, PART, PASS)
+        load_piece(1, LAST)
+        load_piece(2, LAST)
         for a in range(LAST):
             load_piece(DEALT, a)
         load_w1(last_left, LAST, PASS, PASS + WIDE)
@@ -162,8 +161,8 @@ def tile_list_stereo_disparity_cost_kernel(tc, tab_words, tab_scales, offs, pos1
         def quantize(src, words, scales):
             nc.vector.quantize_mx(out=words.bitcast(FP8X4), scales=scales, in_=src)
 
-        def quant_w1(b, c0, c1):
-            quantize(rounded[b][:, PACK * c0 : PACK * c1], w1_words[b][:, c0:c1], w1_sc[b][:, c0:c1])
+        def quant_w1(b, c0, c1, src=None):
+            quantize(rounded[b][:, PACK * c0 : PACK * c1] if src is None else src, w1_words[b][:, c0:c1], w1_sc[b][:, c0:c1])
 
         def gather_words(a, place):
             picked = keep.tile([PART, S], U32, name="v_words", tag=place, align_bytes=ALIGN)
@@ -260,16 +259,27 @@ def tile_list_stereo_disparity_cost_kernel(tc, tab_words, tab_scales, offs, pos1
         gather_words(LAST, "raw01")
         round_plain(0, LAST, on_scalar)
         quant_w1(0, LAST * PART, K_PASSES * PART)
-        for a in range(K_PASSES):
-            round_plain(1, a, on_scalar)
-        quant_w1(1, 0, LAST * PART)
-        quant_w1(1, LAST * PART, K_PASSES * PART)
+        rows = [joint[a][:].rearrange("p (j c) -> p j c", j=PACK) for a in range(LAST)]
+        interleave(piece(1, 0), rows[0][:, :, :PART], on_scalar)
+        interleave(piece(2, 0), rows[0][:, :, PART:], on_vector)
+        quant_w1(1, 0, PART)
+        quant_w1(2, 0, WIDE)
+        interleave(piece(1, 1), rows[1][:, :, :PART], on_vector)
+        interleave(piece(2, 1), rows[1][:, :, PART:], on_vector)
+        round_plain(1, LAST, on_vector)
+        quant_w1(2, WIDE, 2 * WIDE)
+        quant_w1(1, PART, K_PASSES * PART)
         sq_even = keep.tile([PART, 2 * S], F32, name="sq_even", tag="table0", align_bytes=ALIGN)
-        respond(0, BANK, sq_0[:])
+        left[0], left[1] = raw[1, LAST], padded[:, :P]
+        left[3], left[4] = joint[1][:, :P], joint[1][:, P : 2 * P]
+        left[5], left[6] = joint[0][:, :P], joint[0][:, P : 2 * P]
 
-        left[0], left[1] = raw[2, 1][:, P:], padded[:, :P]
-        left[3], left[4] = raw[1, 0], raw[1, 1]
-        left[5], left[6] = raw[2, 0][:, :P], raw[2, 0][:, P:]
+        by_rows = [h[0][:, j0 : j0 + BANK].rearrange("p (j c) -> p j c", j=PACK) for j0 in range(0, S, BANK)]
+        for n in range(2):
+            square(x_bank(0, n * BANK)[:].rearrange("p (j c) -> p j c", j=PACK), rows[0][:, :, n * PART : (n + 1) * PART])
+        for n in range(2):
+            nc.scalar.activation(out=by_rows[n], in_=rows[0][:, :, n * PART : (n + 1) * PART], func=ACT.Exp, scale=-1.0)
+        gather_left(0, 0, P)
 
         def carry(k, z):
             for j in range(PACK):
@@ -279,20 +289,15 @@ def tile_list_stereo_disparity_cost_kernel(tc, tab_words, tab_scales, offs, pos1
             gather_right(k, 0, P, z)
             carry(k, z)
 
-        for a in range(LAST):
-            round_plain(2, a, on_vector)
-            quant_w1(2, a * WIDE, (a + 1) * WIDE)
-        sq_1 = second[:, : 2 * PACK * WIDE].rearrange("p (r c) -> p r c", c=WIDE)[:, :, :PART]
-        banks_1 = [x_bank(1, j0) for j0 in range(0, S, BANK)]
-        square(banks_1[0][:].rearrange("p (r c) -> p r c", c=PART), sq_1[:, :PACK])
         for c0 in range(0, WIDE, PART):
             src = raw[2, LAST].rearrange("p (j c) -> p j c", j=PACK)[:, :, c0 : c0 + PART]
             interleave(piece(2, LAST)[:, PACK * c0 : PACK * (c0 + PART)], src, on_scalar)
-        square(banks_1[1][:].rearrange("p (r c) -> p r c", c=PART), sq_1[:, PACK:])
-        nc.scalar.activation(out=h[1][:].rearrange("p (r c) -> p r c", c=PART), in_=sq_1, func=ACT.Exp, scale=-1.0)
-        gather_left(0, 0, P)
+        sq_1 = raw[2, LAST].rearrange("p (j n c) -> p n j c", j=PACK, c=PART)
+        for n in range(2):
+            square(x_bank(1, n * BANK)[:].rearrange("p (j c) -> p j c", j=PACK), sq_1[:, n])
+        nc.scalar.activation(out=h[1][:].rearrange("p (n j c) -> p n j c", n=2, j=PACK), in_=sq_1, func=ACT.Exp, scale=-1.0)
         quant_w1(2, LAST * WIDE, LAST * WIDE + PART)
-        match(0, second[:, 2 * PACK * WIDE - PART :])
+        match(0, rounded[2][:].bitcast(F32)[:, S - WIDE : S + WIDE])
         quant_w1(2, LAST * WIDE + PART, K_PASSES * WIDE)
         respond(2, S, sq_even[:, S:])
         third_banks = [x_bank(3, j0) for j0 in range(0, S, BANK)]
@@ -329,9 +334,10 @@ def tile_list_stereo_disparity_cost_kernel(tc, tab_words, tab_scales, offs, pos1
             j = k - FIRST_DEALT
             respond(k, S, late_rows[:, j - 1, :])
             gather_left(k, 0, P)
-            gather_right(k - 1, 0, WIDE, z1_first[:, j - 1, :])
+            reach = 3 * CHUNK if j == 1 else WIDE
+            gather_right(k - 1, 0, reach, late_rows[:, j - 1, BANK : BANK + reach])
         respond(TILES - 1, BANK, late_rows[:, 2, :])
-        left[TILES - 1] = raw[2, 1][:, :P]
+        left[TILES - 1] = joint[0][:, 2 * P :]
         gather_left(TILES - 1, 0, WIDE)
         gather_right(TILES - 2, 0, WIDE, z1_first[:, 2, :])
 
@@ -341,9 +347,12 @@ def tile_list_stereo_disparity_cost_kernel(tc, tab_words, tab_scales, offs, pos1
         nc.scalar.activation(out=warm[:], in_=z0_bf[1][:, PACK * WIDE - 1 :], func=ACT.Sqrt, scale=0.0)
 
         z1_bf = keep.tile([PART, PACK * P], BF16, name="z1_bf", align_bytes=ALIGN)
-        z1_third = late[:, S : 5 * S].rearrange("p (j c) -> p j c", j=PACK)[:, :, BANK : BANK + CHUNK]
-        slant = S - SLIVER
-        z1_fourth = late[:, BANK + 3 * SLIVER : BANK + 3 * SLIVER + PACK * slant].rearrange("p (j c) -> p j c", j=PACK)[:, :, :CHUNK]
+
+        def slanted(start, pitch):
+            return late[:, start : start + PACK * pitch].rearrange("p (j c) -> p j c", j=PACK)[:, :, :CHUNK]
+
+        z1_third = slanted(BANK + WIDE, S - 3 * QUAD)
+        z1_fourth = slanted(BANK + 3 * QUAD, S - 2 * QUAD)
         dealt = range(FIRST_DEALT, TILES)
 
         def round_z1(i0, i1, src):
@@ -364,8 +373,8 @@ def tile_list_stereo_disparity_cost_kernel(tc, tab_words, tab_scales, offs, pos1
             quant_z1(q * CHUNK, (q + 1) * CHUNK)
             close_y(q, 0, BLOCKS)
         third, fourth = 2 * CHUNK, 3 * CHUNK
-        for j, k in enumerate(dealt):
-            gather_right(k, third, fourth, z1_third[:, j, :])
+        for j in range(1, PACK):
+            gather_right(dealt[j], third, fourth, z1_third[:, j, :])
         quant_z(0, WIDE, P, z0_bf[1])
         open_y(2, 0, BLOCKS, "y_bank", Y_BANKS)
         round_z1(third, fourth, z1_third)

from contextlib import ExitStack

import concourse.mybir as mybir
from concourse.masks import make_identity

K, H, N, T, S, P = 1536, 1024, 512, 2048, 1024, 512
FLOPS = 2 * K * H * S + 2 * H * N * P

F32 = mybir.dt.float32
BF16 = mybir.dt.bfloat16
I32 = mybir.dt.int32
U32 = mybir.dt.uint32
U16 = mybir.dt.uint16
U8 = mybir.dt.uint8
FP8X4 = mybir.dt.float8_e4m3fn_x4
FP4X4 = mybir.dt.float4_e2m1fn_x4
ACT = mybir.ActivationFunctionType
MULT = mybir.AluOpType.mult

PART = 128
HALF = PART // 2
QUAD = 32
QUADS = PART // QUAD
ROWS = 4
PACK = 4
PASS = PART * PACK
K_PASSES = K // PASS
R_PASSES = H // PASS
LAST = K_PASSES - 1
BANK = 512
STRIPE = 16
ALIGN = 64
TILES = H // PART
BLOCKS = N // PART
GROUPS = [(0, 128), (128, 256), (256, 512), (512, 1024)]
DEALT = len(GROUPS) - 1
FIRST_DEALT = GROUPS[DEALT][0] // PART
WIDE = P // 2
CHUNK = 128
SLIVER = CHUNK // 2
X_BANKS = 4
Y_BANKS = 3


def tile_list_stereo_disparity_cost_kernel(tc, tab_words, tab_scales, offs, pos1, pos2, w1, gain, w2_words, w2_scales, out):
    nc = tc.nc
    with ExitStack() as ctx:
        keep = ctx.enter_context(tc.tile_pool(name="keep", bufs=1))
        psum = ctx.enter_context(tc.psum_pool(name="psum", bufs=X_BANKS))

        offs_sb = keep.tile([PART, S // STRIPE], U16, name="offs_sb")
        pos1_sb = keep.tile([PART, P // STRIPE], U16, name="pos1_sb")
        pos2_sb = keep.tile([PART, P // STRIPE], U16, name="pos2_sb")
        gain_rows = keep.tile([PART, PASS], F32, name="gain_rows")
        identity = keep.tile([PART, PART], F32, name="identity")
        spread_early = keep.tile([PART, FIRST_DEALT, P], F32, name="spread_early")
        spread_dealt = keep.tile([PART, PACK, P], F32, name="spread_dealt")
        gains = [spread_early[:, k, :] for k in range(FIRST_DEALT)] + [spread_dealt[:, j, :] for j in range(PACK)]
        table = [keep.tile([PART, T], I32, name="table", tag="table%d" % a, align_bytes=ALIGN) for a in range(K_PASSES)]
        table_sc = keep.tile([PART, T // 4], I32, name="table_sc", align_bytes=ALIGN)
        v_sc = keep.tile([PART, S], U8, name="v_sc", align_bytes=ALIGN)
        v_words = {}
        late = keep.tile([PART, 6 * S], F32, name="late", align_bytes=ALIGN)
        late_rows = late[:, : PACK * S].rearrange("p (j c) -> p j c", j=PACK)
        z0_rows = late[:, 3 * S + P : 5 * S + P].rearrange("p (j i) -> p j i", j=PACK)
        second = keep.tile([PART, PACK * WIDE], F32, name="second", align_bytes=ALIGN)
        joint = [keep.tile([PART, PACK * 3 * PART], F32, name="joint%d" % a, align_bytes=ALIGN) for a in range(LAST)]
        padded = keep.tile([PART, WIDE + PACK * PASS], F32, name="padded", align_bytes=ALIGN)
        raw = {}
        for b, (c0, c1) in enumerate(GROUPS):
            for a in range(K_PASSES):
                if b in (1, 2) and a < LAST:
                    continue
                if (b, a) == (2, LAST):
                    raw[b, a] = second[:, : PACK * WIDE]
                elif (b, a) == (DEALT, 0):
                    raw[b, a] = padded[:, WIDE:]
                elif (b, a) != (DEALT, LAST):
                    raw[b, a] = keep.tile([PART, PACK * (c1 - c0)], F32, name="raw", tag="raw%d%d" % (b, a), align_bytes=ALIGN)[:]
        last = keep.tile([PART, PACK * PASS], F32, name="last", align_bytes=ALIGN)
        last_left, last_right = last[:, : PACK * WIDE], last[:, PACK * WIDE :]

        rounded, w1_words, w1_sc = [], [], []
        for b, (c0, c1) in enumerate(GROUPS):
            rounded.append(keep.tile([PART, K_PASSES * PACK * (c1 - c0)], BF16, name="bf%d" % b, align_bytes=ALIGN))
            w1_words.append(keep.tile([PART, K_PASSES * (c1 - c0)], U32, name="words%d" % b, align_bytes=ALIGN))
            w1_sc.append(keep.tile([PART, K_PASSES * (c1 - c0)], U8, name="sc%d" % b, align_bytes=ALIGN))
        w2_sb = keep.tile([PART, R_PASSES, N // 2], I32, name="w2_sb", align_bytes=ALIGN)
        w2_sc = keep.tile([PART, R_PASSES, N // 4], I32, name="w2_sc", align_bytes=ALIGN)
        z_words = [keep.tile([PART, P], U32, name="z_words%d" % b, align_bytes=ALIGN) for b in range(R_PASSES)]
        z_sc = [keep.tile([PART, P], U8, name="z_sc%d" % b, align_bytes=ALIGN) for b in range(R_PASSES)]
        h = [keep.tile([PART, S], F32, name="h%d" % k) for k in range(TILES)]
        warm = keep.tile([PART, 1], F32, name="warm")

        def load_w1(dst, a, c0, c1):
            rows = w1[a * PASS : (a + 1) * PASS, c0:c1]
            nc.sync.dma_start(out=dst.rearrange("p (j c) -> p j c", j=PACK), in_=rows.rearrange("(p j) c -> p j c", j=PACK))

        def load_piece(b, a):
            load_w1(raw[b, a], a, *GROUPS[b])

        def load_table(a):
            nc.sync.dma_start(out=table[a][:], in_=tab_words[a].rearrange("p t i -> p (t i)").bitcast(I32))

        nc.gpsimd.memset(gain_rows[:], 0.0)
        make_identity(nc, identity[:])
        nc.vector.memset(table_sc[:], 0)
        nc.vector.memset(w2_sc[:], 0)
        load_table(0)
        nc.sync.dma_start(offs_sb[:], offs)
        nc.sync.dma_start(out=gain_rows[:R_PASSES], in_=gain.rearrange("(b r) -> b r", b=R_PASSES))
        load_table(1)
        nc.sync.dma_start(pos1_sb[:], pos1)
        nc.sync.dma_start(pos2_sb[:], pos2)
        for quad in range(QUADS):
            rows = tab_scales[:, ROWS * quad : ROWS * (quad + 1), :]
            nc.sync.dma_start(out=table_sc[QUAD * quad : QUAD * quad + ROWS * K_PASSES, :], in_=rows.bitcast(I32))
        load_piece(0, 0)
        load_piece(0, 1)
        load_table(2)
        load_piece(0, 2)
        for a in range(LAST):
            load_w1(joint[a][:], a, PART, PASS)
        load_piece(1, LAST)
        load_piece(2, LAST)
        for a in range(LAST):
            load_piece(DEALT, a)
        load_w1(last_left, LAST, PASS, PASS + WIDE)
        load_w1(last_right, LAST, PASS + WIDE, H)
        nc.sync.dma_start(out=w2_sb[:], in_=w2_words.rearrange("b p c -> p b c").bitcast(I32))
        for s in range(ROWS):
            rows = w2_scales[:, s : ROWS * QUADS : ROWS, :].rearrange("b q n -> q b n")
            nc.sync.dma_start(out=w2_sc[s:PART:QUAD, :, :], in_=rows.bitcast(I32))

        def on_scalar(dst, src):
            nc.scalar.copy(out=dst, in_=src)

        def on_vector(dst, src):
            nc.vector.tensor_copy(out=dst, in_=src)

        def piece(b, a):
            width = PACK * (GROUPS[b][1] - GROUPS[b][0])
            return rounded[b][:, a * width : (a + 1) * width]

        def interleave(dst, src, copy):
            copy(dst.rearrange("p (c i j) -> p c j i", i=4, j=PACK), src.rearrange("p j (c i) -> p c j i", i=4))

        def round_plain(b, a, copy):
            interleave(piece(b, a), raw[b, a].rearrange("p (j c) -> p j c", j=PACK), copy)

        def round_dealt(a):
            dst = piece(DEALT, a).rearrange("p (t m j) -> p m j t", t=PACK, j=PACK)
            src = raw[DEALT, a].rearrange("p (j m t) -> p m j t", j=PACK, t=PACK)
            for m0 in range(0, PART, HALF):
                on_vector(dst[:, m0 : m0 + HALF], src[:, m0 : m0 + HALF])

        def round_last(src, m0):
            dst = piece(DEALT, LAST).rearrange("p (t m j) -> p m j t", t=PACK, j=PACK)
            on_scalar(dst[:, m0 : m0 + HALF], src.rearrange("p (j m t) -> p m j t", j=PACK, t=PACK))

        def quantize(src, words, scales):
            nc.vector.quantize_mx(out=words.bitcast(FP8X4), scales=scales, in_=src)

        def quant_w1(b, c0, c1, src=None):
            quantize(rounded[b][:, PACK * c0 : PACK * c1] if src is None else src, w1_words[b][:, c0:c1], w1_sc[b][:, c0:c1])

        def gather_words(a, place):
            picked = keep.tile([PART, S], U32, name="v_words", tag=place, align_bytes=ALIGN)
            nc.vector.tensor_copy(picked[:], table[a][:].bitcast(U32).indirect(offs_sb[:]))
            v_words[a] = picked

        def x_pass(acc, k, a, j0):
            b = max(n for n, group in enumerate(GROUPS) if group[0] <= k * PART)
            c0 = a * (GROUPS[b][1] - GROUPS[b][0]) + k * PART - GROUPS[b][0]
            nc.tensor.matmul_mx(
                out=acc,
                lhsT=w1_words[b][:, c0 : c0 + PART].bitcast(FP8X4),
                lhsT_scale=w1_sc[b][:, c0 : c0 + PART],
                rhs=v_words[a][:, j0 : j0 + BANK].bitcast(FP8X4),
                rhs_scale=v_sc[ROWS * a : PART, j0 : j0 + BANK],
                start=(a == 0),
                stop=(a == LAST),
            )

        def x_bank(k, j0):
            acc = psum.tile([PART, BANK], F32, name="bank")
            for a in range(K_PASSES):
                x_pass(acc[:], k, a, j0)
            return acc

        def square(acc, sq):
            nc.scalar.activation(out=sq, in_=acc, func=ACT.Square)

        def exponent(k, j0, j1, sq):
            nc.scalar.activation(out=h[k][:, j0:j1], in_=sq, func=ACT.Exp, scale=-1.0)

        def respond(k, step, sq):
            for j0 in range(0, S, BANK):
                square(x_bank(k, j0)[:], sq[:, j0 : j0 + BANK])
            for j0 in range(0, S, step):
                exponent(k, j0, j0 + step, sq[:, j0 : j0 + step])

        left = {}

        def gather_left(k, i0, i1):
            nc.vector.tensor_tensor(left[k][:, i0:i1], h[k][:].indirect(pos1_sb[:, i0 // STRIPE : i1 // STRIPE]), gains[k][:, i0:i1], MULT)

        def gather_right(k, i0, i1, z):
            nc.vector.tensor_tensor(z, h[k][:].indirect(pos2_sb[:, i0 // STRIPE : i1 // STRIPE]), left[k][:, i0:i1], MULT)

        def quant_z(b, i0, i1, src):
            quantize(src, z_words[b][:, i0:i1], z_sc[b][:, i0:i1])

        def y_pass(acc, nt, b, q, start, stop):
            cols = slice(q * CHUNK, (q + 1) * CHUNK)
            nc.tensor.matmul_mx(
                out=acc,
                lhsT=w2_sb[:, b, :].bitcast(U8)[:, 2 * PART * nt : 2 * PART * (nt + 1)].bitcast(FP4X4),
                lhsT_scale=w2_sc[:, b, :].bitcast(U8)[:, PART * nt : PART * (nt + 1)],
                rhs=z_words[b][:, cols].bitcast(FP8X4),
                rhs_scale=z_sc[b][:, cols],
                start=start,
                stop=stop,
            )

        out_rows = out.rearrange("(nt p) i -> p nt i", p=PART)
        y_acc = {}
        mag = keep.tile([PART, PACK, BLOCKS, CHUNK], F32, name="mag", tag="table2", align_bytes=ALIGN)
        cost = keep.tile([PART, PACK, BLOCKS, CHUNK], F32, name="cost", tag="table1", align_bytes=ALIGN)

        def open_y(q, n0, n1, tag, bufs):
            y_acc[q, n0] = psum.tile([PART, BLOCKS, CHUNK], F32, name="y_acc", tag=tag, bufs=bufs)
            for nt in range(n0, n1):
                y_pass(y_acc[q, n0][:, nt - n0, :], nt, 0, q, nt == n0, False)

        def close_y(q, n0, n1):
            for nt in range(n0, n1):
                y_pass(y_acc[q, n0][:, nt - n0, :], nt, 1, q, False, nt == n1 - 1)

        def magnitude(q, n0, n1, slot):
            nc.scalar.activation(out=mag[:, slot, n0:n1, :], in_=y_acc[q, n0][:, : n1 - n0, :], func=ACT.Abs)

        def root_and_store(q, n0, n1, slot):
            nc.scalar.activation(out=cost[:, q, n0:n1, :], in_=mag[:, slot, n0:n1, :], func=ACT.Sqrt)
            nc.sync.dma_start(out=out_rows[:, n0:n1, q * CHUNK : (q + 1) * CHUNK], in_=cost[:, q, n0:n1, :])

        for a in range(LAST):
            gather_words(a, "v%d" % a)
        nc.vector.tensor_copy(v_sc[:], table_sc[:].bitcast(U8).indirect(offs_sb[:]))
        for a in range(LAST):
            round_plain(0, a, on_scalar)
        for b, spread in enumerate((spread_early, spread_dealt)):
            turned = psum.tile([PART, BLOCKS, CHUNK], F32, name="turned", tag="y_bank", bufs=Y_BANKS)
            for n in range(PACK):
                columns = gain_rows[:, n:PASS:PACK] if b else gain_rows[:, n * PART : (n + 1) * PART]
                nc.tensor.transpose(turned[:, n, :], columns, identity[:])
            on_scalar(spread[:], turned[:, :, b : b + 1].to_broadcast([PART, PACK, P]))
        quant_w1(0, 0, LAST * PART)
        gather_words(LAST, "raw01")
        round_plain(0, LAST, on_scalar)
        quant_w1(0, LAST * PART, K_PASSES * PART)
        rows = [joint[a][:].rearrange("p (j c) -> p j c", j=PACK) for a in range(LAST)]
        interleave(piece(1, 0), rows[0][:, :, :PART], on_scalar)
        interleave(piece(2, 0), rows[0][:, :, PART:], on_vector)
        quant_w1(1, 0, PART)
        quant_w1(2, 0, WIDE)
        interleave(piece(1, 1), rows[1][:, :, :PART], on_vector)
        interleave(piece(2, 1), rows[1][:, :, PART:], on_vector)
        round_plain(1, LAST, on_vector)
        quant_w1(2, WIDE, 2 * WIDE)
        quant_w1(1, PART, K_PASSES * PART)
        sq_even = keep.tile([PART, 2 * S], F32, name="sq_even", tag="table0", align_bytes=ALIGN)
        left[0], left[1] = raw[1, LAST], padded[:, :P]
        left[3], left[4] = joint[1][:, :P], joint[1][:, P : 2 * P]
        left[5], left[6] = joint[0][:, :P], joint[0][:, P : 2 * P]

        by_rows = [h[0][:, j0 : j0 + BANK].rearrange("p (j c) -> p j c", j=PACK) for j0 in range(0, S, BANK)]
        for n in range(2):
            square(x_bank(0, n * BANK)[:].rearrange("p (j c) -> p j c", j=PACK), rows[0][:, :, n * PART : (n + 1) * PART])
        for n in range(2):
            nc.scalar.activation(out=by_rows[n], in_=rows[0][:, :, n * PART : (n + 1) * PART], func=ACT.Exp, scale=-1.0)
        gather_left(0, 0, P)

        def carry(k, z):
            for j in range(PACK):
                nc.sync.dma_start(out=z0_rows[QUAD * k : QUAD * (k + 1), j, :], in_=z[j:PART:PACK])

        def match(k, z):
            gather_right(k, 0, P, z)
            carry(k, z)

        for c0 in range(0, WIDE, PART):
            src = raw[2, LAST].rearrange("p (j c) -> p j c", j=PACK)[:, :, c0 : c0 + PART]
            interleave(piece(2, LAST)[:, PACK * c0 : PACK * (c0 + PART)], src, on_scalar)
        sq_1 = raw[2, LAST].rearrange("p (j n c) -> p n j c", j=PACK, c=PART)
        for n in range(2):
            square(x_bank(1, n * BANK)[:].rearrange("p (j c) -> p j c", j=PACK), sq_1[:, n])
        nc.scalar.activation(out=h[1][:].rearrange("p (n j c) -> p n j c", n=2, j=PACK), in_=sq_1, func=ACT.Exp, scale=-1.0)
        quant_w1(2, LAST * WIDE, LAST * WIDE + PART)
        match(0, rounded[2][:].bitcast(F32)[:, S - WIDE : S + WIDE])
        quant_w1(2, LAST * WIDE + PART, K_PASSES * WIDE)
        respond(2, S, sq_even[:, S:])
        third_banks = [x_bank(3, j0) for j0 in range(0, S, BANK)]
        sq_3a = keep.tile([PART, BANK], F32, name="sq_3a")
        sq_3b = last[:, WIDE : WIDE + BANK]
        square(third_banks[0][:], sq_3a[:])
        exponent(3, 0, BANK, sq_3a[:])
        left[2] = last[:, 3 * WIDE : 5 * WIDE]

        round_dealt(0)
        gather_left(1, 0, P)
        quant_w1(DEALT, 0, PASS)
        round_dealt(1)
        z_1 = raw[DEALT, 1][:, :P]
        gather_right(1, 0, WIDE, z_1[:, :WIDE])
        quant_w1(DEALT, PASS, 2 * PASS)
        gather_right(1, WIDE, P, z_1[:, WIDE:])
        carry(1, z_1)
        round_last(last_left, 0)
        round_last(last_right, HALF)
        quant_w1(DEALT, 2 * PASS, 2 * PASS + PART)
        quant_w1(DEALT, 2 * PASS + PART, 3 * PASS)
        square(third_banks[1][:], sq_3b)
        exponent(3, BANK, S, sq_3b)
        gather_left(2, 0, P)
        gather_left(3, 0, P)
        match(2, sq_3b)
        match(3, last[:, 5 * WIDE : 7 * WIDE])
        respond(4, S, sq_even[:, :S])
        gather_left(4, 0, P)

        z1_first = late_rows[:, :, BANK : BANK + WIDE]
        for k in range(FIRST_DEALT + 1, TILES - 1):
            j = k - FIRST_DEALT
            respond(k, S, late_rows[:, j - 1, :])
            gather_left(k, 0, P)
            reach = 3 * CHUNK if j == 1 else WIDE
            gather_right(k - 1, 0, reach, late_rows[:, j - 1, BANK : BANK + reach])
        respond(TILES - 1, BANK, late_rows[:, 2, :])
        left[TILES - 1] = joint[0][:, 2 * P :]
        gather_left(TILES - 1, 0, WIDE)
        gather_right(TILES - 2, 0, WIDE, z1_first[:, 2, :])

        z0_bf = [late[:, 2 * S : 2 * S + BANK].bitcast(BF16), late[:, 3 * S - WIDE : 3 * S + WIDE].bitcast(BF16)]
        for n in range(2):
            interleave(z0_bf[n], z0_rows[:, :, n * WIDE : (n + 1) * WIDE], on_scalar)
        nc.scalar.activation(out=warm[:], in_=z0_bf[1][:, PACK * WIDE - 1 :], func=ACT.Sqrt, scale=0.0)

        z1_bf = keep.tile([PART, PACK * P], BF16, name="z1_bf", align_bytes=ALIGN)

        def slanted(start, pitch):
            return late[:, start : start + PACK * pitch].rearrange("p (j c) -> p j c", j=PACK)[:, :, :CHUNK]

        z1_third = slanted(BANK + WIDE, S - 3 * QUAD)
        z1_fourth = slanted(BANK + 3 * QUAD, S - 2 * QUAD)
        dealt = range(FIRST_DEALT, TILES)

        def round_z1(i0, i1, src):
            interleave(z1_bf[:, PACK * i0 : PACK * i1], src, on_vector)

        def quant_z1(i0, i1):
            quant_z(1, i0, i1, z1_bf[:, PACK * i0 : PACK * i1])

        quant_z(0, 0, WIDE, z0_bf[0])
        gather_right(TILES - 1, 0, WIDE, z1_first[:, 3, :])
        left[TILES - 1] = late[:, 2 * S - WIDE : 2 * S + WIDE]
        gather_left(TILES - 1, WIDE, P)
        for q in range(2):
            open_y(q, 0, BLOCKS, "y_bank", Y_BANKS)
        for i0 in range(0, WIDE, CHUNK):
            round_z1(i0, i0 + CHUNK, z1_first[:, :, i0 : i0 + CHUNK])
        for q in range(2):
            quant_z1(q * CHUNK, (q + 1) * CHUNK)
            close_y(q, 0, BLOCKS)
        third, fourth = 2 * CHUNK, 3 * CHUNK
        for j in range(1, PACK):
            gather_right(dealt[j], third, fourth, z1_third[:, j, :])
        quant_z(0, WIDE, P, z0_bf[1])
        open_y(2, 0, BLOCKS, "y_bank", Y_BANKS)
        round_z1(third, fourth, z1_third)
        quant_z1(third, fourth)
        close_y(2, 0, BLOCKS)
        parts = [(0, BLOCKS // 2), (BLOCKS // 2, BLOCKS)]
        open_y(3, *parts[0], "y_bank", Y_BANKS)
        open_y(3, *parts[1], "bank", X_BANKS)
        magnitude(0, 0, BLOCKS, 0)
        magnitude(1, 0, BLOCKS, 1)
        root_and_store(0, 0, BLOCKS, 0)
        root_and_store(1, 0, BLOCKS, 1)
        magnitude(2, 0, BLOCKS, 2)
        root_and_store(2, 0, BLOCKS, 2)

        for j in range(PACK - 1):
            gather_right(dealt[j], fourth, P, z1_fourth[:, j, :])
        slivers = [slice(c0, c0 + SLIVER) for c0 in range(0, CHUNK, SLIVER)]
        for cols in slivers:
            gather_right(TILES - 1, fourth + cols.start, fourth + cols.stop, z1_fourth[:, PACK - 1, cols])
        for cols in slivers:
            round_z1(fourth + cols.start, fourth + cols.stop, z1_fourth[:, :, cols])
        for cols in slivers:
            quant_z1(fourth + cols.start, fourth + cols.stop)
        for part in parts:
            close_y(3, *part)
        for part in parts:
            magnitude(3, *part, 2)
        for part in parts:
            root_and_store(3, *part, 2)
